import numpy as np
import ml_dtypes


def mxq(x, axis, fmt="e4m3"):
    dtype, down = {"e4m3": (ml_dtypes.float8_e4m3fn, 7), "e5m2": (ml_dtypes.float8_e5m2, 14)}[fmt]
    v = np.moveaxis(np.asarray(x, np.float32).astype(ml_dtypes.bfloat16).astype(np.float64), axis, -1)
    blocks = v.reshape(v.shape[:-1] + (-1, 32))
    amax = np.abs(blocks).max(-1, keepdims=True)
    byte = np.maximum(np.where(amax > 0, np.frexp(amax)[1] - 1 + 127, 0) - down, 1)
    scale = np.exp2(byte - 127.0)
    codes = (blocks / scale).astype(np.float32).astype(dtype).astype(np.float64)
    return np.moveaxis((codes * scale).reshape(v.shape), -1, axis)


WIDE = False


def mx_kscale(k):
    if not WIDE:
        return np.ones(k)
    levels = np.array([18, -18])
    if k % 512:
        return np.exp2(np.random.permutation(np.resize(levels, k // 32))).repeat(32)
    a = np.empty((k // 512, 16))
    for p in range(k // 512):
        a[p, :8] = np.random.permutation(np.resize(levels, 8))
        for g in range(8):
            far = levels[np.abs(levels - a[p, g]) >= 10]
            a[p, g + 8] = far[np.random.randint(len(far))]
    return np.exp2(a.ravel()).repeat(32)


def f64(x):
    return np.asarray(x).astype(np.float64)


def striped(idx):
    return np.tile(np.asarray(idx).reshape(-1, 16).T, (8, 1)).astype(np.uint16)


def unstriped(offs):
    return offs[:16].T.reshape(-1).astype(np.int64)


B, N, T, D, R, TU = 1, 512, 2048, 512, 512, 2048


def setup_inputs():
    n = np.random.standard_normal
    idx = np.random.permutation(T)[:B * N]
    uidx = np.random.permutation(TU)[:B * R]
    s = mx_kscale(D)[:, None]
    z = np.ones(TU)
    z[uidx] = mx_kscale(B * R)
    u = np.ones(T)
    u[idx] = mx_kscale(B * N)
    r = np.random.uniform(0.5, 2.0, T) * u
    ur = np.random.uniform(0.5, 2.0, TU) * z
    return {
        "uT": (n((D, TU)) * s / ur).astype(np.float32),
        "vT": (n((D, T)) * (1.00 / np.sqrt(D)) / s / r).astype(np.float32),
        "y": n((B, R, N)).astype(np.float32),
        "us": ur[uidx].reshape(B, R, 1).astype(np.float32),
        "ts": np.tile(r, (128, 1)).astype(np.float32),
        "offs": striped(idx),
        "uoffs": striped(uidx),
    }


def reference(uT, vT, y, us, ts, offs, uoffs):
    idx = unstriped(offs)
    pick = lambda x: x[:, idx].reshape(x.shape[0], B, N).transpose(1, 0, 2)
    uidx = unstriped(uoffs)
    w = pick(f64(vT))
    x = f64(uT)[:, uidx].reshape(D, B, R).transpose(1, 0, 2)
    a = mxq(x, 1, "e4m3").transpose(0, 2, 1) @ mxq(w, 1, "e4m3")
    sc = f64(us) * pick(f64(ts))[:, :1, :]
    a = a * sc
    g = (a - f64(y))
    h = sc * g
    dv = mxq(x, 2, "e4m3") @ mxq(h, 1, "e5m2")
    gv = np.zeros((D, T))
    gv[:, idx] = dv.transpose(1, 0, 2).reshape(D, B * N)
    du = mxq(w, 2, "e4m3") @ mxq(h, 2, "e5m2").transpose(0, 2, 1)
    gu = np.zeros((D, TU))
    gu[:, uidx] = du.transpose(1, 0, 2).reshape(D, B * R)
    return gv, gu

@@ -1,0 +1,197 @@
+from contextlib import ExitStack
+
+import concourse.mybir as mybir
+from concourse.masks import make_identity
+
+D, R, N, T = 512, 512, 512, 2048
+P = 128
+PACK = 4
+CHUNK = 128
+FLOPS = 3 * 2 * D * R * N
+
+F32 = mybir.dt.float32
+BF16 = mybir.dt.bfloat16
+U32 = mybir.dt.uint32
+U16 = mybir.dt.uint16
+U8 = mybir.dt.uint8
+E4M3 = mybir.dt.float8_e4m3fn_x4
+E5M2 = mybir.dt.float8_e5m2_x4
+MULT = mybir.AluOpType.mult
+SUB = mybir.AluOpType.subtract
+COPY = mybir.ActivationFunctionType.Copy
+
+
+def tile_attend_gmf_sq_vu_kernel(tc, uT, vT, y, us, ts, offs, uoffs, out_0, out_1):
+    nc = tc.nc
+    with ExitStack() as ctx:
+        lists = ctx.enter_context(tc.tile_pool(name="lists", bufs=1))
+        sb = ctx.enter_context(tc.tile_pool(name="sb", bufs=1))
+        psum = ctx.enter_context(tc.psum_pool(name="psum", bufs=1))
+
+        def bank(k, shape, dtype, name):
+            return psum.tile(shape, dtype, name=name, tag="bank%d" % k)
+
+        def mx_tiles(name):
+            codes = sb.tile([P, 512], U32, name=name + "_codes", align_bytes=64)
+            scales = sb.tile([P, 512], U8, name=name + "_scales", align_bytes=64)
+            return codes, scales
+
+        def quantise(operand, fmt, values, first, count):
+            codes, scales = operand
+            nc.vector.quantize_mx(
+                out=codes[:, first:first + count].bitcast(fmt),
+                scales=scales[:, first:first + count],
+                in_=values[:, PACK * first:PACK * (first + count)],
+            )
+
+        def product(out, lhs, lhs_first, rhs, rhs_fmt, rhs_first, rhs_count):
+            nc.tensor.matmul_mx(
+                out=out,
+                lhsT=lhs[0][:, lhs_first:lhs_first + P].bitcast(E4M3),
+                lhsT_scale=lhs[1][:, lhs_first:lhs_first + P],
+                rhs=rhs[0][:, rhs_first:rhs_first + rhs_count].bitcast(rhs_fmt),
+                rhs_scale=rhs[1][:, rhs_first:rhs_first + rhs_count],
+                start=True,
+                stop=True,
+            )
+
+        item_list = lists.tile([P, N // 16], U16, name="item_list")
+        user_list = lists.tile([P, R // 16], U16, name="user_list")
+        u_rows = [sb.tile([P, T], F32, name="u_rows%d" % t) for t in range(PACK)]
+        v_rows = [sb.tile([P, T], F32, name="v_rows%d" % t) for t in range(PACK)]
+        ts_row = sb.tile([P, T], F32, name="ts_row")
+        us_col = sb.tile([P, PACK], F32, name="us_col")
+        y_sb = sb.tile([P, PACK, N], F32, name="y_sb")
+        u_hbm = uT.rearrange("(p t) n -> p t n", t=PACK)
+        v_hbm = vT.rearrange("(p t) n -> p t n", t=PACK)
+
+        nc.vector.memset(ts_row[:], 0.0)
+        nc.sync.dma_start(u_rows[0][:], u_hbm[:, 0, :])
+        nc.sync.dma_start(user_list[:], uoffs)
+        nc.sync.dma_start(item_list[:], offs)
+        nc.sync.dma_start(us_col[:], us.rearrange("b (p t) o -> p (b t o)", t=PACK))
+        nc.scalar.dma_start(ts_row[0:1, :], ts[0:1, :])
+        for t in range(1, PACK):
+            nc.sync.dma_start(u_rows[t][:], u_hbm[:, t, :])
+        for t in range(PACK):
+            nc.sync.dma_start(v_rows[t][:], v_hbm[:, t, :])
+        nc.sync.dma_start(y_sb[:], y.rearrange("b (p t) i -> p (b t) i", t=PACK))
+
+        ident_bf = sb.tile([P, P], BF16, name="ident_bf")
+        ident_f32 = sb.tile([P, P], F32, name="ident_f32")
+        make_identity(nc, ident_f32[:])
+        make_identity(nc, ident_bf[:])
+
+        def turn(source, first_bank, name):
+            turned = sb.tile([P, PACK, P, PACK], BF16, name=name, align_bytes=64)
+            for t in range(PACK):
+                ps = bank(first_bank + t, [P, PACK, P], BF16, "%s_ps%d" % (name, t))
+                for s in range(PACK):
+                    nc.tensor.transpose(ps[:, s, :], source[:, s, t, :], ident_bf[:])
+                nc.scalar.copy(turned[:, t, :, :], ps[:].rearrange("q s p -> q p s"))
+            return turned[:].rearrange("q t p s -> q (t p s)")
+
+        x = sb.tile([P, PACK, P, PACK], BF16, name="x", align_bytes=64)
+        for t in range(PACK):
+            nc.vector.tensor_copy(x[:, :, :, t].rearrange("p s q -> p q s"), u_rows[t][:].indirect(user_list[:]))
+            if t == 0:
+                ts_g = sb.tile([P, N], F32, name="ts_g")
+                nc.vector.tensor_copy(ts_g[:], ts_row[:].indirect(item_list[:]))
+        ts_ps = bank(0, [P, PACK, P], F32, "ts_ps")
+        for c in range(PACK):
+            nc.tensor.transpose(ts_ps[:, c, :], ts_g[:, c * P:(c + 1) * P], ident_f32[:])
+        ts_col = sb.tile([P, PACK], F32, name="ts_col")
+        nc.scalar.copy(ts_col[:], ts_ps[:, :, 0])
+        ts_all = bank(1, [P, N], F32, "ts_all")
+        for c in range(PACK):
+            nc.tensor.transpose(ts_all[:, c * P:(c + 1) * P], ts_col[:, c:c + 1].to_broadcast([P, P]), ident_f32[:])
+        sc_planes = sb.tile([P, PACK, N], F32, name="sc_planes")
+        for t in range(PACK):
+            nc.scalar.activation(sc_planes[:, t, :], ts_all[:], COPY, scale=us_col[:, t:t + 1])
+        sc = sb.tile([P, N, PACK], F32, name="sc")
+        nc.scalar.copy(sc[:], sc_planes[:].rearrange("p t i -> p i t"))
+
+        x_d = mx_tiles("x_d")
+        quantise(x_d, E4M3, x[:].rearrange("p s q t -> p (s q t)"), 0, R)
+        x_turned = turn(x[:].rearrange("p s q t -> p s t q"), 4, "x_turned")
+
+        w = sb.tile([P, N, PACK], BF16, name="w", align_bytes=64)
+        w_flat = w[:].rearrange("p i t -> p (i t)")
+        w_d = mx_tiles("w_d")
+        x_r = mx_tiles("x_r")
+        for t in range(PACK - 1):
+            nc.vector.tensor_copy(w[:, :, t], v_rows[t][:].indirect(item_list[:]))
+        quantise(x_r, E4M3, x_turned, 0, D)
+        half = N // 2
+        for k in range(2):
+            nc.vector.tensor_copy(
+                w[:, k * half:(k + 1) * half, PACK - 1],
+                v_rows[PACK - 1][:].indirect(item_list[:, k * half // 16:(k + 1) * half // 16]),
+            )
+        for k in range(2):
+            quantise(w_d, E4M3, w_flat, k * half, half)
+
+        chunks = N // CHUNK
+        a_ps = []
+        for c in range(chunks):
+            ps = bank(c, [P, PACK, CHUNK], F32, "a_ps%d" % c)
+            for t in range(PACK):
+                product(ps[:, t, :], x_d, t * P, w_d, E4M3, c * CHUNK, CHUNK)
+            a_ps.append(ps)
+
+        a = sb.tile([P, N, PACK], F32, name="a")
+        g = sb.tile([P, N, PACK], F32, name="g")
+        h = sb.tile([P, N, PACK], BF16, name="h", align_bytes=64)
+        h_flat = h[:].rearrange("p i t -> p (i t)")
+        h_r = mx_tiles("h_r")
+
+        def cols(c):
+            return slice(c * CHUNK, (c + 1) * CHUNK)
+
+        steps = [
+            lambda c: nc.vector.tensor_tensor(a[:, cols(c), :], a_ps[c][:].rearrange("p t i -> p i t"), sc[:, cols(c), :], MULT),
+            lambda c: nc.vector.tensor_tensor(g[:, cols(c), :], a[:, cols(c), :], y_sb[:, :, cols(c)].rearrange("p t i -> p i t"), SUB),
+            lambda c: nc.vector.tensor_tensor(h[:, cols(c), :], g[:, cols(c), :], sc[:, cols(c), :], MULT),
+            lambda c: quantise(h_r, E5M2, h_flat, c * CHUNK, CHUNK),
+        ]
+        for wave in range(chunks + len(steps) - 1):
+            for k in range(len(steps)):
+                c = wave - k
+                if 0 <= c < chunks:
+                    steps[k](c)
+
+        w_turned = turn(w[:].rearrange("p (q s) t -> p s t q", s=PACK), 0, "w_turned")
+
+        windows = [[sb.tile([P, T], F32, name="window%d_%d" % (o, k)) for k in range(2)] for o in range(2)]
+        out_hbm = [o.rearrange("(p t) n -> p t n", t=PACK) for o in (out_0, out_1)]
+        dv = [sb.tile([P, N], F32, name="dv%d" % t) for t in range(PACK)]
+        du = [sb.tile([P, P, PACK], F32, name="du%d" % t) for t in range(PACK)]
+        for t in range(PACK):
+            ps = bank(4 + t, [P, N], F32, "dv_ps%d" % t)
+            product(ps[:], x_r, t * P, h_r, E5M2, 0, N)
+            nc.scalar.copy(dv[t][:], ps[:])
+
+        def place(o, t, values, index_list):
+            window = windows[o][t % 2]
+            nc.vector.tensor_copy(window[:].indirect(index_list[:]), values)
+            nc.sync.dma_start(out_hbm[o][:, t, :], window[:])
+
+        for o in range(2):
+            for k in range(2):
+                nc.vector.memset(windows[o][k][:], 0.0)
+
+        w_i = mx_tiles("w_i")
+        h_i = mx_tiles("h_i")
+        quantise(w_i, E4M3, w_turned, 0, D)
+        h_turned = turn(h[:].rearrange("p (q s) t -> p s t q", s=PACK), 4, "h_turned")
+        quantise(h_i, E5M2, h_turned, 0, R)
+        for t in range(PACK):
+            ps = bank(t, [P, PACK, P], F32, "du_ps%d" % t)
+            product(ps[:].rearrange("m t p -> m (t p)"), w_i, t * P, h_i, E5M2, 0, R)
+            nc.scalar.copy(du[t][:], ps[:].rearrange("m t p -> m p t"))
+
+        for first in (0, 2):
+            for t in (first, first + 1):
+                place(0, t, dv[t][:], item_list)
+            for t in (first, first + 1):
+                place(1, t, du[t][:].rearrange("m p t -> m (p t)"), user_list)

@@ -65,13 +65,16 @@ def tile_attend_gmf_sq_vu_kernel(tc, uT, vT, y, us, ts, offs, uoffs, out_0, out_
         u_hbm = uT.rearrange("(p t) n -> p t n", t=PACK)
         v_hbm = vT.rearrange("(p t) n -> p t n", t=PACK)
 
-        nc.vector.memset(ts_row[:], 0.0)
-        nc.sync.dma_start(u_rows[0][:], u_hbm[:, 0, :])
+        nc.gpsimd.memset(ts_row[:], 0.0)
+        for k in range(2):
+            nc.sync.dma_start(u_rows[0][:, k * T // 2:(k + 1) * T // 2], u_hbm[:, 0, k * T // 2:(k + 1) * T // 2])
         nc.sync.dma_start(user_list[:], uoffs)
         nc.sync.dma_start(item_list[:], offs)
         nc.sync.dma_start(us_col[:], us.rearrange("b (p t) o -> p (b t o)", t=PACK))
         nc.scalar.dma_start(ts_row[0:1, :], ts[0:1, :])
-        for t in range(1, PACK):
+        for k in range(2):
+            nc.sync.dma_start(u_rows[1][:, k * T // 2:(k + 1) * T // 2], u_hbm[:, 1, k * T // 2:(k + 1) * T // 2])
+        for t in range(2, PACK):
             nc.sync.dma_start(u_rows[t][:], u_hbm[:, t, :])
         for t in range(PACK):
             nc.sync.dma_start(v_rows[t][:], v_hbm[:, t, :])
@@ -139,7 +142,7 @@ def tile_attend_gmf_sq_vu_kernel(tc, uT, vT, y, us, ts, offs, uoffs, out_0, out_
                 product(ps[:, t, :], x_d, t * P, w_d, E4M3, c * CHUNK, CHUNK)
             a_ps.append(ps)
 
-        a = sb.tile([P, N, PACK], F32, name="a")
+        a = sb.tile([P, N // 2, PACK, 2], F32, name="a")
         g = sb.tile([P, N, PACK], F32, name="g")
         h = sb.tile([P, N, PACK], BF16, name="h", align_bytes=64)
         h_flat = h[:].rearrange("p i t -> p (i t)")
@@ -148,9 +151,16 @@ def tile_attend_gmf_sq_vu_kernel(tc, uT, vT, y, us, ts, offs, uoffs, out_0, out_
         def cols(c):
             return slice(c * CHUNK, (c + 1) * CHUNK)
 
+        def pairs(c):
+            return slice(c * CHUNK // 2, (c + 1) * CHUNK // 2)
+
+        def by_pairs(planes):
+            return planes.rearrange("p t (j e) -> p j t e", e=2)
+
         steps = [
-            lambda c: nc.vector.tensor_tensor(a[:, cols(c), :], a_ps[c][:].rearrange("p t i -> p i t"), sc[:, cols(c), :], MULT),
-            lambda c: nc.vector.tensor_tensor(g[:, cols(c), :], a[:, cols(c), :], y_sb[:, :, cols(c)].rearrange("p t i -> p i t"), SUB),
+            lambda c: nc.vector.tensor_tensor(a[:, pairs(c), :, :], by_pairs(a_ps[c][:]), by_pairs(sc_planes[:, :, cols(c)]), MULT),
+            lambda c: nc.vector.tensor_tensor(
+                g[:, cols(c), :].rearrange("p (j e) t -> p j t e", e=2), a[:, pairs(c), :, :], by_pairs(y_sb[:, :, cols(c)]), SUB),
             lambda c: nc.vector.tensor_tensor(h[:, cols(c), :], g[:, cols(c), :], sc[:, cols(c), :], MULT),
             lambda c: quantise(h_r, E5M2, h_flat, c * CHUNK, CHUNK),
         ]
@@ -178,7 +188,7 @@ def tile_attend_gmf_sq_vu_kernel(tc, uT, vT, y, us, ts, offs, uoffs, out_0, out_
 
         for o in range(2):
             for k in range(2):
-                nc.vector.memset(windows[o][k][:], 0.0)
+                nc.gpsimd.memset(windows[o][k][:], 0.0)
 
         w_i = mx_tiles("w_i")
         h_i = mx_tiles("h_i")

@@ -31,16 +31,16 @@ def tile_attend_gmf_sq_vu_kernel(tc, uT, vT, y, us, ts, offs, uoffs, out_0, out_
         def bank(k, shape, dtype, name):
             return psum.tile(shape, dtype, name=name, tag="bank%d" % k)
 
-        def mx_tiles(name):
-            codes = sb.tile([P, 512], U32, name=name + "_codes", align_bytes=64)
-            scales = sb.tile([P, 512], U8, name=name + "_scales", align_bytes=64)
+        def mx_tiles(name, width=512, tag=None):
+            codes = sb.tile([P, width], U32, name=name + "_codes", align_bytes=64, tag=tag or name + "_codes")
+            scales = sb.tile([P, width], U8, name=name + "_scales", align_bytes=64)
             return codes, scales
 
-        def quantise(operand, fmt, values, first, count):
+        def quantise(operand, fmt, values, first, count, pad=0):
             codes, scales = operand
             nc.vector.quantize_mx(
-                out=codes[:, first:first + count].bitcast(fmt),
-                scales=scales[:, first:first + count],
+                out=codes[:, pad + first:pad + first + count].bitcast(fmt),
+                scales=scales[:, pad + first:pad + first + count],
                 in_=values[:, PACK * first:PACK * (first + count)],
             )
 
@@ -58,7 +58,7 @@ def tile_attend_gmf_sq_vu_kernel(tc, uT, vT, y, us, ts, offs, uoffs, out_0, out_
         item_list = lists.tile([P, N // 16], U16, name="item_list")
         user_list = lists.tile([P, R // 16], U16, name="user_list")
         u_rows = [sb.tile([P, T], F32, name="u_rows%d" % t) for t in range(PACK)]
-        v_rows = [sb.tile([P, T], F32, name="v_rows%d" % t) for t in range(PACK)]
+        v_rows = [sb.tile([P, T], F32, name="v_rows%d" % t, tag="v_rows%d" % t, align_bytes=64) for t in range(PACK)]
         ts_row = sb.tile([P, T], F32, name="ts_row")
         us_col = sb.tile([P, PACK], F32, name="us_col")
         y_sb = sb.tile([P, PACK, N], F32, name="y_sb")
@@ -80,23 +80,22 @@ def tile_attend_gmf_sq_vu_kernel(tc, uT, vT, y, us, ts, offs, uoffs, out_0, out_
             nc.sync.dma_start(v_rows[t][:], v_hbm[:, t, :])
         nc.sync.dma_start(y_sb[:], y.rearrange("b (p t) i -> p (b t) i", t=PACK))
 
-        ident_bf = sb.tile([P, P], BF16, name="ident_bf")
         ident_f32 = sb.tile([P, P], F32, name="ident_f32")
         make_identity(nc, ident_f32[:])
-        make_identity(nc, ident_bf[:])
 
-        def turn(source, first_bank, name):
-            turned = sb.tile([P, PACK, P, PACK], BF16, name=name, align_bytes=64)
-            for t in range(PACK):
-                ps = bank(first_bank + t, [P, PACK, P], BF16, "%s_ps%d" % (name, t))
+        def turn(words, first_bank, name):
+            turned = sb.tile([P, 2, 2, P, PACK], BF16, name=name, align_bytes=64)
+            for u in range(2):
+                ps = bank(first_bank + u, [P, PACK * P], F32, "%s_ps%d" % (name, u))
                 for s in range(PACK):
-                    nc.tensor.transpose(ps[:, s, :], source[:, s, t, :], ident_bf[:])
-                nc.scalar.copy(turned[:, t, :, :], ps[:].rearrange("q s p -> q p s"))
-            return turned[:].rearrange("q t p s -> q (t p s)")
+                    nc.tensor.transpose(ps[:, s * P:(s + 1) * P], words[:, s, u, :], ident_f32[:])
+                nc.scalar.copy(turned[:, u, :, :, :], ps[:].bitcast(BF16).rearrange("q (s p e) -> q e p s", s=PACK, e=2))
+            return turned[:].rearrange("q u e p s -> q (u e p s)")
 
         x = sb.tile([P, PACK, P, PACK], BF16, name="x", align_bytes=64)
+        x_planes = sb.tile([P, PACK, R], F32, name="x_planes")
         for t in range(PACK):
-            nc.vector.tensor_copy(x[:, :, :, t].rearrange("p s q -> p q s"), u_rows[t][:].indirect(user_list[:]))
+            nc.vector.tensor_copy(x_planes[:, t, :], u_rows[t][:].indirect(user_list[:]))
             if t == 0:
                 ts_g = sb.tile([P, N], F32, name="ts_g")
                 nc.vector.tensor_copy(ts_g[:], ts_row[:].indirect(item_list[:]))
@@ -111,42 +110,42 @@ def tile_attend_gmf_sq_vu_kernel(tc, uT, vT, y, us, ts, offs, uoffs, out_0, out_
         sc_planes = sb.tile([P, PACK, N], F32, name="sc_planes")
         for t in range(PACK):
             nc.scalar.activation(sc_planes[:, t, :], ts_all[:], COPY, scale=us_col[:, t:t + 1])
-        sc = sb.tile([P, N, PACK], F32, name="sc")
-        nc.scalar.copy(sc[:], sc_planes[:].rearrange("p t i -> p i t"))
+        nc.scalar.copy(x[:].rearrange("p s q t -> p q t s"), x_planes[:].rearrange("p t (q s) -> p q t s", s=PACK))
 
         x_d = mx_tiles("x_d")
-        quantise(x_d, E4M3, x[:].rearrange("p s q t -> p (s q t)"), 0, R)
-        x_turned = turn(x[:].rearrange("p s q t -> p s t q"), 4, "x_turned")
+        x_flat = x[:].rearrange("p s q t -> p (s q t)")
+        quantise(x_d, E4M3, x_flat, 0, R)
+        x_turned = turn(x_flat.bitcast(F32).rearrange("p (s q u) -> p s u q", s=PACK, u=2), 4, "x_turned")
 
         w = sb.tile([P, N, PACK], BF16, name="w", align_bytes=64)
         w_flat = w[:].rearrange("p i t -> p (i t)")
         w_d = mx_tiles("w_d")
-        x_r = mx_tiles("x_r")
         for t in range(PACK - 1):
             nc.vector.tensor_copy(w[:, :, t], v_rows[t][:].indirect(item_list[:]))
-        quantise(x_r, E4M3, x_turned, 0, D)
         half = N // 2
+        chunks = N // CHUNK
+        a_ps = []
         for k in range(2):
             nc.vector.tensor_copy(
                 w[:, k * half:(k + 1) * half, PACK - 1],
                 v_rows[PACK - 1][:].indirect(item_list[:, k * half // 16:(k + 1) * half // 16]),
             )
-        for k in range(2):
-            quantise(w_d, E4M3, w_flat, k * half, half)
-
-        chunks = N // CHUNK
-        a_ps = []
-        for c in range(chunks):
-            ps = bank(c, [P, PACK, CHUNK], F32, "a_ps%d" % c)
-            for t in range(PACK):
-                product(ps[:, t, :], x_d, t * P, w_d, E4M3, c * CHUNK, CHUNK)
-            a_ps.append(ps)
+            for c in (2 * k, 2 * k + 1):
+                quantise(w_d, E4M3, w_flat, c * CHUNK, CHUNK)
+                ps = bank(c, [P, PACK, CHUNK], F32, "a_ps%d" % c)
+                for t in range(PACK):
+                    product(ps[:, t, :], x_d, t * P, w_d, E4M3, c * CHUNK, CHUNK)
+                a_ps.append(ps)
+        x_r = mx_tiles("x_r", tag="v_rows%d" % (PACK - 1))
+        quantise(x_r, E4M3, x_turned, 0, D)
 
         a = sb.tile([P, N // 2, PACK, 2], F32, name="a")
-        g = sb.tile([P, N, PACK], F32, name="g")
+        g = sb.tile([P, N // 2, PACK, 2], F32, name="g")
         h = sb.tile([P, N, PACK], BF16, name="h", align_bytes=64)
         h_flat = h[:].rearrange("p i t -> p (i t)")
-        h_r = mx_tiles("h_r")
+        h_r = mx_tiles("h_r", half + N)
+        nc.gpsimd.memset(h_r[0][:, 0:half], 0)
+        nc.gpsimd.memset(h_r[1][:, 0:half].bitcast(U32), 0)
 
         def cols(c):
             return slice(c * CHUNK, (c + 1) * CHUNK)
@@ -159,49 +158,63 @@ def tile_attend_gmf_sq_vu_kernel(tc, uT, vT, y, us, ts, offs, uoffs, out_0, out_
 
         steps = [
             lambda c: nc.vector.tensor_tensor(a[:, pairs(c), :, :], by_pairs(a_ps[c][:]), by_pairs(sc_planes[:, :, cols(c)]), MULT),
+            lambda c: nc.vector.tensor_tensor(g[:, pairs(c), :, :], a[:, pairs(c), :, :], by_pairs(y_sb[:, :, cols(c)]), SUB),
             lambda c: nc.vector.tensor_tensor(
-                g[:, cols(c), :].rearrange("p (j e) t -> p j t e", e=2), a[:, pairs(c), :, :], by_pairs(y_sb[:, :, cols(c)]), SUB),
-            lambda c: nc.vector.tensor_tensor(h[:, cols(c), :], g[:, cols(c), :], sc[:, cols(c), :], MULT),
-            lambda c: quantise(h_r, E5M2, h_flat, c * CHUNK, CHUNK),
+                h[:, cols(c), :].rearrange("p (j e) t -> p j t e", e=2), g[:, pairs(c), :, :], by_pairs(sc_planes[:, :, cols(c)]), MULT),
+            lambda c: quantise(h_r, E5M2, h_flat, c * CHUNK, CHUNK, half),
         ]
-        for wave in range(chunks + len(steps) - 1):
-            for k in range(len(steps)):
-                c = wave - k
-                if 0 <= c < chunks:
-                    steps[k](c)
+        for k, c in ((0, 0), (0, 1), (1, 0), (1, 1), (2, 0), (2, 1), (0, 2), (3, 0), (3, 1),
+                     (0, 3), (1, 2), (1, 3), (2, 2), (2, 3), (3, 2), (3, 3)):
+            steps[k](c)
 
-        w_turned = turn(w[:].rearrange("p (q s) t -> p s t q", s=PACK), 0, "w_turned")
+        w_turned = turn(w_flat.bitcast(F32).rearrange("p (q s u) -> p s u q", s=PACK, u=2), 0, "w_turned")
 
-        windows = [[sb.tile([P, T], F32, name="window%d_%d" % (o, k)) for k in range(2)] for o in range(2)]
+        windows = [[sb.tile([P, T], F32, name="window%d_%d" % (o, k)) for k in range(3 - o)] for o in range(2)]
         out_hbm = [o.rearrange("(p t) n -> p t n", t=PACK) for o in (out_0, out_1)]
         dv = [sb.tile([P, N], F32, name="dv%d" % t) for t in range(PACK)]
         du = [sb.tile([P, P, PACK], F32, name="du%d" % t) for t in range(PACK)]
-        for t in range(PACK):
-            ps = bank(4 + t, [P, N], F32, "dv_ps%d" % t)
-            product(ps[:], x_r, t * P, h_r, E5M2, 0, N)
+
+        def item_gradient(t, k):
+            ps = bank(k, [P, N], F32, "dv_ps%d" % t)
+            product(ps[:], x_r, t * P, h_r, E5M2, half, N)
             nc.scalar.copy(dv[t][:], ps[:])
 
+        for k in range(2):
+            ps = bank(6 - 2 * k, [P, N], F32, "dv0_ps%d" % k)
+            product(ps[:], x_r, 0, h_r, E5M2, k * half, N)
+            nc.scalar.copy(dv[0][:, k * half:(k + 1) * half], ps[:, half:N])
+        item_gradient(1, 5)
+
         def place(o, t, values, index_list):
-            window = windows[o][t % 2]
-            nc.vector.tensor_copy(window[:].indirect(index_list[:]), values)
+            window = windows[o][t % len(windows[o])]
+            if (o, t) == (0, 0):
+                for k in range(2):
+                    nc.vector.tensor_copy(
+                        window[:].indirect(index_list[:, k * half // 16:(k + 1) * half // 16]), values[:, k * half:(k + 1) * half])
+            else:
+                nc.vector.tensor_copy(window[:].indirect(index_list[:]), values)
             nc.sync.dma_start(out_hbm[o][:, t, :], window[:])
 
-        for o in range(2):
-            for k in range(2):
-                nc.gpsimd.memset(windows[o][k][:], 0.0)
+        for k in range(2):
+            nc.vector.memset(windows[0][k][:], 0.0)
+        for window in (windows[0][2], windows[1][0], windows[1][1]):
+            nc.gpsimd.memset(window[:], 0.0)
 
         w_i = mx_tiles("w_i")
         h_i = mx_tiles("h_i")
         quantise(w_i, E4M3, w_turned, 0, D)
-        h_turned = turn(h[:].rearrange("p (q s) t -> p s t q", s=PACK), 4, "h_turned")
+        h_turned = turn(h_flat.bitcast(F32).rearrange("p (q s u) -> p s u q", s=PACK, u=2), 4, "h_turned")
         quantise(h_i, E5M2, h_turned, 0, R)
+        item_gradient(2, 5)
         for t in range(PACK):
             ps = bank(t, [P, PACK, P], F32, "du_ps%d" % t)
             product(ps[:].rearrange("m t p -> m (t p)"), w_i, t * P, h_i, E5M2, 0, R)
             nc.scalar.copy(du[t][:], ps[:].rearrange("m t p -> m p t"))
+            if t == 1:
+                item_gradient(3, 1)
 
-        for first in (0, 2):
-            for t in (first, first + 1):
+        for o, t in ((0, 0), (0, 1), (0, 2), (1, 0), (1, 1), (0, 3), (1, 2), (1, 3)):
+            if o == 0:
                 place(0, t, dv[t][:], item_list)
-            for t in (first, first + 1):
+            else:
                 place(1, t, du[t][:].rearrange("m p t -> m (p t)"), user_list)

@@ -7,7 +7,11 @@ D, R, N, T = 512, 512, 512, 2048
 P = 128
 PACK = 4
 CHUNK = 128
+HALF = N // 2
+PER_COLUMN = 16
+WINDOWS = 3
 FLOPS = 3 * 2 * D * R * N
+BYTES = 4 * (4 * D * T + R * N + R + T) + 2 * P * (R + N) // PER_COLUMN
 
 F32 = mybir.dt.float32
 BF16 = mybir.dt.bfloat16
@@ -28,19 +32,19 @@ def tile_attend_gmf_sq_vu_kernel(tc, uT, vT, y, us, ts, offs, uoffs, out_0, out_
         sb = ctx.enter_context(tc.tile_pool(name="sb", bufs=1))
         psum = ctx.enter_context(tc.psum_pool(name="psum", bufs=1))
 
-        def bank(k, shape, dtype, name):
-            return psum.tile(shape, dtype, name=name, tag="bank%d" % k)
+        def bank(number, shape, name):
+            return psum.tile(shape, F32, name=name, tag="bank%d" % number)
 
         def mx_tiles(name, width=512, tag=None):
             codes = sb.tile([P, width], U32, name=name + "_codes", align_bytes=64, tag=tag or name + "_codes")
             scales = sb.tile([P, width], U8, name=name + "_scales", align_bytes=64)
             return codes, scales
 
-        def quantise(operand, fmt, values, first, count, pad=0):
+        def quantise(operand, fmt, values, first, count, shift=0):
             codes, scales = operand
             nc.vector.quantize_mx(
-                out=codes[:, pad + first:pad + first + count].bitcast(fmt),
-                scales=scales[:, pad + first:pad + first + count],
+                out=codes[:, shift + first:shift + first + count].bitcast(fmt),
+                scales=scales[:, shift + first:shift + first + count],
                 in_=values[:, PACK * first:PACK * (first + count)],
             )
 
@@ -55,8 +59,11 @@ def tile_attend_gmf_sq_vu_kernel(tc, uT, vT, y, us, ts, offs, uoffs, out_0, out_
                 stop=True,
             )
 
-        item_list = lists.tile([P, N // 16], U16, name="item_list")
-        user_list = lists.tile([P, R // 16], U16, name="user_list")
+        def list_half(index_list, k):
+            return index_list[:, k * HALF // PER_COLUMN:(k + 1) * HALF // PER_COLUMN]
+
+        item_list = lists.tile([P, N // PER_COLUMN], U16, name="item_list")
+        user_list = lists.tile([P, R // PER_COLUMN], U16, name="user_list")
         u_rows = [sb.tile([P, T], F32, name="u_rows%d" % t) for t in range(PACK)]
         v_rows = [sb.tile([P, T], F32, name="v_rows%d" % t, tag="v_rows%d" % t, align_bytes=64) for t in range(PACK)]
         ts_row = sb.tile([P, T], F32, name="ts_row")
@@ -65,156 +72,196 @@ def tile_attend_gmf_sq_vu_kernel(tc, uT, vT, y, us, ts, offs, uoffs, out_0, out_
         u_hbm = uT.rearrange("(p t) n -> p t n", t=PACK)
         v_hbm = vT.rearrange("(p t) n -> p t n", t=PACK)
 
+        def load_in_two(t):
+            for k in range(2):
+                columns = slice(k * T // 2, (k + 1) * T // 2)
+                nc.sync.dma_start(u_rows[t][:, columns], u_hbm[:, t, columns])
+
         nc.gpsimd.memset(ts_row[:], 0.0)
-        for k in range(2):
-            nc.sync.dma_start(u_rows[0][:, k * T // 2:(k + 1) * T // 2], u_hbm[:, 0, k * T // 2:(k + 1) * T // 2])
+        load_in_two(0)
         nc.sync.dma_start(user_list[:], uoffs)
         nc.sync.dma_start(item_list[:], offs)
         nc.sync.dma_start(us_col[:], us.rearrange("b (p t) o -> p (b t o)", t=PACK))
         nc.scalar.dma_start(ts_row[0:1, :], ts[0:1, :])
-        for k in range(2):
-            nc.sync.dma_start(u_rows[1][:, k * T // 2:(k + 1) * T // 2], u_hbm[:, 1, k * T // 2:(k + 1) * T // 2])
+        load_in_two(1)
         for t in range(2, PACK):
             nc.sync.dma_start(u_rows[t][:], u_hbm[:, t, :])
         for t in range(PACK):
             nc.sync.dma_start(v_rows[t][:], v_hbm[:, t, :])
         nc.sync.dma_start(y_sb[:], y.rearrange("b (p t) i -> p (b t) i", t=PACK))
 
-        ident_f32 = sb.tile([P, P], F32, name="ident_f32")
-        make_identity(nc, ident_f32[:])
+        identity = sb.tile([P, P], F32, name="identity")
+        make_identity(nc, identity[:])
 
-        def turn(words, first_bank, name):
+        def turn(pairs_of_t, banks, name):
             turned = sb.tile([P, 2, 2, P, PACK], BF16, name=name, align_bytes=64)
             for u in range(2):
-                ps = bank(first_bank + u, [P, PACK * P], F32, "%s_ps%d" % (name, u))
+                ps = bank(banks[u], [P, PACK * P], "%s_ps%d" % (name, u))
                 for s in range(PACK):
-                    nc.tensor.transpose(ps[:, s * P:(s + 1) * P], words[:, s, u, :], ident_f32[:])
+                    nc.tensor.transpose(ps[:, s * P:(s + 1) * P], pairs_of_t[:, s, u, :], identity[:])
                 nc.scalar.copy(turned[:, u, :, :, :], ps[:].bitcast(BF16).rearrange("q (s p e) -> q e p s", s=PACK, e=2))
             return turned[:].rearrange("q u e p s -> q (u e p s)")
 
         x = sb.tile([P, PACK, P, PACK], BF16, name="x", align_bytes=64)
-        x_planes = sb.tile([P, PACK, R], F32, name="x_planes")
-        for t in range(PACK):
-            nc.vector.tensor_copy(x_planes[:, t, :], u_rows[t][:].indirect(user_list[:]))
-            if t == 0:
-                ts_g = sb.tile([P, N], F32, name="ts_g")
-                nc.vector.tensor_copy(ts_g[:], ts_row[:].indirect(item_list[:]))
-        ts_ps = bank(0, [P, PACK, P], F32, "ts_ps")
-        for c in range(PACK):
-            nc.tensor.transpose(ts_ps[:, c, :], ts_g[:, c * P:(c + 1) * P], ident_f32[:])
-        ts_col = sb.tile([P, PACK], F32, name="ts_col")
+        x_gathered = sb.tile([P, PACK, R], F32, name="x_gathered")
+        nc.vector.tensor_copy(x_gathered[:, 0, :], u_rows[0][:].indirect(user_list[:]))
+        ts_gathered = sb.tile([P, N], F32, name="ts_gathered")
+        nc.vector.tensor_copy(ts_gathered[:], ts_row[:].indirect(item_list[:]))
+        for t in range(1, PACK):
+            nc.vector.tensor_copy(x_gathered[:, t, :], u_rows[t][:].indirect(user_list[:]))
+
+        ts_ps = bank(0, [P, PACK, P], "ts_ps")
+        for c in range(N // P):
+            nc.tensor.transpose(ts_ps[:, c, :], ts_gathered[:, c * P:(c + 1) * P], identity[:])
+        ts_col = sb.tile([P, N // P], F32, name="ts_col")
         nc.scalar.copy(ts_col[:], ts_ps[:, :, 0])
-        ts_all = bank(1, [P, N], F32, "ts_all")
-        for c in range(PACK):
-            nc.tensor.transpose(ts_all[:, c * P:(c + 1) * P], ts_col[:, c:c + 1].to_broadcast([P, P]), ident_f32[:])
-        sc_planes = sb.tile([P, PACK, N], F32, name="sc_planes")
+        ts_all = bank(1, [P, N], "ts_all")
+        for c in range(N // P):
+            nc.tensor.transpose(ts_all[:, c * P:(c + 1) * P], ts_col[:, c:c + 1].to_broadcast([P, P]), identity[:])
+        scale = sb.tile([P, PACK, N], F32, name="scale")
         for t in range(PACK):
-            nc.scalar.activation(sc_planes[:, t, :], ts_all[:], COPY, scale=us_col[:, t:t + 1])
-        nc.scalar.copy(x[:].rearrange("p s q t -> p q t s"), x_planes[:].rearrange("p t (q s) -> p q t s", s=PACK))
+            nc.scalar.activation(scale[:, t, :], ts_all[:], COPY, scale=us_col[:, t:t + 1])
+        nc.scalar.copy(x[:].rearrange("p s q t -> p q t s"), x_gathered[:].rearrange("p t (q s) -> p q t s", s=PACK))
 
         x_d = mx_tiles("x_d")
         x_flat = x[:].rearrange("p s q t -> p (s q t)")
         quantise(x_d, E4M3, x_flat, 0, R)
-        x_turned = turn(x_flat.bitcast(F32).rearrange("p (s q u) -> p s u q", s=PACK, u=2), 4, "x_turned")
+        x_turned = turn(x_flat.bitcast(F32).rearrange("p (s q u) -> p s u q", s=PACK, u=2), (4, 5), "x_turned")
 
         w = sb.tile([P, N, PACK], BF16, name="w", align_bytes=64)
         w_flat = w[:].rearrange("p i t -> p (i t)")
         w_d = mx_tiles("w_d")
-        for t in range(PACK - 1):
+        last = PACK - 1
+        for t in range(last):
             nc.vector.tensor_copy(w[:, :, t], v_rows[t][:].indirect(item_list[:]))
-        half = N // 2
-        chunks = N // CHUNK
-        a_ps = []
-        for k in range(2):
-            nc.vector.tensor_copy(
-                w[:, k * half:(k + 1) * half, PACK - 1],
-                v_rows[PACK - 1][:].indirect(item_list[:, k * half // 16:(k + 1) * half // 16]),
-            )
-            for c in (2 * k, 2 * k + 1):
+
+        direct, turned_back = (0, 1), (2, 3)
+        a_ps = {}
+        for k, chunks in enumerate((direct, turned_back)):
+            nc.vector.tensor_copy(w[:, k * HALF:(k + 1) * HALF, last], v_rows[last][:].indirect(list_half(item_list, k)))
+            for c in chunks:
                 quantise(w_d, E4M3, w_flat, c * CHUNK, CHUNK)
-                ps = bank(c, [P, PACK, CHUNK], F32, "a_ps%d" % c)
-                for t in range(PACK):
-                    product(ps[:, t, :], x_d, t * P, w_d, E4M3, c * CHUNK, CHUNK)
-                a_ps.append(ps)
-        x_r = mx_tiles("x_r", tag="v_rows%d" % (PACK - 1))
+                a_ps[c] = bank(c, [P, PACK, CHUNK], "a_ps%d" % c)
+                if c in direct:
+                    for t in range(PACK):
+                        product(a_ps[c][:, t, :], x_d, t * P, w_d, E4M3, c * CHUNK, CHUNK)
+                else:
+                    product(a_ps[c][:].rearrange("i t p -> i (t p)"), w_d, c * CHUNK, x_d, E4M3, 0, R)
+        x_r = mx_tiles("x_r", tag="v_rows%d" % last)
         quantise(x_r, E4M3, x_turned, 0, D)
 
-        a = sb.tile([P, N // 2, PACK, 2], F32, name="a")
+        a_by_item = {}
+        a_by_row = {}
+        for c in turned_back:
+            a_by_item[c] = sb.tile([P, PACK, P], F32, name="a_by_item%d" % c)
+            nc.scalar.activation(a_by_item[c][:], a_ps[c][:], COPY, scale=ts_col[:, c:c + 1])
+        for c, number in zip(turned_back, (7, 5)):
+            ps = bank(number, [P, PACK, CHUNK], "a_back%d" % c)
+            a_by_row[c] = sb.tile([P, PACK, CHUNK], F32, name="a_by_row%d" % c, tag="a_by_row%d" % c)
+            for t in range(PACK):
+                nc.tensor.transpose(ps[:, t, :], a_by_item[c][:, t, :], identity[:])
+            for t in range(PACK):
+                nc.scalar.activation(a_by_row[c][:, t, :], ps[:, t, :], COPY, scale=us_col[:, t:t + 1])
+
+        a = sb.tile([P, HALF // 2, PACK, 2], F32, name="a")
         g = sb.tile([P, N // 2, PACK, 2], F32, name="g")
         h = sb.tile([P, N, PACK], BF16, name="h", align_bytes=64)
         h_flat = h[:].rearrange("p i t -> p (i t)")
-        h_r = mx_tiles("h_r", half + N)
-        nc.gpsimd.memset(h_r[0][:, 0:half], 0)
-        nc.gpsimd.memset(h_r[1][:, 0:half].bitcast(U32), 0)
+        h_r = mx_tiles("h_r", HALF + N)
+        nc.gpsimd.memset(h_r[0][:, 0:HALF], 0)
+        nc.gpsimd.memset(h_r[1][:, 0:HALF].bitcast(U32), 0)
 
-        def cols(c):
+        def items(c):
             return slice(c * CHUNK, (c + 1) * CHUNK)
 
-        def pairs(c):
+        def item_pairs(c):
             return slice(c * CHUNK // 2, (c + 1) * CHUNK // 2)
 
-        def by_pairs(planes):
-            return planes.rearrange("p t (j e) -> p j t e", e=2)
+        def by_pairs(rows):
+            return rows.rearrange("p t (j e) -> p j t e", e=2)
 
-        steps = [
-            lambda c: nc.vector.tensor_tensor(a[:, pairs(c), :, :], by_pairs(a_ps[c][:]), by_pairs(sc_planes[:, :, cols(c)]), MULT),
-            lambda c: nc.vector.tensor_tensor(g[:, pairs(c), :, :], a[:, pairs(c), :, :], by_pairs(y_sb[:, :, cols(c)]), SUB),
-            lambda c: nc.vector.tensor_tensor(
-                h[:, cols(c), :].rearrange("p (j e) t -> p j t e", e=2), g[:, pairs(c), :, :], by_pairs(sc_planes[:, :, cols(c)]), MULT),
-            lambda c: quantise(h_r, E5M2, h_flat, c * CHUNK, CHUNK, half),
-        ]
-        for k, c in ((0, 0), (0, 1), (1, 0), (1, 1), (2, 0), (2, 1), (0, 2), (3, 0), (3, 1),
-                     (0, 3), (1, 2), (1, 3), (2, 2), (2, 3), (3, 2), (3, 3)):
-            steps[k](c)
+        def scale_a(c):
+            nc.vector.tensor_tensor(a[:, item_pairs(c), :, :], by_pairs(a_ps[c][:]), by_pairs(scale[:, :, items(c)]), MULT)
 
-        w_turned = turn(w_flat.bitcast(F32).rearrange("p (q s u) -> p s u q", s=PACK, u=2), 0, "w_turned")
+        def subtract_y(c):
+            scaled = a[:, item_pairs(c), :, :] if c in direct else by_pairs(a_by_row[c][:])
+            nc.vector.tensor_tensor(g[:, item_pairs(c), :, :], scaled, by_pairs(y_sb[:, :, items(c)]), SUB)
 
-        windows = [[sb.tile([P, T], F32, name="window%d_%d" % (o, k)) for k in range(3 - o)] for o in range(2)]
-        out_hbm = [o.rearrange("(p t) n -> p t n", t=PACK) for o in (out_0, out_1)]
-        dv = [sb.tile([P, N], F32, name="dv%d" % t) for t in range(PACK)]
+        def scale_g(c):
+            nc.vector.tensor_tensor(
+                h[:, items(c), :].rearrange("p (j e) t -> p j t e", e=2),
+                g[:, item_pairs(c), :, :], by_pairs(scale[:, :, items(c)]), MULT)
+
+        def quantise_h(c):
+            quantise(h_r, E5M2, h_flat, c * CHUNK, CHUNK, HALF)
+
+        dv = {t: sb.tile([P, N], F32, name="dv%d" % t) for t in range(2, PACK)}
+
+        for step in (scale_a, subtract_y, scale_g):
+            for c in direct:
+                step(c)
+        subtract_y(turned_back[0])
+        for c in direct:
+            quantise_h(c)
+        subtract_y(turned_back[1])
+        for step in (scale_g, quantise_h):
+            for c in turned_back:
+                step(c)
+
+        windows = [[sb.tile([P, T], F32, name="window%d_%d" % (o, k)) for k in range(WINDOWS)] for o in range(2)]
+        out_hbm = [out.rearrange("(p t) n -> p t n", t=PACK) for out in (out_0, out_1)]
         du = [sb.tile([P, P, PACK], F32, name="du%d" % t) for t in range(PACK)]
+        dv_half = {}
 
-        def item_gradient(t, k):
-            ps = bank(k, [P, N], F32, "dv_ps%d" % t)
-            product(ps[:], x_r, t * P, h_r, E5M2, half, N)
+        def item_gradient_half(t, k, number, tag):
+            ps = bank(number, [P, N], "dv_ps%d_%d" % (t, k))
+            product(ps[:], x_r, t * P, h_r, E5M2, k * HALF, N)
+            dv_half[t, k] = sb.tile([P, HALF], F32, name="dv%d_%d" % (t, k), tag=tag)
+            nc.scalar.copy(dv_half[t, k][:], ps[:, HALF:N])
+
+        def item_gradient(t, number):
+            ps = bank(number, [P, N], "dv_ps%d" % t)
+            product(ps[:], x_r, t * P, h_r, E5M2, HALF, N)
             nc.scalar.copy(dv[t][:], ps[:])
 
-        for k in range(2):
-            ps = bank(6 - 2 * k, [P, N], F32, "dv0_ps%d" % k)
-            product(ps[:], x_r, 0, h_r, E5M2, k * half, N)
-            nc.scalar.copy(dv[0][:, k * half:(k + 1) * half], ps[:, half:N])
-        item_gradient(1, 5)
+        item_gradient_half(0, 0, 6, "a_by_row%d" % turned_back[0])
+        item_gradient_half(1, 0, 1, "a_by_row%d" % turned_back[1])
+        item_gradient_half(0, 1, 4, "dv0_1")
+        item_gradient_half(1, 1, 0, "dv1_1")
+        item_gradient(2, 0)
 
-        def place(o, t, values, index_list):
-            window = windows[o][t % len(windows[o])]
-            if (o, t) == (0, 0):
-                for k in range(2):
-                    nc.vector.tensor_copy(
-                        window[:].indirect(index_list[:, k * half // 16:(k + 1) * half // 16]), values[:, k * half:(k + 1) * half])
-            else:
-                nc.vector.tensor_copy(window[:].indirect(index_list[:]), values)
-            nc.sync.dma_start(out_hbm[o][:, t, :], window[:])
-
-        for k in range(2):
-            nc.vector.memset(windows[0][k][:], 0.0)
-        for window in (windows[0][2], windows[1][0], windows[1][1]):
+        zeroed_by_vector = 2
+        for window in windows[0][:zeroed_by_vector]:
+            nc.vector.memset(window[:], 0.0)
+        for window in windows[0][zeroed_by_vector:] + windows[1]:
             nc.gpsimd.memset(window[:], 0.0)
 
         w_i = mx_tiles("w_i")
         h_i = mx_tiles("h_i")
-        quantise(w_i, E4M3, w_turned, 0, D)
-        h_turned = turn(h_flat.bitcast(F32).rearrange("p (q s u) -> p s u q", s=PACK, u=2), 4, "h_turned")
+        h_turned = turn(h_flat.bitcast(F32).rearrange("p (q s u) -> p s u q", s=PACK, u=2), (4, 0), "h_turned")
         quantise(h_i, E5M2, h_turned, 0, R)
-        item_gradient(2, 5)
-        for t in range(PACK):
-            ps = bank(t, [P, PACK, P], F32, "du_ps%d" % t)
-            product(ps[:].rearrange("m t p -> m (t p)"), w_i, t * P, h_i, E5M2, 0, R)
-            nc.scalar.copy(du[t][:], ps[:].rearrange("m t p -> m p t"))
-            if t == 1:
-                item_gradient(3, 1)
+        w_turned = turn(w_flat.bitcast(F32).rearrange("p (q s u) -> p s u q", s=PACK, u=2), (6, 4), "w_turned")
+        quantise(w_i, E4M3, w_turned, 0, D)
+        item_gradient(3, 4)
+        for t, number in enumerate((2, 3, 5, 7)):
+            ps = bank(number, [P, PACK, P], "du_ps%d" % t)
+            product(ps[:].rearrange("p s q -> p (s q)"), w_i, t * P, h_i, E5M2, 0, R)
+            nc.scalar.copy(du[t][:], ps[:].rearrange("p s q -> p q s"))
 
-        for o, t in ((0, 0), (0, 1), (0, 2), (1, 0), (1, 1), (0, 3), (1, 2), (1, 3)):
-            if o == 0:
-                place(0, t, dv[t][:], item_list)
-            else:
-                place(1, t, du[t][:].rearrange("m p t -> m (p t)"), user_list)
+        def scatter(o, t, offsets, values):
+            nc.vector.tensor_copy(windows[o][t % WINDOWS][:].indirect(offsets), values)
+
+        def store(o, t):
+            nc.sync.dma_start(out_hbm[o][:, t, :], windows[o][t % WINDOWS][:])
+
+        for t in range(2):
+            scatter(0, t, list_half(item_list, 0), dv_half[t, 0][:])
+        for t in range(2):
+            scatter(0, t, list_half(item_list, 1), dv_half[t, 1][:])
+            store(0, t)
+        for t in range(2, PACK):
+            scatter(0, t, item_list[:], dv[t][:])
+            store(0, t)
+        for t in range(PACK):
+            scatter(1, t, user_list[:], du[t][:].rearrange("p q s -> p (q s)"))
+            store(1, t)

@@ -93,78 +93,100 @@ def tile_attend_gmf_sq_vu_kernel(tc, uT, vT, y, us, ts, offs, uoffs, out_0, out_
         identity = sb.tile([P, P], F32, name="identity")
         make_identity(nc, identity[:])
 
-        def turn(pairs_of_t, banks, name):
-            turned = sb.tile([P, 2, 2, P, PACK], BF16, name=name, align_bytes=64)
-            for u in range(2):
-                ps = bank(banks[u], [P, PACK * P], "%s_ps%d" % (name, u))
-                for s in range(PACK):
-                    nc.tensor.transpose(ps[:, s * P:(s + 1) * P], pairs_of_t[:, s, u, :], identity[:])
-                nc.scalar.copy(turned[:, u, :, :, :], ps[:].bitcast(BF16).rearrange("q (s p e) -> q e p s", s=PACK, e=2))
-            return turned[:].rearrange("q u e p s -> q (u e p s)")
+        def turn_interleaved(turned, values, u, number, name):
+            words = values.bitcast(F32).rearrange("p (q s u) -> p s u q", s=PACK, u=2)
+            ps = bank(number, [P, PACK * P], name)
+            for s in range(PACK):
+                nc.tensor.transpose(ps[:, s * P:(s + 1) * P], words[:, s, u, :], identity[:])
+            nc.scalar.copy(
+                turned[:, u * 1024:(u + 1) * 1024].rearrange("q (e p s) -> q e p s", e=2, s=PACK),
+                ps[:].bitcast(BF16).rearrange("q (s p e) -> q e p s", s=PACK, e=2))
+
+        def turn_planes(turned, planes, u, number, name):
+            ps = bank(number, [P, 2, 2, P], name)
+            for e in range(2):
+                words = planes[:, e * N:(e + 1) * N].bitcast(F32).rearrange("p (q v) -> p v q", v=2)
+                for v in range(2):
+                    nc.tensor.transpose(ps[:, e, v, :], words[:, v, :], identity[:])
+            nc.scalar.copy(
+                turned[:, u * 1024:(u + 1) * 1024].bitcast(F32).rearrange("q (e p v) -> q e p v", e=2, v=2),
+                ps[:].rearrange("q e v p -> q e p v"))
 
         x = sb.tile([P, PACK, P, PACK], BF16, name="x", align_bytes=64)
-        x_gathered = sb.tile([P, PACK, R], F32, name="x_gathered")
-        nc.vector.tensor_copy(x_gathered[:, 0, :], u_rows[0][:].indirect(user_list[:]))
+        x_planes = [sb.tile([P, 2 * R], BF16, name="x_planes%d" % u) for u in range(2)]
+        nc.vector.tensor_copy(x_planes[0][:, 0:R], u_rows[0][:].indirect(user_list[:]))
         ts_gathered = sb.tile([P, N], F32, name="ts_gathered")
         nc.vector.tensor_copy(ts_gathered[:], ts_row[:].indirect(item_list[:]))
         for t in range(1, PACK):
-            nc.vector.tensor_copy(x_gathered[:, t, :], u_rows[t][:].indirect(user_list[:]))
+            nc.vector.tensor_copy(x_planes[t // 2][:, t % 2 * R:(t % 2 + 1) * R], u_rows[t][:].indirect(user_list[:]))
 
         ts_ps = bank(0, [P, PACK, P], "ts_ps")
         for c in range(N // P):
             nc.tensor.transpose(ts_ps[:, c, :], ts_gathered[:, c * P:(c + 1) * P], identity[:])
         ts_col = sb.tile([P, N // P], F32, name="ts_col")
         nc.scalar.copy(ts_col[:], ts_ps[:, :, 0])
-        ts_all = bank(1, [P, N], "ts_all")
-        for c in range(N // P):
+        direct, late = (0, 1), (2, 3)
+        SCALED = N
+        minus_us = sb.tile([P, PACK], F32, name="minus_us")
+        nc.scalar.activation(minus_us[:], us_col[:], COPY, scale=-1.0)
+        x_turned = sb.tile([P, PACK * D], BF16, name="x_turned", align_bytes=64)
+        for u in range(2):
+            nc.scalar.copy(
+                x[:, :, :, 2 * u:2 * u + 2].rearrange("p s q e -> p q e s"),
+                x_planes[u][:].rearrange("p (e q s) -> p q e s", e=2, s=PACK))
+            turn_planes(x_turned, x_planes[u][:], u, 4 + u, "x_turn%d" % u)
+        x_flat = x[:].rearrange("p s q t -> p (s q t)")
+        ts_all = bank(5, [P, SCALED], "ts_all")
+        for c in range(SCALED // P):
             nc.tensor.transpose(ts_all[:, c * P:(c + 1) * P], ts_col[:, c:c + 1].to_broadcast([P, P]), identity[:])
-        scale = sb.tile([P, PACK, N], F32, name="scale")
+        scale = sb.tile([P, PACK, SCALED], F32, name="scale", tag="scale", align_bytes=64)
         for t in range(PACK):
             nc.scalar.activation(scale[:, t, :], ts_all[:], COPY, scale=us_col[:, t:t + 1])
-        nc.scalar.copy(x[:].rearrange("p s q t -> p q t s"), x_gathered[:].rearrange("p t (q s) -> p q t s", s=PACK))
 
-        x_d = mx_tiles("x_d")
-        x_flat = x[:].rearrange("p s q t -> p (s q t)")
-        quantise(x_d, E4M3, x_flat, 0, R)
-        x_turned = turn(x_flat.bitcast(F32).rearrange("p (s q u) -> p s u q", s=PACK, u=2), (4, 5), "x_turned")
 
         w = sb.tile([P, N, PACK], BF16, name="w", align_bytes=64)
         w_flat = w[:].rearrange("p i t -> p (i t)")
+        w_turned = sb.tile([P, PACK * D], BF16, name="w_turned", align_bytes=64)
         w_d = mx_tiles("w_d")
         last = PACK - 1
-        for t in range(last):
-            nc.vector.tensor_copy(w[:, :, t], v_rows[t][:].indirect(item_list[:]))
+        nc.vector.tensor_copy(w[:, :, 0], v_rows[0][:].indirect(item_list[:]))
+        x_d = mx_tiles("x_d", tag="v_rows0")
+        quantise(x_d, E4M3, x_flat, 0, R)
+        nc.vector.tensor_copy(w[:, :, 1], v_rows[1][:].indirect(item_list[:]))
+        x_r = mx_tiles("x_r", tag="v_rows1")
+        quantise(x_r, E4M3, x_turned[:], 0, D)
+        nc.vector.tensor_copy(w[:, :, 2], v_rows[2][:].indirect(item_list[:]))
 
-        direct, turned_back = (0, 1), (2, 3)
         a_ps = {}
-        for k, chunks in enumerate((direct, turned_back)):
-            nc.vector.tensor_copy(w[:, k * HALF:(k + 1) * HALF, last], v_rows[last][:].indirect(list_half(item_list, k)))
-            for c in chunks:
-                quantise(w_d, E4M3, w_flat, c * CHUNK, CHUNK)
-                a_ps[c] = bank(c, [P, PACK, CHUNK], "a_ps%d" % c)
-                if c in direct:
-                    for t in range(PACK):
-                        product(a_ps[c][:, t, :], x_d, t * P, w_d, E4M3, c * CHUNK, CHUNK)
-                else:
-                    product(a_ps[c][:].rearrange("i t p -> i (t p)"), w_d, c * CHUNK, x_d, E4M3, 0, R)
-        x_r = mx_tiles("x_r", tag="v_rows%d" % last)
-        quantise(x_r, E4M3, x_turned, 0, D)
-
-        a_by_item = {}
-        a_by_row = {}
-        for c in turned_back:
-            a_by_item[c] = sb.tile([P, PACK, P], F32, name="a_by_item%d" % c)
-            nc.scalar.activation(a_by_item[c][:], a_ps[c][:], COPY, scale=ts_col[:, c:c + 1])
-        for c, number in zip(turned_back, (7, 5)):
-            ps = bank(number, [P, PACK, CHUNK], "a_back%d" % c)
-            a_by_row[c] = sb.tile([P, PACK, CHUNK], F32, name="a_by_row%d" % c, tag="a_by_row%d" % c)
+        nc.vector.tensor_copy(w[:, 0:HALF, last], v_rows[last][:].indirect(list_half(item_list, 0)))
+        for c in direct:
+            quantise(w_d, E4M3, w_flat, c * CHUNK, CHUNK)
+            a_ps[c] = bank(c, [P, PACK, CHUNK], "a_ps%d" % c)
             for t in range(PACK):
-                nc.tensor.transpose(ps[:, t, :], a_by_item[c][:, t, :], identity[:])
-            for t in range(PACK):
-                nc.scalar.activation(a_by_row[c][:, t, :], ps[:, t, :], COPY, scale=us_col[:, t:t + 1])
+                product(a_ps[c][:, t, :], x_d, t * P, w_d, E4M3, c * CHUNK, CHUNK)
+        nc.vector.tensor_copy(w[:, HALF:N, last], v_rows[last][:].indirect(list_half(item_list, 1)))
+        quantise(w_d, E4M3, w_flat, HALF, HALF)
+        late_ps = [bank(2 + u, [P, 2, HALF], "late_ps%d" % u) for u in range(2)]
+        for t in range(PACK):
+            product(late_ps[t // 2][:, t % 2, :], x_d, t * P, w_d, E4M3, HALF, HALF)
 
-        a = sb.tile([P, HALF // 2, PACK, 2], F32, name="a")
-        g = sb.tile([P, N // 2, PACK, 2], F32, name="g")
+        minus_us_y = sb.tile([P, PACK, HALF], F32, name="minus_us_y")
+        for t in range(PACK):
+            nc.scalar.activation(minus_us_y[:, t, :], y_sb[:, t, HALF:N], COPY, scale=minus_us[:, t:t + 1])
+        us_g = {c: bank(2 + c, [P, 2, 2, P], "us_g%d" % c) for c in late}
+
+        def add_turned(c, rows, first, final):
+            for t in range(PACK):
+                nc.tensor.matmul(
+                    us_g[c][:, t // 2, t % 2, :], rows[:, t, :], identity[:],
+                    start=first and t == 0, stop=final and t == last, is_transpose=True)
+
+        turn_interleaved(w_turned, w_flat, 0, 6, "w_turn0")
+        for c in late:
+            add_turned(c, minus_us_y[:, :, c * CHUNK - HALF:(c + 1) * CHUNK - HALF], True, False)
+
+        a = {c: sb.tile([P, CHUNK // 2, PACK, 2], F32, name="a%d" % c) for c in direct}
+        g = {c: sb.tile([P, CHUNK // 2, PACK, 2], F32, name="g%d" % c, tag="g%d" % c) for c in direct}
         h = sb.tile([P, N, PACK], BF16, name="h", align_bytes=64)
         h_flat = h[:].rearrange("p i t -> p (i t)")
         h_r = mx_tiles("h_r", HALF + N)
@@ -174,61 +196,71 @@ def tile_attend_gmf_sq_vu_kernel(tc, uT, vT, y, us, ts, offs, uoffs, out_0, out_
         def items(c):
             return slice(c * CHUNK, (c + 1) * CHUNK)
 
-        def item_pairs(c):
-            return slice(c * CHUNK // 2, (c + 1) * CHUNK // 2)
-
         def by_pairs(rows):
             return rows.rearrange("p t (j e) -> p j t e", e=2)
 
         def scale_a(c):
-            nc.vector.tensor_tensor(a[:, item_pairs(c), :, :], by_pairs(a_ps[c][:]), by_pairs(scale[:, :, items(c)]), MULT)
+            nc.vector.tensor_tensor(a[c][:], by_pairs(a_ps[c][:]), by_pairs(scale[:, :, items(c)]), MULT)
 
         def subtract_y(c):
-            scaled = a[:, item_pairs(c), :, :] if c in direct else by_pairs(a_by_row[c][:])
-            nc.vector.tensor_tensor(g[:, item_pairs(c), :, :], scaled, by_pairs(y_sb[:, :, items(c)]), SUB)
+            nc.vector.tensor_tensor(g[c][:], a[c][:], by_pairs(y_sb[:, :, items(c)]), SUB)
 
         def scale_g(c):
             nc.vector.tensor_tensor(
                 h[:, items(c), :].rearrange("p (j e) t -> p j t e", e=2),
-                g[:, item_pairs(c), :, :], by_pairs(scale[:, :, items(c)]), MULT)
+                g[c][:], by_pairs(scale[:, :, items(c)]), MULT)
 
         def quantise_h(c):
             quantise(h_r, E5M2, h_flat, c * CHUNK, CHUNK, HALF)
-
-        dv = {t: sb.tile([P, N], F32, name="dv%d" % t) for t in range(2, PACK)}
-
-        for step in (scale_a, subtract_y, scale_g):
-            for c in direct:
-                step(c)
-        subtract_y(turned_back[0])
-        for c in direct:
-            quantise_h(c)
-        subtract_y(turned_back[1])
-        for step in (scale_g, quantise_h):
-            for c in turned_back:
-                step(c)
 
         windows = [[sb.tile([P, T], F32, name="window%d_%d" % (o, k)) for k in range(WINDOWS)] for o in range(2)]
         out_hbm = [out.rearrange("(p t) n -> p t n", t=PACK) for out in (out_0, out_1)]
         du = [sb.tile([P, P, PACK], F32, name="du%d" % t) for t in range(PACK)]
         dv_half = {}
+        dv_ps = {}
 
-        def item_gradient_half(t, k, number, tag):
-            ps = bank(number, [P, N], "dv_ps%d_%d" % (t, k))
-            product(ps[:], x_r, t * P, h_r, E5M2, k * HALF, N)
+        def half_product(t, k, number):
+            dv_ps[t, k] = bank(number, [P, N], "dv_ps%d_%d" % (t, k))
+            product(dv_ps[t, k][:], x_r, t * P, h_r, E5M2, k * HALF, N)
+
+        def half_copy(t, k, tag):
             dv_half[t, k] = sb.tile([P, HALF], F32, name="dv%d_%d" % (t, k), tag=tag)
-            nc.scalar.copy(dv_half[t, k][:], ps[:, HALF:N])
+            nc.scalar.copy(dv_half[t, k][:], dv_ps[t, k][:, HALF:N])
 
-        def item_gradient(t, number):
-            ps = bank(number, [P, N], "dv_ps%d" % t)
-            product(ps[:], x_r, t * P, h_r, E5M2, HALF, N)
-            nc.scalar.copy(dv[t][:], ps[:])
-
-        item_gradient_half(0, 0, 6, "a_by_row%d" % turned_back[0])
-        item_gradient_half(1, 0, 1, "a_by_row%d" % turned_back[1])
-        item_gradient_half(0, 1, 4, "dv0_1")
-        item_gradient_half(1, 1, 0, "dv1_1")
-        item_gradient(2, 0)
+        for step in (scale_a, subtract_y, scale_g, quantise_h):
+            for c in direct:
+                step(c)
+        half_product(0, 0, 0)
+        half_copy(0, 0, "dv0_0")
+        h_by_item = {}
+        for c in late:
+            us_a = sb.tile([P, PACK, CHUNK], F32, name="us_a%d" % c, tag="g%d" % (c - 2))
+            for t in range(PACK):
+                nc.vector.scalar_tensor_tensor(
+                    us_a[:, t, :], late_ps[t // 2][:, t % 2, items(c - 2)], us_col[:, t:t + 1], scale[:, t, items(c)],
+                    MULT, MULT)
+            add_turned(c, us_a[:], False, True)
+            h_by_item[c] = sb.tile([P, 2, P, 2], BF16, name="h_by_item%d" % c, tag="h_by_item%d" % c)
+            nc.scalar.activation(
+                h_by_item[c][:], us_g[c][:].rearrange("i u e q -> i u q e"), COPY, scale=ts_col[:, c:c + 1])
+        w_i = mx_tiles("w_i", tag="scale")
+        quantise(w_i, E4M3, w_turned[:], 0, D // 2)
+        half_product(1, 0, 1)
+        half_copy(1, 0, "dv1_0")
+        for c, number in zip(late, (7, 2)):
+            ps = bank(number, [P, 2, P], "h_back%d" % c)
+            words = h_by_item[c][:].rearrange("i u q e -> i (u q e)").bitcast(F32)
+            for u in range(2):
+                nc.tensor.transpose(ps[:, u, :], words[:, u * P:(u + 1) * P], identity[:])
+            nc.scalar.copy(
+                h_flat[:, c * CHUNK * PACK:(c + 1) * CHUNK * PACK].bitcast(F32).rearrange("q (i u) -> q i u", u=2),
+                ps[:].rearrange("q u i -> q i u"))
+            quantise_h(c)
+        half_product(2, 0, 6)
+        half_copy(2, 0, "h_by_item3")
+        for t, number in enumerate((4, 0, 5)):
+            half_product(t, 1, number)
+            half_copy(t, 1, "dv%d_1" % t)
 
         zeroed_by_vector = 2
         for window in windows[0][:zeroed_by_vector]:
@@ -236,14 +268,18 @@ def tile_attend_gmf_sq_vu_kernel(tc, uT, vT, y, us, ts, offs, uoffs, out_0, out_
         for window in windows[0][zeroed_by_vector:] + windows[1]:
             nc.gpsimd.memset(window[:], 0.0)
 
-        w_i = mx_tiles("w_i")
         h_i = mx_tiles("h_i")
-        h_turned = turn(h_flat.bitcast(F32).rearrange("p (q s u) -> p s u q", s=PACK, u=2), (4, 0), "h_turned")
-        quantise(h_i, E5M2, h_turned, 0, R)
-        w_turned = turn(w_flat.bitcast(F32).rearrange("p (q s u) -> p s u q", s=PACK, u=2), (6, 4), "w_turned")
-        quantise(w_i, E4M3, w_turned, 0, D)
-        item_gradient(3, 4)
-        for t, number in enumerate((2, 3, 5, 7)):
+        h_turned = sb.tile([P, PACK * R], BF16, name="h_turned", align_bytes=64)
+        for u, number in enumerate((4, 0)):
+            turn_interleaved(h_turned, h_flat, u, number, "h_turn%d" % u)
+        quantise(h_i, E5M2, h_turned[:], 0, R)
+        turn_interleaved(w_turned, w_flat, 1, 4, "w_turn1")
+        quantise(w_i, E4M3, w_turned[:], D // 2, D // 2)
+        ps = bank(4, [P, N], "dv_ps3")
+        product(ps[:], x_r, last * P, h_r, E5M2, HALF, N)
+        dv_last = sb.tile([P, N], F32, name="dv_last")
+        nc.scalar.copy(dv_last[:], ps[:])
+        for t, number in enumerate((4, 4, 4, 4)):
             ps = bank(number, [P, PACK, P], "du_ps%d" % t)
             product(ps[:].rearrange("p s q -> p (s q)"), w_i, t * P, h_i, E5M2, 0, R)
             nc.scalar.copy(du[t][:], ps[:].rearrange("p s q -> p q s"))
@@ -254,14 +290,13 @@ def tile_attend_gmf_sq_vu_kernel(tc, uT, vT, y, us, ts, offs, uoffs, out_0, out_
         def store(o, t):
             nc.sync.dma_start(out_hbm[o][:, t, :], windows[o][t % WINDOWS][:])
 
-        for t in range(2):
+        for t in range(last):
             scatter(0, t, list_half(item_list, 0), dv_half[t, 0][:])
-        for t in range(2):
+        for t in range(last):
             scatter(0, t, list_half(item_list, 1), dv_half[t, 1][:])
             store(0, t)
-        for t in range(2, PACK):
-            scatter(0, t, item_list[:], dv[t][:])
-            store(0, t)
+        scatter(0, last, item_list[:], dv_last[:])
+        store(0, last)
         for t in range(PACK):
             scatter(1, t, user_list[:], du[t][:].rearrange("p q s -> p (q s)"))
             store(1, t)

@@ -187,7 +187,7 @@ def tile_attend_gmf_sq_vu_kernel(tc, uT, vT, y, us, ts, offs, uoffs, out_0, out_
 
         a = {c: sb.tile([P, CHUNK // 2, PACK, 2], F32, name="a%d" % c) for c in direct}
         g = {c: sb.tile([P, CHUNK // 2, PACK, 2], F32, name="g%d" % c, tag="g%d" % c) for c in direct}
-        h = sb.tile([P, N, PACK], BF16, name="h", align_bytes=64)
+        h = sb.tile([P, N, PACK], BF16, name="h", tag="h", align_bytes=64)
         h_flat = h[:].rearrange("p i t -> p (i t)")
         h_r = mx_tiles("h_r", HALF + N)
         nc.gpsimd.memset(h_r[0][:, 0:HALF], 0)
@@ -268,18 +268,18 @@ def tile_attend_gmf_sq_vu_kernel(tc, uT, vT, y, us, ts, offs, uoffs, out_0, out_
         for window in windows[0][zeroed_by_vector:] + windows[1]:
             nc.gpsimd.memset(window[:], 0.0)
 
+        last_ps = bank(1, [P, N], "dv_ps3")
+        product(last_ps[:], x_r, last * P, h_r, E5M2, HALF, N)
         h_i = mx_tiles("h_i")
         h_turned = sb.tile([P, PACK * R], BF16, name="h_turned", align_bytes=64)
         for u, number in enumerate((4, 0)):
             turn_interleaved(h_turned, h_flat, u, number, "h_turn%d" % u)
         quantise(h_i, E5M2, h_turned[:], 0, R)
-        turn_interleaved(w_turned, w_flat, 1, 4, "w_turn1")
+        dv_last = sb.tile([P, N], F32, name="dv_last", tag="h", align_bytes=64)
+        nc.scalar.copy(dv_last[:], last_ps[:])
+        turn_interleaved(w_turned, w_flat, 1, 5, "w_turn1")
         quantise(w_i, E4M3, w_turned[:], D // 2, D // 2)
-        ps = bank(4, [P, N], "dv_ps3")
-        product(ps[:], x_r, last * P, h_r, E5M2, HALF, N)
-        dv_last = sb.tile([P, N], F32, name="dv_last")
-        nc.scalar.copy(dv_last[:], ps[:])
-        for t, number in enumerate((4, 4, 4, 4)):
+        for t, number in enumerate((3, 7, 2, 6)):
             ps = bank(number, [P, PACK, P], "du_ps%d" % t)
             product(ps[:].rearrange("p s q -> p (s q)"), w_i, t * P, h_i, E5M2, 0, R)
             nc.scalar.copy(du[t][:], ps[:].rearrange("p s q -> p q s"))

@@ -102,23 +102,13 @@ def tile_attend_gmf_sq_vu_kernel(tc, uT, vT, y, us, ts, offs, uoffs, out_0, out_
                 turned[:, u * 1024:(u + 1) * 1024].rearrange("q (e p s) -> q e p s", e=2, s=PACK),
                 ps[:].bitcast(BF16).rearrange("q (s p e) -> q e p s", s=PACK, e=2))
 
-        def turn_planes(turned, planes, u, number, name):
-            ps = bank(number, [P, 2, 2, P], name)
-            for e in range(2):
-                words = planes[:, e * N:(e + 1) * N].bitcast(F32).rearrange("p (q v) -> p v q", v=2)
-                for v in range(2):
-                    nc.tensor.transpose(ps[:, e, v, :], words[:, v, :], identity[:])
-            nc.scalar.copy(
-                turned[:, u * 1024:(u + 1) * 1024].bitcast(F32).rearrange("q (e p v) -> q e p v", e=2, v=2),
-                ps[:].rearrange("q e v p -> q e p v"))
-
         x = sb.tile([P, PACK, P, PACK], BF16, name="x", align_bytes=64)
-        x_planes = [sb.tile([P, 2 * R], BF16, name="x_planes%d" % u) for u in range(2)]
-        nc.vector.tensor_copy(x_planes[0][:, 0:R], u_rows[0][:].indirect(user_list[:]))
+        x_gathered = sb.tile([P, PACK, R], F32, name="x_gathered")
+        nc.vector.tensor_copy(x_gathered[:, 0, :], u_rows[0][:].indirect(user_list[:]))
         ts_gathered = sb.tile([P, N], F32, name="ts_gathered")
         nc.vector.tensor_copy(ts_gathered[:], ts_row[:].indirect(item_list[:]))
         for t in range(1, PACK):
-            nc.vector.tensor_copy(x_planes[t // 2][:, t % 2 * R:(t % 2 + 1) * R], u_rows[t][:].indirect(user_list[:]))
+            nc.vector.tensor_copy(x_gathered[:, t, :], u_rows[t][:].indirect(user_list[:]))
 
         ts_ps = bank(0, [P, PACK, P], "ts_ps")
         for c in range(N // P):
@@ -130,11 +120,13 @@ def tile_attend_gmf_sq_vu_kernel(tc, uT, vT, y, us, ts, offs, uoffs, out_0, out_
         minus_us = sb.tile([P, PACK], F32, name="minus_us")
         nc.scalar.activation(minus_us[:], us_col[:], COPY, scale=-1.0)
         x_turned = sb.tile([P, PACK * D], BF16, name="x_turned", align_bytes=64)
-        for u in range(2):
+        nc.scalar.copy(x[:].rearrange("p s q t -> p q t s"), x_gathered[:].rearrange("p t (q s) -> p q t s", s=PACK))
+        for t in range(PACK):
+            ps = bank(4 + t % 2, [P, PACK, P], "x_turn%d" % t)
+            for s in range(PACK):
+                nc.tensor.transpose(ps[:, s, :], x_gathered[:, t, :].rearrange("p (q s) -> p s q", s=PACK)[:, s, :], identity[:])
             nc.scalar.copy(
-                x[:, :, :, 2 * u:2 * u + 2].rearrange("p s q e -> p q e s"),
-                x_planes[u][:].rearrange("p (e q s) -> p q e s", e=2, s=PACK))
-            turn_planes(x_turned, x_planes[u][:], u, 4 + u, "x_turn%d" % u)
+                x_turned[:, t * D:(t + 1) * D].rearrange("q (p s) -> q p s", s=PACK), ps[:].rearrange("q s p -> q p s"))
         x_flat = x[:].rearrange("p s q t -> p (s q t)")
         ts_all = bank(5, [P, SCALED], "ts_all")
         for c in range(SCALED // P):

@@ -224,6 +224,8 @@ def tile_attend_gmf_sq_vu_kernel(tc, uT, vT, y, us, ts, offs, uoffs, out_0, out_
                 step(c)
         half_product(0, 0, 0)
         half_copy(0, 0, "dv0_0")
+        half_product(1, 0, 1)
+        half_copy(1, 0, "dv1_0")
         h_by_item = {}
         for c in late:
             us_a = sb.tile([P, PACK, CHUNK], F32, name="us_a%d" % c, tag="g%d" % (c - 2))
@@ -237,8 +239,6 @@ def tile_attend_gmf_sq_vu_kernel(tc, uT, vT, y, us, ts, offs, uoffs, out_0, out_
                 h_by_item[c][:], us_g[c][:].rearrange("i u e q -> i u q e"), COPY, scale=ts_col[:, c:c + 1])
         w_i = mx_tiles("w_i", tag="scale")
         quantise(w_i, E4M3, w_turned[:], 0, D // 2)
-        half_product(1, 0, 1)
-        half_copy(1, 0, "dv1_0")
         for c, number in zip(late, (7, 2)):
             ps = bank(number, [P, 2, P], "h_back%d" % c)
             words = h_by_item[c][:].rearrange("i u q e -> i (u q e)").bitcast(F32)

@@ -205,9 +205,9 @@ def tile_attend_gmf_sq_vu_kernel(tc, uT, vT, y, us, ts, offs, uoffs, out_0, out_
         def quantise_h(c):
             quantise(h_r, E5M2, h_flat, c * CHUNK, CHUNK, HALF)
 
-        windows = [[sb.tile([P, T], F32, name="window%d_%d" % (o, k)) for k in range(WINDOWS)] for o in range(2)]
+        windows = [[sb.tile([P, T], F32, name="window%d_%d" % (o, k)) for k in range(count)] for o, count in enumerate((4, 2))]
         out_hbm = [out.rearrange("(p t) n -> p t n", t=PACK) for out in (out_0, out_1)]
-        du = [sb.tile([P, P, PACK], F32, name="du%d" % t) for t in range(PACK)]
+        du = [sb.tile([P, P, PACK], F32, name="du%d" % t, tag="du%d" % t) for t in range(PACK)]
         dv_half = {}
         dv_ps = {}
 
@@ -267,8 +267,8 @@ def tile_attend_gmf_sq_vu_kernel(tc, uT, vT, y, us, ts, offs, uoffs, out_0, out_
         for u, number in enumerate((4, 0)):
             turn_interleaved(h_turned, h_flat, u, number, "h_turn%d" % u)
         quantise(h_i, E5M2, h_turned[:], 0, R)
-        dv_last = sb.tile([P, N], F32, name="dv_last", tag="h", align_bytes=64)
-        nc.scalar.copy(dv_last[:], last_ps[:])
+        dv_half[last, 0] = sb.tile([P, HALF], F32, name="dv3_0", tag="h", align_bytes=64)
+        nc.scalar.copy(dv_half[last, 0][:], last_ps[:, 0:HALF])
         turn_interleaved(w_turned, w_flat, 1, 5, "w_turn1")
         quantise(w_i, E4M3, w_turned[:], D // 2, D // 2)
         for t, number in enumerate((3, 7, 2, 6)):
@@ -277,18 +277,26 @@ def tile_attend_gmf_sq_vu_kernel(tc, uT, vT, y, us, ts, offs, uoffs, out_0, out_
             nc.scalar.copy(du[t][:], ps[:].rearrange("p s q -> p q s"))
 
         def scatter(o, t, offsets, values):
-            nc.vector.tensor_copy(windows[o][t % WINDOWS][:].indirect(offsets), values)
+            nc.vector.tensor_copy(windows[o][t % len(windows[o])][:].indirect(offsets), values)
 
         def store(o, t):
-            nc.sync.dma_start(out_hbm[o][:, t, :], windows[o][t % WINDOWS][:])
+            nc.sync.dma_start(out_hbm[o][:, t, :], windows[o][t % len(windows[o])][:])
+
+        def user_block(t):
+            scatter(1, t, user_list[:], du[t][:].rearrange("p q s -> p (q s)"))
+            store(1, t)
 
         for t in range(last):
             scatter(0, t, list_half(item_list, 0), dv_half[t, 0][:])
         for t in range(last):
             scatter(0, t, list_half(item_list, 1), dv_half[t, 1][:])
             store(0, t)
-        scatter(0, last, item_list[:], dv_last[:])
+        scatter(0, last, list_half(item_list, 0), dv_half[last, 0][:])
+        user_block(0)
+        user_block(1)
+        dv_half[last, 1] = sb.tile([P, HALF], F32, name="dv3_1", tag="du0")
+        nc.scalar.copy(dv_half[last, 1][:], last_ps[:, HALF:N])
+        scatter(0, last, list_half(item_list, 1), dv_half[last, 1][:])
         store(0, last)
-        for t in range(PACK):
-            scatter(1, t, user_list[:], du[t][:].rearrange("p q s -> p (q s)"))
-            store(1, t)
+        user_block(2)
+        user_block(3)

@@ -131,23 +131,25 @@ def tile_attend_gmf_sq_vu_kernel(tc, uT, vT, y, us, ts, offs, uoffs, out_0, out_
         ts_all = bank(5, [P, SCALED], "ts_all")
         for c in range(SCALED // P):
             nc.tensor.transpose(ts_all[:, c * P:(c + 1) * P], ts_col[:, c:c + 1].to_broadcast([P, P]), identity[:])
-        scale = sb.tile([P, PACK, SCALED], F32, name="scale", tag="scale", align_bytes=64)
-        for t in range(PACK):
-            nc.scalar.activation(scale[:, t, :], ts_all[:], COPY, scale=us_col[:, t:t + 1])
-
-
         w = sb.tile([P, N, PACK], BF16, name="w", align_bytes=64)
         w_flat = w[:].rearrange("p i t -> p (i t)")
         w_turned = sb.tile([P, PACK * D], BF16, name="w_turned", align_bytes=64)
         w_d = mx_tiles("w_d")
         last = PACK - 1
-        nc.vector.tensor_copy(w[:, :, 0], v_rows[0][:].indirect(item_list[:]))
+        w_gathered = sb.tile([P, 2, N], F32, name="w_gathered")
+        nc.vector.tensor_copy(w_gathered[:, 0, :], v_rows[0][:].indirect(item_list[:]))
         x_d = mx_tiles("x_d", tag="v_rows0")
         quantise(x_d, E4M3, x_flat, 0, R)
-        nc.vector.tensor_copy(w[:, :, 1], v_rows[1][:].indirect(item_list[:]))
+        nc.vector.tensor_copy(w_gathered[:, 1, :], v_rows[1][:].indirect(item_list[:]))
+        nc.scalar.copy(
+            w[:, :, 0:2].rearrange("p (j f) e -> p j e f", f=4), w_gathered[:].rearrange("p e (j f) -> p j e f", f=4))
         x_r = mx_tiles("x_r", tag="v_rows1")
         quantise(x_r, E4M3, x_turned[:], 0, D)
         nc.vector.tensor_copy(w[:, :, 2], v_rows[2][:].indirect(item_list[:]))
+
+        scale = sb.tile([P, PACK, SCALED], F32, name="scale", tag="scale", align_bytes=64)
+        for t in range(PACK):
+            nc.scalar.activation(scale[:, t, :], ts_all[:], COPY, scale=us_col[:, t:t + 1])
 
         a_ps = {}
         nc.vector.tensor_copy(w[:, 0:HALF, last], v_rows[last][:].indirect(list_half(item_list, 0)))

@@ -22,6 +22,7 @@ E4M3 = mybir.dt.float8_e4m3fn_x4
 E5M2 = mybir.dt.float8_e5m2_x4
 MULT = mybir.AluOpType.mult
 SUB = mybir.AluOpType.subtract
+ADD = mybir.AluOpType.add
 COPY = mybir.ActivationFunctionType.Copy
 
 
@@ -48,10 +49,10 @@ def tile_attend_gmf_sq_vu_kernel(tc, uT, vT, y, us, ts, offs, uoffs, out_0, out_
                 in_=values[:, PACK * first:PACK * (first + count)],
             )
 
-        def product(out, lhs, lhs_first, rhs, rhs_fmt, rhs_first, rhs_count):
+        def product(out, lhs, lhs_first, rhs, rhs_fmt, rhs_first, rhs_count, lhs_fmt=E4M3):
             nc.tensor.matmul_mx(
                 out=out,
-                lhsT=lhs[0][:, lhs_first:lhs_first + P].bitcast(E4M3),
+                lhsT=lhs[0][:, lhs_first:lhs_first + P].bitcast(lhs_fmt),
                 lhsT_scale=lhs[1][:, lhs_first:lhs_first + P],
                 rhs=rhs[0][:, rhs_first:rhs_first + rhs_count].bitcast(rhs_fmt),
                 rhs_scale=rhs[1][:, rhs_first:rhs_first + rhs_count],
@@ -59,39 +60,43 @@ def tile_attend_gmf_sq_vu_kernel(tc, uT, vT, y, us, ts, offs, uoffs, out_0, out_
                 stop=True,
             )
 
-        def list_half(index_list, k):
-            return index_list[:, k * HALF // PER_COLUMN:(k + 1) * HALF // PER_COLUMN]
+        def list_part(index_list, first, count):
+            return index_list[:, first // PER_COLUMN:(first + count) // PER_COLUMN]
 
         item_list = lists.tile([P, N // PER_COLUMN], U16, name="item_list")
         user_list = lists.tile([P, R // PER_COLUMN], U16, name="user_list")
-        u_rows = [sb.tile([P, T], F32, name="u_rows%d" % t) for t in range(PACK)]
+        u_rows = [sb.tile([P, T], F32, name="u_rows%d" % t, tag="u_rows%d" % t) for t in range(PACK)]
         v_rows = [sb.tile([P, T], F32, name="v_rows%d" % t, tag="v_rows%d" % t, align_bytes=64) for t in range(PACK)]
-        ts_row = sb.tile([P, T], F32, name="ts_row")
+        ts_row = sb.tile([P, T], F32, name="ts_row", tag="ts_row")
         us_col = sb.tile([P, PACK], F32, name="us_col")
-        y_sb = sb.tile([P, PACK, N], F32, name="y_sb")
+        y_first = sb.tile([P, PACK, CHUNK], F32, name="y_first")
+        y_late = sb.tile([P, PACK, N - CHUNK], F32, name="y_late")
         u_hbm = uT.rearrange("(p t) n -> p t n", t=PACK)
         v_hbm = vT.rearrange("(p t) n -> p t n", t=PACK)
 
-        def load_in_two(t):
-            for k in range(2):
-                columns = slice(k * T // 2, (k + 1) * T // 2)
-                nc.sync.dma_start(u_rows[t][:, columns], u_hbm[:, t, columns])
-
-        nc.gpsimd.memset(ts_row[:], 0.0)
-        load_in_two(0)
+        ts_runs = sb.tile([P, T // P], F32, name="ts_runs", tag="x", align_bytes=64)
+        nc.sync.dma_start(ts_runs[:], ts[0:1, :].rearrange("o (p k) -> p (o k)", p=P))
+        nc.sync.dma_start(u_rows[0][:], u_hbm[:, 0, :])
         nc.sync.dma_start(user_list[:], uoffs)
         nc.sync.dma_start(item_list[:], offs)
         nc.sync.dma_start(us_col[:], us.rearrange("b (p t) o -> p (b t o)", t=PACK))
-        nc.scalar.dma_start(ts_row[0:1, :], ts[0:1, :])
-        load_in_two(1)
-        for t in range(2, PACK):
+        for t in range(1, PACK):
             nc.sync.dma_start(u_rows[t][:], u_hbm[:, t, :])
         for t in range(PACK):
             nc.sync.dma_start(v_rows[t][:], v_hbm[:, t, :])
-        nc.sync.dma_start(y_sb[:], y.rearrange("b (p t) i -> p (b t) i", t=PACK))
+        y_hbm = y.rearrange("b (p t) i -> p (b t) i", t=PACK)
+        nc.sync.dma_start(y_first[:], y_hbm[:, :, 0:CHUNK])
+        nc.sync.dma_start(y_late[:], y_hbm[:, :, CHUNK:N])
 
         identity = sb.tile([P, P], F32, name="identity")
         make_identity(nc, identity[:])
+        for b in range(T // P // PACK):
+            ps = bank(b, [P, PACK, P], "ts_spread%d" % b)
+            for k in range(PACK):
+                column = b * PACK + k
+                nc.tensor.transpose(ps[:, k, :], ts_runs[:, column:column + 1].to_broadcast([P, P]), identity[:])
+            nc.scalar.copy(
+                ts_row[:].rearrange("m (n b k) -> m b n k", b=T // P // PACK, k=PACK)[:, b], ps[:].rearrange("m k n -> m n k"))
 
         def turn_interleaved(turned, values, u, number, name):
             words = values.bitcast(F32).rearrange("p (q s u) -> p s u q", s=PACK, u=2)
@@ -102,72 +107,82 @@ def tile_attend_gmf_sq_vu_kernel(tc, uT, vT, y, us, ts, offs, uoffs, out_0, out_
                 turned[:, u * 1024:(u + 1) * 1024].rearrange("q (e p s) -> q e p s", e=2, s=PACK),
                 ps[:].bitcast(BF16).rearrange("q (s p e) -> q e p s", s=PACK, e=2))
 
-        x = sb.tile([P, PACK, P, PACK], BF16, name="x", align_bytes=64)
-        x_gathered = sb.tile([P, PACK, R], F32, name="x_gathered")
-        nc.vector.tensor_copy(x_gathered[:, 0, :], u_rows[0][:].indirect(user_list[:]))
+        x = sb.tile([P, PACK, P, PACK], BF16, name="x", tag="x", align_bytes=64)
         ts_gathered = sb.tile([P, N], F32, name="ts_gathered")
         nc.vector.tensor_copy(ts_gathered[:], ts_row[:].indirect(item_list[:]))
-        for t in range(1, PACK):
-            nc.vector.tensor_copy(x_gathered[:, t, :], u_rows[t][:].indirect(user_list[:]))
 
         ts_ps = bank(0, [P, PACK, P], "ts_ps")
         for c in range(N // P):
             nc.tensor.transpose(ts_ps[:, c, :], ts_gathered[:, c * P:(c + 1) * P], identity[:])
         ts_col = sb.tile([P, N // P], F32, name="ts_col")
         nc.scalar.copy(ts_col[:], ts_ps[:, :, 0])
-        direct, late = (0, 1), (2, 3)
-        SCALED = N
-        minus_us = sb.tile([P, PACK], F32, name="minus_us")
-        nc.scalar.activation(minus_us[:], us_col[:], COPY, scale=-1.0)
-        x_turned = sb.tile([P, PACK * D], BF16, name="x_turned", align_bytes=64)
-        nc.scalar.copy(x[:].rearrange("p s q t -> p q t s"), x_gathered[:].rearrange("p t (q s) -> p q t s", s=PACK))
+        late = (1, 2, 3)
+        scale = sb.tile([P, PACK, N], F32, name="scale")
         for t in range(PACK):
-            ps = bank(4 + t % 2, [P, PACK, P], "x_turn%d" % t)
+            nc.scalar.activation(scale[:, t, :], ts_gathered[:], COPY, scale=us_col[:, t:t + 1])
+        x_turned = sb.tile([P, PACK * D], BF16, name="x_turned", tag="x_turned", align_bytes=64)
+        x_gathered = [sb.tile([P, 2 * R], F32, name="x_gathered%d" % u, tag=tag) for u, tag in enumerate(("x_gathered", "ts_row"))]
+        for t in range(PACK):
+            u, e = divmod(t, 2)
+            nc.vector.tensor_copy(x_gathered[u][:, e * R:(e + 1) * R], u_rows[t][:].indirect(user_list[:]))
+            if e == 1:
+                nc.scalar.copy(
+                    x[:, :, :, 2 * u:2 * u + 2].rearrange("p s q e -> p q e s"),
+                    x_gathered[u][:].rearrange("p (e q s) -> p q e s", e=2, s=PACK))
+            ps = bank(4 + e, [P, PACK, P], "x_turn%d" % t)
             for s in range(PACK):
-                nc.tensor.transpose(ps[:, s, :], x_gathered[:, t, :].rearrange("p (q s) -> p s q", s=PACK)[:, s, :], identity[:])
+                nc.tensor.transpose(ps[:, s, :], x_gathered[u][:, e * R + s:(e + 1) * R:PACK], identity[:])
             nc.scalar.copy(
                 x_turned[:, t * D:(t + 1) * D].rearrange("q (p s) -> q p s", s=PACK), ps[:].rearrange("q s p -> q p s"))
         x_flat = x[:].rearrange("p s q t -> p (s q t)")
-        ts_all = bank(5, [P, SCALED], "ts_all")
-        for c in range(SCALED // P):
-            nc.tensor.transpose(ts_all[:, c * P:(c + 1) * P], ts_col[:, c:c + 1].to_broadcast([P, P]), identity[:])
-        w = sb.tile([P, N, PACK], BF16, name="w", align_bytes=64)
-        w_flat = w[:].rearrange("p i t -> p (i t)")
         w_turned = sb.tile([P, PACK * D], BF16, name="w_turned", align_bytes=64)
         w_d = mx_tiles("w_d")
         last = PACK - 1
-        w_gathered = sb.tile([P, 2, N], F32, name="w_gathered")
-        nc.vector.tensor_copy(w_gathered[:, 0, :], v_rows[0][:].indirect(item_list[:]))
+        w_gathered = sb.tile([P, 2 * N], F32, name="w_gathered", tag="u_rows3")
+
+        def turn_w_plane(t):
+            ps = bank(6 + t, [P, PACK, P], "w_turn_plane%d" % t)
+            for s in range(PACK):
+                nc.tensor.transpose(ps[:, s, :], w_gathered[:, t * N + s:(t + 1) * N:PACK], identity[:])
+            nc.scalar.copy(
+                w_turned[:, t * D:(t + 1) * D].rearrange("q (p s) -> q p s", s=PACK), ps[:].rearrange("q s p -> q p s"))
+
+        nc.vector.tensor_copy(w_gathered[:, 0:N], v_rows[0][:].indirect(item_list[:]))
+        turn_w_plane(0)
         x_d = mx_tiles("x_d", tag="v_rows0")
         quantise(x_d, E4M3, x_flat, 0, R)
-        nc.vector.tensor_copy(w_gathered[:, 1, :], v_rows[1][:].indirect(item_list[:]))
-        nc.scalar.copy(
-            w[:, :, 0:2].rearrange("p (j f) e -> p j e f", f=4), w_gathered[:].rearrange("p e (j f) -> p j e f", f=4))
-        x_r = mx_tiles("x_r", tag="v_rows1")
+        x_r = mx_tiles("x_r", tag="x")
         quantise(x_r, E4M3, x_turned[:], 0, D)
+        w = sb.tile([P, N, PACK], BF16, name="w", tag="x_turned", align_bytes=64)
+        w_flat = w[:].rearrange("p i t -> p (i t)")
+        nc.vector.tensor_copy(w_gathered[:, N:2 * N], v_rows[1][:].indirect(item_list[:]))
+        nc.scalar.copy(
+            w[:, :, 0:2].rearrange("p (j f) e -> p j e f", f=4), w_gathered[:].rearrange("p (e j f) -> p j e f", e=2, f=4))
+        turn_w_plane(1)
         nc.vector.tensor_copy(w[:, :, 2], v_rows[2][:].indirect(item_list[:]))
 
-        scale = sb.tile([P, PACK, SCALED], F32, name="scale", tag="scale", align_bytes=64)
-        for t in range(PACK):
-            nc.scalar.activation(scale[:, t, :], ts_all[:], COPY, scale=us_col[:, t:t + 1])
+        def items(c):
+            return slice(c * CHUNK, (c + 1) * CHUNK)
 
         a_ps = {}
-        nc.vector.tensor_copy(w[:, 0:HALF, last], v_rows[last][:].indirect(list_half(item_list, 0)))
-        for c in direct:
+        nc.vector.tensor_copy(w[:, 0:HALF, last], v_rows[last][:].indirect(list_part(item_list, 0, HALF)))
+        for c in range(2):
             quantise(w_d, E4M3, w_flat, c * CHUNK, CHUNK)
-            a_ps[c] = bank(c, [P, PACK, CHUNK], "a_ps%d" % c)
+            ps = bank(c, [P, PACK, CHUNK], "a_ps%d" % c)
             for t in range(PACK):
-                product(a_ps[c][:, t, :], x_d, t * P, w_d, E4M3, c * CHUNK, CHUNK)
-        nc.vector.tensor_copy(w[:, HALF:N, last], v_rows[last][:].indirect(list_half(item_list, 1)))
-        quantise(w_d, E4M3, w_flat, HALF, HALF)
-        late_ps = [bank(2 + u, [P, 2, HALF], "late_ps%d" % u) for u in range(2)]
-        for t in range(PACK):
-            product(late_ps[t // 2][:, t % 2, :], x_d, t * P, w_d, E4M3, HALF, HALF)
+                product(ps[:, t, :], x_d, t * P, w_d, E4M3, c * CHUNK, CHUNK)
+                a_ps[c, t] = ps[:, t, :]
+            if c == 0:
+                first_ps = ps
+        nc.vector.tensor_copy(w[:, HALF:N, last], v_rows[last][:].indirect(list_part(item_list, HALF, HALF)))
 
-        minus_us_y = sb.tile([P, PACK, HALF], F32, name="minus_us_y")
-        for t in range(PACK):
-            nc.scalar.activation(minus_us_y[:, t, :], y_sb[:, t, HALF:N], COPY, scale=minus_us[:, t:t + 1])
-        us_g = {c: bank(2 + c, [P, 2, 2, P], "us_g%d" % c) for c in late}
+        minus_us = sb.tile([P, PACK], F32, name="minus_us", tag="v_rows3", align_bytes=64)
+        nc.scalar.activation(minus_us[:], us_col[:], COPY, scale=-1.0)
+        minus_us_y = sb.tile([P, PACK, N - CHUNK], F32, name="minus_us_y", tag="u_rows3")
+        for columns in (slice(0, CHUNK), slice(CHUNK, N - CHUNK)):
+            for t in range(PACK):
+                nc.scalar.activation(minus_us_y[:, t, columns], y_late[:, t, columns], COPY, scale=minus_us[:, t:t + 1])
+        us_g = {c: bank(3 + c, [P, 2, 2, P], "us_g%d" % c) for c in late}
 
         def add_turned(c, rows, first, final):
             for t in range(PACK):
@@ -175,130 +190,155 @@ def tile_attend_gmf_sq_vu_kernel(tc, uT, vT, y, us, ts, offs, uoffs, out_0, out_
                     us_g[c][:, t // 2, t % 2, :], rows[:, t, :], identity[:],
                     start=first and t == 0, stop=final and t == last, is_transpose=True)
 
-        turn_interleaved(w_turned, w_flat, 0, 6, "w_turn0")
         for c in late:
-            add_turned(c, minus_us_y[:, :, c * CHUNK - HALF:(c + 1) * CHUNK - HALF], True, False)
+            add_turned(c, minus_us_y[:, :, (c - 1) * CHUNK:c * CHUNK], True, False)
 
-        a = {c: sb.tile([P, CHUNK // 2, PACK, 2], F32, name="a%d" % c) for c in direct}
-        g = {c: sb.tile([P, CHUNK // 2, PACK, 2], F32, name="g%d" % c, tag="g%d" % c) for c in direct}
+        a = sb.tile([P, CHUNK // 2, PACK, 2], F32, name="a")
+        g = sb.tile([P, CHUNK // 2, PACK, 2], F32, name="g", tag="g", align_bytes=64)
         h = sb.tile([P, N, PACK], BF16, name="h", tag="h", align_bytes=64)
         h_flat = h[:].rearrange("p i t -> p (i t)")
-        h_r = mx_tiles("h_r", HALF + N)
-        nc.gpsimd.memset(h_r[0][:, 0:HALF], 0)
-        nc.gpsimd.memset(h_r[1][:, 0:HALF].bitcast(U32), 0)
-
-        def items(c):
-            return slice(c * CHUNK, (c + 1) * CHUNK)
+        h_first = mx_tiles("h_first")
+        nc.gpsimd.memset(h_first[0][:, CHUNK:N], 0)
+        nc.gpsimd.memset(h_first[1][:, CHUNK:N].bitcast(U32), 0)
+        h_late = mx_tiles("h_late")
+        zeros = sb.tile([P, CHUNK], F32, name="zeros")
+        nc.gpsimd.memset(zeros[:], 0.0)
 
         def by_pairs(rows):
             return rows.rearrange("p t (j e) -> p j t e", e=2)
 
-        def scale_a(c):
-            nc.vector.tensor_tensor(a[c][:], by_pairs(a_ps[c][:]), by_pairs(scale[:, :, items(c)]), MULT)
+        us_a = {c: sb.tile([P, PACK, CHUNK], F32, name="us_a%d" % c) for c in late}
 
-        def subtract_y(c):
-            nc.vector.tensor_tensor(g[c][:], a[c][:], by_pairs(y_sb[:, :, items(c)]), SUB)
-
-        def scale_g(c):
-            nc.vector.tensor_tensor(
-                h[:, items(c), :].rearrange("p (j e) t -> p j t e", e=2),
-                g[c][:], by_pairs(scale[:, :, items(c)]), MULT)
-
-        def quantise_h(c):
-            quantise(h_r, E5M2, h_flat, c * CHUNK, CHUNK, HALF)
-
-        windows = [[sb.tile([P, T], F32, name="window%d_%d" % (o, k)) for k in range(count)] for o, count in enumerate((4, 2))]
-        out_hbm = [out.rearrange("(p t) n -> p t n", t=PACK) for out in (out_0, out_1)]
-        du = [sb.tile([P, P, PACK], F32, name="du%d" % t, tag="du%d" % t) for t in range(PACK)]
-        dv_half = {}
-        dv_ps = {}
-
-        def half_product(t, k, number):
-            dv_ps[t, k] = bank(number, [P, N], "dv_ps%d_%d" % (t, k))
-            product(dv_ps[t, k][:], x_r, t * P, h_r, E5M2, k * HALF, N)
-
-        def half_copy(t, k, tag):
-            dv_half[t, k] = sb.tile([P, HALF], F32, name="dv%d_%d" % (t, k), tag=tag)
-            nc.scalar.copy(dv_half[t, k][:], dv_ps[t, k][:, HALF:N])
-
-        for step in (scale_a, subtract_y, scale_g, quantise_h):
-            for c in direct:
-                step(c)
-        half_product(0, 0, 0)
-        half_copy(0, 0, "dv0_0")
-        half_product(1, 0, 1)
-        half_copy(1, 0, "dv1_0")
-        h_by_item = {}
-        for c in late:
-            us_a = sb.tile([P, PACK, CHUNK], F32, name="us_a%d" % c, tag="g%d" % (c - 2))
-            for t in range(PACK):
+        def scale_late(c, planes):
+            for t in planes:
                 nc.vector.scalar_tensor_tensor(
-                    us_a[:, t, :], late_ps[t // 2][:, t % 2, items(c - 2)], us_col[:, t:t + 1], scale[:, t, items(c)],
-                    MULT, MULT)
-            add_turned(c, us_a[:], False, True)
+                    us_a[c][:, t, :], a_ps[c, t], us_col[:, t:t + 1], scale[:, t, items(c)], MULT, MULT)
+
+        h_by_item = {}
+
+        def finish_late(c):
+            add_turned(c, us_a[c][:], False, True)
             h_by_item[c] = sb.tile([P, 2, P, 2], BF16, name="h_by_item%d" % c, tag="h_by_item%d" % c)
             nc.scalar.activation(
                 h_by_item[c][:], us_g[c][:].rearrange("i u e q -> i u q e"), COPY, scale=ts_col[:, c:c + 1])
-        w_i = mx_tiles("w_i", tag="scale")
-        quantise(w_i, E4M3, w_turned[:], 0, D // 2)
-        for c, number in zip(late, (7, 2)):
-            ps = bank(number, [P, 2, P], "h_back%d" % c)
+
+        def turn_back(c):
+            ps = bank(7, [P, 2, P], "h_back%d" % c)
             words = h_by_item[c][:].rearrange("i u q e -> i (u q e)").bitcast(F32)
             for u in range(2):
                 nc.tensor.transpose(ps[:, u, :], words[:, u * P:(u + 1) * P], identity[:])
             nc.scalar.copy(
                 h_flat[:, c * CHUNK * PACK:(c + 1) * CHUNK * PACK].bitcast(F32).rearrange("q (i u) -> q i u", u=2),
                 ps[:].rearrange("q u i -> q i u"))
-            quantise_h(c)
-        half_product(2, 0, 6)
-        half_copy(2, 0, "h_by_item3")
-        for t, number in enumerate((4, 0, 5)):
-            half_product(t, 1, number)
-            half_copy(t, 1, "dv%d_1" % t)
+            quantise(h_late, E5M2, h_flat, c * CHUNK, CHUNK)
 
+        nc.vector.tensor_tensor(a[:], by_pairs(first_ps[:]), by_pairs(scale[:, :, items(0)]), MULT)
+        quantise(w_d, E4M3, w_flat, HALF, HALF)
+        for u in range(2):
+            ps = bank(2 + u, [P, 2, HALF], "late_ps%d" % u)
+            for e in range(2):
+                product(ps[:, e, :], x_d, (2 * u + e) * P, w_d, E4M3, HALF, HALF)
+                for c in (2, 3):
+                    a_ps[c, 2 * u + e] = ps[:, e, items(c - 2)]
+        nc.vector.tensor_tensor(g[:], a[:], by_pairs(y_first[:]), SUB)
+        scale_late(1, (0, 1))
+        nc.vector.tensor_tensor(
+            h[:, items(0), :].rearrange("p (j e) t -> p j t e", e=2), g[:], by_pairs(scale[:, :, items(0)]), MULT)
+        scale_late(1, (2, 3))
+        quantise(h_first, E5M2, h_flat, 0, CHUNK)
+
+        first_dv_ps = []
+
+        def first_product(t):
+            ps = bank(t, [P, N], "first_dv_ps%d" % t)
+            product(ps[:], x_r, t * P, h_first, E5M2, 0, N)
+            first_dv_ps.append(ps)
+
+        finish_late(1)
+        first_product(0)
+        dv_00 = sb.tile([P, CHUNK], F32, name="dv_00")
+        nc.scalar.copy(dv_00[:], first_dv_ps[0][:, 0:CHUNK])
+        first_product(1)
+        scale_late(2, range(PACK))
+        scale_late(3, range(PACK))
+        w_i = mx_tiles("w_i", tag="g")
+        quantise(w_i, E4M3, w_turned[:], 0, D // 2)
+        turn_back(1)
+        first_product(2)
+        first_product(3)
+        dv_0 = sb.tile([P, 2, CHUNK], F32, name="dv_0", tag="h_by_item1")
+        for t in range(1, last):
+            nc.scalar.copy(dv_0[:, t - 1, :], first_dv_ps[t][:, 0:CHUNK])
+        finish_late(2)
+
+        def late_product(c, tag):
+            ps = bank(3 + c, [P, D], "dv_by_item_ps%d" % c)
+            product(ps[:], h_late, c * CHUNK, x_r, E4M3, 0, D, E5M2)
+            rows = sb.tile([P, D], F32, name="dv_by_item%d" % c, tag=tag, align_bytes=64)
+            nc.scalar.copy(rows[:], ps[:])
+            turned = bank(c - 1, [P, PACK, CHUNK], "dv_turned_ps%d" % c)
+            for t in range(PACK):
+                nc.tensor.transpose(turned[:, t, :], rows[:, t * P:(t + 1) * P], identity[:])
+            return turned
+
+        turned = late_product(1, "v_rows2")
+        turn_back(2)
+        dv_03 = sb.tile([P, CHUNK], F32, name="dv_03", tag="h_by_item2")
+        nc.scalar.copy(dv_03[:], first_dv_ps[last][:, 0:CHUNK])
+        finish_late(3)
+        turn_back(3)
+        dv_1 = sb.tile([P, PACK, CHUNK], F32, name="dv_1", tag="h_by_item3")
+        nc.scalar.copy(dv_1[:, 0, :], turned[:, 0, :])
+        nc.scalar.copy(dv_1[:, 1:, :], turned[:, 1:, :])
+        dv_rest = sb.tile([P, 2, HALF], F32, name="dv_rest", tag="ts_row")
+        rest_ps = {}
+        for c, tag in ((2, "v_rows3"), (3, "v_rows2")):
+            rest_ps[c] = late_product(c, tag)
+            nc.scalar.copy(dv_rest[:, :, items(c - 2)], rest_ps[c][:, 0:2, :])
+
+        windows = [[sb.tile([P, T], F32, name="window%d_%d" % (o, k)) for k in range(count)] for o, count in enumerate((4, 3))]
+        out_hbm = [out.rearrange("(p t) n -> p t n", t=PACK) for out in (out_0, out_1)]
         zeroed_by_vector = 2
         for window in windows[0][:zeroed_by_vector]:
             nc.vector.memset(window[:], 0.0)
         for window in windows[0][zeroed_by_vector:] + windows[1]:
             nc.gpsimd.memset(window[:], 0.0)
 
-        last_ps = bank(1, [P, N], "dv_ps3")
-        product(last_ps[:], x_r, last * P, h_r, E5M2, HALF, N)
         h_i = mx_tiles("h_i")
         h_turned = sb.tile([P, PACK * R], BF16, name="h_turned", align_bytes=64)
-        for u, number in enumerate((4, 0)):
+        for u, number in enumerate((3, 7)):
             turn_interleaved(h_turned, h_flat, u, number, "h_turn%d" % u)
         quantise(h_i, E5M2, h_turned[:], 0, R)
-        dv_half[last, 0] = sb.tile([P, HALF], F32, name="dv3_0", tag="h", align_bytes=64)
-        nc.scalar.copy(dv_half[last, 0][:], last_ps[:, 0:HALF])
-        turn_interleaved(w_turned, w_flat, 1, 5, "w_turn1")
+        turn_interleaved(w_turned, w_flat, 1, 6, "w_turn1")
         quantise(w_i, E4M3, w_turned[:], D // 2, D // 2)
-        for t, number in enumerate((3, 7, 2, 6)):
+        dv_last = sb.tile([P, 2, HALF], F32, name="dv_last", tag="h", align_bytes=64)
+        for c in (2, 3):
+            nc.scalar.copy(dv_last[:, :, items(c - 2)], rest_ps[c][:, 2:PACK, :])
+        du = [sb.tile([P, P, PACK], F32, name="du%d" % t, tag="u_rows%d" % t) for t in range(PACK)]
+        for t, number in enumerate((0, 4, 5, 3)):
             ps = bank(number, [P, PACK, P], "du_ps%d" % t)
             product(ps[:].rearrange("p s q -> p (s q)"), w_i, t * P, h_i, E5M2, 0, R)
             nc.scalar.copy(du[t][:], ps[:].rearrange("p s q -> p q s"))
 
-        def scatter(o, t, offsets, values):
-            nc.vector.tensor_copy(windows[o][t % len(windows[o])][:].indirect(offsets), values)
+        def window(o, t):
+            return windows[o][t % len(windows[o])]
+
+        def scatter_chunk(t, c, values):
+            nc.vector.tensor_tensor(window(0, t)[:].indirect(list_part(item_list, c * CHUNK, CHUNK)), values, zeros[:], ADD)
 
         def store(o, t):
-            nc.sync.dma_start(out_hbm[o][:, t, :], windows[o][t % len(windows[o])][:])
+            nc.sync.dma_start(out_hbm[o][:, t, :], window(o, t)[:])
 
-        def user_block(t):
-            scatter(1, t, user_list[:], du[t][:].rearrange("p q s -> p (q s)"))
-            store(1, t)
-
-        for t in range(last):
-            scatter(0, t, list_half(item_list, 0), dv_half[t, 0][:])
-        for t in range(last):
-            scatter(0, t, list_half(item_list, 1), dv_half[t, 1][:])
+        scatter_chunk(0, 0, dv_00[:])
+        for t in range(1, last):
+            scatter_chunk(t, 0, dv_0[:, t - 1, :])
+        scatter_chunk(last, 0, dv_03[:])
+        for t in range(PACK):
+            scatter_chunk(t, 1, dv_1[:, t, :])
+        for t in range(PACK):
+            values = (dv_rest, dv_last)[t // 2][:, t % 2, :]
+            nc.vector.tensor_copy(window(0, t)[:].indirect(list_part(item_list, HALF, HALF)), values)
             store(0, t)
-        scatter(0, last, list_half(item_list, 0), dv_half[last, 0][:])
-        user_block(0)
-        user_block(1)
-        dv_half[last, 1] = sb.tile([P, HALF], F32, name="dv3_1", tag="du0")
-        nc.scalar.copy(dv_half[last, 1][:], last_ps[:, HALF:N])
-        scatter(0, last, list_half(item_list, 1), dv_half[last, 1][:])
-        store(0, last)
-        user_block(2)
-        user_block(3)
+        for t in range(PACK):
+            nc.vector.tensor_copy(window(1, t)[:].indirect(user_list[:]), du[t][:].rearrange("p q s -> p (q s)"))
+            store(1, t)

@@ -63,18 +63,20 @@ def tile_attend_gmf_sq_vu_kernel(tc, uT, vT, y, us, ts, offs, uoffs, out_0, out_
         def list_part(index_list, first, count):
             return index_list[:, first // PER_COLUMN:(first + count) // PER_COLUMN]
 
+        def list_half(index_list, k):
+            return list_part(index_list, k * HALF, HALF)
+
         item_list = lists.tile([P, N // PER_COLUMN], U16, name="item_list")
         user_list = lists.tile([P, R // PER_COLUMN], U16, name="user_list")
         u_rows = [sb.tile([P, T], F32, name="u_rows%d" % t, tag="u_rows%d" % t) for t in range(PACK)]
         v_rows = [sb.tile([P, T], F32, name="v_rows%d" % t, tag="v_rows%d" % t, align_bytes=64) for t in range(PACK)]
-        ts_row = sb.tile([P, T], F32, name="ts_row", tag="ts_row")
+        ts_row = sb.tile([P, T], F32, name="ts_row", tag="ts_row", align_bytes=64)
         us_col = sb.tile([P, PACK], F32, name="us_col")
-        y_first = sb.tile([P, PACK, CHUNK], F32, name="y_first")
-        y_late = sb.tile([P, PACK, N - CHUNK], F32, name="y_late")
+        y_sb = sb.tile([P, PACK, N], F32, name="y_sb")
         u_hbm = uT.rearrange("(p t) n -> p t n", t=PACK)
         v_hbm = vT.rearrange("(p t) n -> p t n", t=PACK)
 
-        ts_runs = sb.tile([P, T // P], F32, name="ts_runs", tag="x", align_bytes=64)
+        ts_runs = sb.tile([P, T // P], F32, name="ts_runs")
         nc.sync.dma_start(ts_runs[:], ts[0:1, :].rearrange("o (p k) -> p (o k)", p=P))
         nc.sync.dma_start(u_rows[0][:], u_hbm[:, 0, :])
         nc.sync.dma_start(user_list[:], uoffs)
@@ -84,9 +86,7 @@ def tile_attend_gmf_sq_vu_kernel(tc, uT, vT, y, us, ts, offs, uoffs, out_0, out_
             nc.sync.dma_start(u_rows[t][:], u_hbm[:, t, :])
         for t in range(PACK):
             nc.sync.dma_start(v_rows[t][:], v_hbm[:, t, :])
-        y_hbm = y.rearrange("b (p t) i -> p (b t) i", t=PACK)
-        nc.sync.dma_start(y_first[:], y_hbm[:, :, 0:CHUNK])
-        nc.sync.dma_start(y_late[:], y_hbm[:, :, CHUNK:N])
+        nc.sync.dma_start(y_sb[:], y.rearrange("b (p t) i -> p (b t) i", t=PACK))
 
         identity = sb.tile([P, P], F32, name="identity")
         make_identity(nc, identity[:])
@@ -99,7 +99,9 @@ def tile_attend_gmf_sq_vu_kernel(tc, uT, vT, y, us, ts, offs, uoffs, out_0, out_
                 ts_row[:].rearrange("m (n b k) -> m b n k", b=T // P // PACK, k=PACK)[:, b], ps[:].rearrange("m k n -> m n k"))
 
         def turn_interleaved(turned, values, u, number, name):
-            words = values.bitcast(F32).rearrange("p (q s u) -> p s u q", s=PACK, u=2)
+            turn_words(turned, values.bitcast(F32).rearrange("p (q s u) -> p s u q", s=PACK, u=2), u, number, name)
+
+        def turn_words(turned, words, u, number, name):
             ps = bank(number, [P, PACK * P], name)
             for s in range(PACK):
                 nc.tensor.transpose(ps[:, s * P:(s + 1) * P], words[:, s, u, :], identity[:])
@@ -107,7 +109,15 @@ def tile_attend_gmf_sq_vu_kernel(tc, uT, vT, y, us, ts, offs, uoffs, out_0, out_
                 turned[:, u * 1024:(u + 1) * 1024].rearrange("q (e p s) -> q e p s", e=2, s=PACK),
                 ps[:].bitcast(BF16).rearrange("q (s p e) -> q e p s", s=PACK, e=2))
 
-        x = sb.tile([P, PACK, P, PACK], BF16, name="x", tag="x", align_bytes=64)
+        x_turned = sb.tile([P, PACK * D], BF16, name="x_turned", tag="x_turned", align_bytes=64)
+        x_gathered = sb.tile([P, 2 * R], F32, name="x_gathered")
+        for t in range(2):
+            nc.vector.tensor_copy(x_gathered[:, t * R:(t + 1) * R], u_rows[t][:].indirect(user_list[:]))
+            ps = bank(4 + t, [P, PACK, P], "x_turn%d" % t)
+            for s in range(PACK):
+                nc.tensor.transpose(ps[:, s, :], x_gathered[:, t * R + s:(t + 1) * R:PACK], identity[:])
+            nc.scalar.copy(
+                x_turned[:, t * D:(t + 1) * D].rearrange("q (p s) -> q p s", s=PACK), ps[:].rearrange("q s p -> q p s"))
         ts_gathered = sb.tile([P, N], F32, name="ts_gathered")
         nc.vector.tensor_copy(ts_gathered[:], ts_row[:].indirect(item_list[:]))
 
@@ -116,73 +126,64 @@ def tile_attend_gmf_sq_vu_kernel(tc, uT, vT, y, us, ts, offs, uoffs, out_0, out_
             nc.tensor.transpose(ts_ps[:, c, :], ts_gathered[:, c * P:(c + 1) * P], identity[:])
         ts_col = sb.tile([P, N // P], F32, name="ts_col")
         nc.scalar.copy(ts_col[:], ts_ps[:, :, 0])
-        late = (1, 2, 3)
-        scale = sb.tile([P, PACK, N], F32, name="scale")
+        direct, late = (0, 1), (2, 3)
+        x = sb.tile([P, PACK, P, PACK], BF16, name="x", tag="ts_row", align_bytes=64)
+        nc.scalar.copy(
+            x[:, :, :, 0:2].rearrange("p s q e -> p q e s"), x_gathered[:].rearrange("p (e q s) -> p q e s", e=2, s=PACK))
+        for t in range(2, PACK):
+            nc.vector.tensor_copy(x[:, :, :, t].rearrange("p s q -> p q s"), u_rows[t][:].indirect(user_list[:]))
+        x_flat = x[:].rearrange("p s q t -> p (s q t)")
+        x_d = mx_tiles("x_d")
+        quantise(x_d, E4M3, x_flat, 0, R)
+        turn_words(x_turned, x_flat.bitcast(F32).rearrange("p (s q u) -> p s u q", s=PACK, u=2), 1, 4, "x_turn_words")
+        scale = sb.tile([P, PACK, N], F32, name="scale", tag="scale", align_bytes=64)
         for t in range(PACK):
             nc.scalar.activation(scale[:, t, :], ts_gathered[:], COPY, scale=us_col[:, t:t + 1])
-        x_turned = sb.tile([P, PACK * D], BF16, name="x_turned", tag="x_turned", align_bytes=64)
-        x_gathered = [sb.tile([P, 2 * R], F32, name="x_gathered%d" % u, tag=tag) for u, tag in enumerate(("x_gathered", "ts_row"))]
-        for t in range(PACK):
-            u, e = divmod(t, 2)
-            nc.vector.tensor_copy(x_gathered[u][:, e * R:(e + 1) * R], u_rows[t][:].indirect(user_list[:]))
-            if e == 1:
-                nc.scalar.copy(
-                    x[:, :, :, 2 * u:2 * u + 2].rearrange("p s q e -> p q e s"),
-                    x_gathered[u][:].rearrange("p (e q s) -> p q e s", e=2, s=PACK))
-            ps = bank(4 + e, [P, PACK, P], "x_turn%d" % t)
-            for s in range(PACK):
-                nc.tensor.transpose(ps[:, s, :], x_gathered[u][:, e * R + s:(e + 1) * R:PACK], identity[:])
-            nc.scalar.copy(
-                x_turned[:, t * D:(t + 1) * D].rearrange("q (p s) -> q p s", s=PACK), ps[:].rearrange("q s p -> q p s"))
-        x_flat = x[:].rearrange("p s q t -> p (s q t)")
+        w_turned_first = sb.tile([P, D], BF16, name="w_turned_first", tag="w", align_bytes=64)
         w_turned = sb.tile([P, PACK * D], BF16, name="w_turned", align_bytes=64)
-        w_d = mx_tiles("w_d")
+        w_d = mx_tiles("w_d", HALF)
         last = PACK - 1
         w_gathered = sb.tile([P, 2 * N], F32, name="w_gathered", tag="u_rows3")
 
-        def turn_w_plane(t):
-            ps = bank(6 + t, [P, PACK, P], "w_turn_plane%d" % t)
+        def turn_w_plane(t, number, turned):
+            ps = bank(number, [P, PACK, P], "w_turn_plane%d" % t)
             for s in range(PACK):
                 nc.tensor.transpose(ps[:, s, :], w_gathered[:, t * N + s:(t + 1) * N:PACK], identity[:])
-            nc.scalar.copy(
-                w_turned[:, t * D:(t + 1) * D].rearrange("q (p s) -> q p s", s=PACK), ps[:].rearrange("q s p -> q p s"))
+            nc.scalar.copy(turned.rearrange("q (p s) -> q p s", s=PACK), ps[:].rearrange("q s p -> q p s"))
 
         nc.vector.tensor_copy(w_gathered[:, 0:N], v_rows[0][:].indirect(item_list[:]))
-        turn_w_plane(0)
-        x_d = mx_tiles("x_d", tag="v_rows0")
-        quantise(x_d, E4M3, x_flat, 0, R)
-        x_r = mx_tiles("x_r", tag="x")
+        turn_w_plane(0, 6, w_turned_first[:])
+        x_r = mx_tiles("x_r")
         quantise(x_r, E4M3, x_turned[:], 0, D)
-        w = sb.tile([P, N, PACK], BF16, name="w", tag="x_turned", align_bytes=64)
+        w_i = mx_tiles("w_i", tag="x_turned")
+        quantise(w_i, E4M3, w_turned_first[:], 0, P)
+        w = sb.tile([P, N, PACK], BF16, name="w", tag="w", align_bytes=64)
         w_flat = w[:].rearrange("p i t -> p (i t)")
         nc.vector.tensor_copy(w_gathered[:, N:2 * N], v_rows[1][:].indirect(item_list[:]))
         nc.scalar.copy(
             w[:, :, 0:2].rearrange("p (j f) e -> p j e f", f=4), w_gathered[:].rearrange("p (e j f) -> p j e f", e=2, f=4))
-        turn_w_plane(1)
-        nc.vector.tensor_copy(w[:, :, 2], v_rows[2][:].indirect(item_list[:]))
-
-        def items(c):
-            return slice(c * CHUNK, (c + 1) * CHUNK)
+        nc.vector.tensor_copy(w[:, 0:HALF, 2], v_rows[2][:].indirect(list_half(item_list, 0)))
+        w_late = sb.tile([P, 2 * HALF], F32, name="w_late", tag="v_rows1", align_bytes=64)
+        nc.vector.tensor_copy(w_late[:, 0:HALF], v_rows[2][:].indirect(list_half(item_list, 1)))
+        turn_w_plane(1, 7, w_turned[:, D:2 * D])
 
         a_ps = {}
-        nc.vector.tensor_copy(w[:, 0:HALF, last], v_rows[last][:].indirect(list_part(item_list, 0, HALF)))
-        for c in range(2):
+        nc.vector.tensor_copy(w[:, 0:HALF, last], v_rows[last][:].indirect(list_half(item_list, 0)))
+        for c in direct:
             quantise(w_d, E4M3, w_flat, c * CHUNK, CHUNK)
-            ps = bank(c, [P, PACK, CHUNK], "a_ps%d" % c)
+            a_ps[c] = bank(c, [P, PACK, CHUNK], "a_ps%d" % c)
             for t in range(PACK):
-                product(ps[:, t, :], x_d, t * P, w_d, E4M3, c * CHUNK, CHUNK)
-                a_ps[c, t] = ps[:, t, :]
-            if c == 0:
-                first_ps = ps
-        nc.vector.tensor_copy(w[:, HALF:N, last], v_rows[last][:].indirect(list_part(item_list, HALF, HALF)))
+                product(a_ps[c][:, t, :], x_d, t * P, w_d, E4M3, c * CHUNK, CHUNK)
+        nc.vector.tensor_copy(w_late[:, HALF:N], v_rows[last][:].indirect(list_half(item_list, 1)))
+        nc.scalar.copy(
+            w[:, HALF:N, 2:4].rearrange("p (j f) e -> p j e f", f=4), w_late[:].rearrange("p (e j f) -> p j e f", e=2, f=4))
 
         minus_us = sb.tile([P, PACK], F32, name="minus_us", tag="v_rows3", align_bytes=64)
         nc.scalar.activation(minus_us[:], us_col[:], COPY, scale=-1.0)
-        minus_us_y = sb.tile([P, PACK, N - CHUNK], F32, name="minus_us_y", tag="u_rows3")
-        for columns in (slice(0, CHUNK), slice(CHUNK, N - CHUNK)):
-            for t in range(PACK):
-                nc.scalar.activation(minus_us_y[:, t, columns], y_late[:, t, columns], COPY, scale=minus_us[:, t:t + 1])
-        us_g = {c: bank(3 + c, [P, 2, 2, P], "us_g%d" % c) for c in late}
+        minus_us_y = sb.tile([P, PACK, HALF], F32, name="minus_us_y")
+        for t in range(PACK):
+            nc.scalar.activation(minus_us_y[:, t, :], y_sb[:, t, HALF:N], COPY, scale=minus_us[:, t:t + 1])
+        us_g = {c: bank(2 + c, [P, 2, 2, P], "us_g%d" % c) for c in late}
 
         def add_turned(c, rows, first, final):
             for t in range(PACK):
@@ -191,154 +192,137 @@ def tile_attend_gmf_sq_vu_kernel(tc, uT, vT, y, us, ts, offs, uoffs, out_0, out_
                     start=first and t == 0, stop=final and t == last, is_transpose=True)
 
         for c in late:
-            add_turned(c, minus_us_y[:, :, (c - 1) * CHUNK:c * CHUNK], True, False)
+            add_turned(c, minus_us_y[:, :, c * CHUNK - HALF:(c + 1) * CHUNK - HALF], True, False)
 
-        a = sb.tile([P, CHUNK // 2, PACK, 2], F32, name="a")
-        g = sb.tile([P, CHUNK // 2, PACK, 2], F32, name="g", tag="g", align_bytes=64)
+        a = {c: sb.tile([P, CHUNK // 2, PACK, 2], F32, name="a%d" % c, tag="a%d" % c, align_bytes=64) for c in direct}
+        g = {c: sb.tile([P, CHUNK // 2, PACK, 2], F32, name="g%d" % c, tag="g%d" % c) for c in direct}
         h = sb.tile([P, N, PACK], BF16, name="h", tag="h", align_bytes=64)
         h_flat = h[:].rearrange("p i t -> p (i t)")
-        h_first = mx_tiles("h_first")
-        nc.gpsimd.memset(h_first[0][:, CHUNK:N], 0)
-        nc.gpsimd.memset(h_first[1][:, CHUNK:N].bitcast(U32), 0)
-        h_late = mx_tiles("h_late")
-        zeros = sb.tile([P, CHUNK], F32, name="zeros")
-        nc.gpsimd.memset(zeros[:], 0.0)
+        h_r = mx_tiles("h_r", HALF + N)
+        nc.gpsimd.memset(h_r[0][:, 0:HALF], 0)
+        nc.gpsimd.memset(h_r[1][:, 0:HALF].bitcast(U32), 0)
+
+        def items(c):
+            return slice(c * CHUNK, (c + 1) * CHUNK)
 
         def by_pairs(rows):
             return rows.rearrange("p t (j e) -> p j t e", e=2)
 
-        us_a = {c: sb.tile([P, PACK, CHUNK], F32, name="us_a%d" % c) for c in late}
+        def scale_a(c):
+            nc.vector.tensor_tensor(a[c][:], by_pairs(a_ps[c][:]), by_pairs(scale[:, :, items(c)]), MULT)
 
-        def scale_late(c, planes):
-            for t in planes:
-                nc.vector.scalar_tensor_tensor(
-                    us_a[c][:, t, :], a_ps[c, t], us_col[:, t:t + 1], scale[:, t, items(c)], MULT, MULT)
+        def subtract_y(c):
+            nc.vector.tensor_tensor(g[c][:], a[c][:], by_pairs(y_sb[:, :, items(c)]), SUB)
 
+        def scale_g(c):
+            nc.vector.tensor_tensor(
+                h[:, items(c), :].rearrange("p (j e) t -> p j t e", e=2),
+                g[c][:], by_pairs(scale[:, :, items(c)]), MULT)
+
+        def quantise_h(c):
+            quantise(h_r, E5M2, h_flat, c * CHUNK, CHUNK, HALF)
+
+        windows = [[sb.tile([P, T], F32, name="window%d_%d" % (o, k)) for k in range(count)] for o, count in enumerate((4, 2))]
+        out_hbm = [out.rearrange("(p t) n -> p t n", t=PACK) for out in (out_0, out_1)]
+        du = [sb.tile([P, P, PACK], F32, name="du%d" % t, tag="du%d" % t) for t in range(PACK)]
+        dv_half = {}
+        dv_ps = {}
+
+        def half_product(t, k, number):
+            dv_ps[t, k] = bank(number, [P, N], "dv_ps%d_%d" % (t, k))
+            product(dv_ps[t, k][:], x_r, t * P, h_r, E5M2, k * HALF, N)
+
+        def half_copy(t, k, tag):
+            dv_half[t, k] = sb.tile([P, HALF], F32, name="dv%d_%d" % (t, k), tag=tag)
+            nc.scalar.copy(dv_half[t, k][:], dv_ps[t, k][:, HALF:N])
+
+        for step in (scale_a, subtract_y):
+            for c in direct:
+                step(c)
+        w_d_late = mx_tiles("w_d_late", HALF, tag="a0")
+        quantise(w_d_late, E4M3, w_flat, HALF, HALF, -HALF)
+        late_ps = [bank(2 + u, [P, 2, HALF], "late_ps%d" % u) for u in range(2)]
+        for t in range(PACK):
+            product(late_ps[t // 2][:, t % 2, :], x_d, t * P, w_d_late, E4M3, 0, HALF)
+        for step in (scale_g, quantise_h):
+            for c in direct:
+                step(c)
+        half_product(0, 0, 0)
+        half_copy(0, 0, "dv0_0")
+        half_product(1, 0, 1)
+        half_copy(1, 0, "dv1_0")
         h_by_item = {}
-
-        def finish_late(c):
-            add_turned(c, us_a[c][:], False, True)
+        for c in late:
+            us_a = sb.tile([P, PACK, CHUNK], F32, name="us_a%d" % c, tag="g%d" % (c - 2))
+            for t in range(PACK):
+                nc.vector.scalar_tensor_tensor(
+                    us_a[:, t, :], late_ps[t // 2][:, t % 2, items(c - 2)], us_col[:, t:t + 1], scale[:, t, items(c)],
+                    MULT, MULT)
+            add_turned(c, us_a[:], False, True)
             h_by_item[c] = sb.tile([P, 2, P, 2], BF16, name="h_by_item%d" % c, tag="h_by_item%d" % c)
             nc.scalar.activation(
                 h_by_item[c][:], us_g[c][:].rearrange("i u e q -> i u q e"), COPY, scale=ts_col[:, c:c + 1])
-
-        def turn_back(c):
-            ps = bank(7, [P, 2, P], "h_back%d" % c)
+        w_i_second = mx_tiles("w_i_second", P, tag="scale")
+        quantise(w_i_second, E4M3, w_turned[:], P, P, -P)
+        for c, number in zip(late, (7, 2)):
+            ps = bank(number, [P, 2, P], "h_back%d" % c)
             words = h_by_item[c][:].rearrange("i u q e -> i (u q e)").bitcast(F32)
             for u in range(2):
                 nc.tensor.transpose(ps[:, u, :], words[:, u * P:(u + 1) * P], identity[:])
             nc.scalar.copy(
                 h_flat[:, c * CHUNK * PACK:(c + 1) * CHUNK * PACK].bitcast(F32).rearrange("q (i u) -> q i u", u=2),
                 ps[:].rearrange("q u i -> q i u"))
-            quantise(h_late, E5M2, h_flat, c * CHUNK, CHUNK)
+            quantise_h(c)
+        half_product(2, 0, 6)
+        half_copy(2, 0, "h_by_item3")
+        for t, number in enumerate((4, 0, 5)):
+            half_product(t, 1, number)
+            half_copy(t, 1, "dv%d_1" % t)
 
-        nc.vector.tensor_tensor(a[:], by_pairs(first_ps[:]), by_pairs(scale[:, :, items(0)]), MULT)
-        quantise(w_d, E4M3, w_flat, HALF, HALF)
-        for u in range(2):
-            ps = bank(2 + u, [P, 2, HALF], "late_ps%d" % u)
-            for e in range(2):
-                product(ps[:, e, :], x_d, (2 * u + e) * P, w_d, E4M3, HALF, HALF)
-                for c in (2, 3):
-                    a_ps[c, 2 * u + e] = ps[:, e, items(c - 2)]
-        nc.vector.tensor_tensor(g[:], a[:], by_pairs(y_first[:]), SUB)
-        scale_late(1, (0, 1))
-        nc.vector.tensor_tensor(
-            h[:, items(0), :].rearrange("p (j e) t -> p j t e", e=2), g[:], by_pairs(scale[:, :, items(0)]), MULT)
-        scale_late(1, (2, 3))
-        quantise(h_first, E5M2, h_flat, 0, CHUNK)
-
-        first_dv_ps = []
-
-        def first_product(t):
-            ps = bank(t, [P, N], "first_dv_ps%d" % t)
-            product(ps[:], x_r, t * P, h_first, E5M2, 0, N)
-            first_dv_ps.append(ps)
-
-        finish_late(1)
-        first_product(0)
-        dv_00 = sb.tile([P, CHUNK], F32, name="dv_00")
-        nc.scalar.copy(dv_00[:], first_dv_ps[0][:, 0:CHUNK])
-        first_product(1)
-        scale_late(2, range(PACK))
-        scale_late(3, range(PACK))
-        w_i = mx_tiles("w_i", tag="g")
-        quantise(w_i, E4M3, w_turned[:], 0, D // 2)
-        turn_back(1)
-        first_product(2)
-        first_product(3)
-        dv_0 = sb.tile([P, 2, CHUNK], F32, name="dv_0", tag="h_by_item1")
-        for t in range(1, last):
-            nc.scalar.copy(dv_0[:, t - 1, :], first_dv_ps[t][:, 0:CHUNK])
-        finish_late(2)
-
-        def late_product(c, tag):
-            ps = bank(3 + c, [P, D], "dv_by_item_ps%d" % c)
-            product(ps[:], h_late, c * CHUNK, x_r, E4M3, 0, D, E5M2)
-            rows = sb.tile([P, D], F32, name="dv_by_item%d" % c, tag=tag, align_bytes=64)
-            nc.scalar.copy(rows[:], ps[:])
-            turned = bank(c - 1, [P, PACK, CHUNK], "dv_turned_ps%d" % c)
-            for t in range(PACK):
-                nc.tensor.transpose(turned[:, t, :], rows[:, t * P:(t + 1) * P], identity[:])
-            return turned
-
-        turned = late_product(1, "v_rows2")
-        turn_back(2)
-        dv_03 = sb.tile([P, CHUNK], F32, name="dv_03", tag="h_by_item2")
-        nc.scalar.copy(dv_03[:], first_dv_ps[last][:, 0:CHUNK])
-        finish_late(3)
-        turn_back(3)
-        dv_1 = sb.tile([P, PACK, CHUNK], F32, name="dv_1", tag="h_by_item3")
-        nc.scalar.copy(dv_1[:, 0, :], turned[:, 0, :])
-        nc.scalar.copy(dv_1[:, 1:, :], turned[:, 1:, :])
-        dv_rest = sb.tile([P, 2, HALF], F32, name="dv_rest", tag="ts_row")
-        rest_ps = {}
-        for c, tag in ((2, "v_rows3"), (3, "v_rows2")):
-            rest_ps[c] = late_product(c, tag)
-            nc.scalar.copy(dv_rest[:, :, items(c - 2)], rest_ps[c][:, 0:2, :])
-
-        windows = [[sb.tile([P, T], F32, name="window%d_%d" % (o, k)) for k in range(count)] for o, count in enumerate((4, 3))]
-        out_hbm = [out.rearrange("(p t) n -> p t n", t=PACK) for out in (out_0, out_1)]
         zeroed_by_vector = 2
         for window in windows[0][:zeroed_by_vector]:
             nc.vector.memset(window[:], 0.0)
         for window in windows[0][zeroed_by_vector:] + windows[1]:
             nc.gpsimd.memset(window[:], 0.0)
 
+        last_ps = bank(1, [P, N], "dv_ps3")
+        product(last_ps[:], x_r, last * P, h_r, E5M2, HALF, N)
         h_i = mx_tiles("h_i")
         h_turned = sb.tile([P, PACK * R], BF16, name="h_turned", align_bytes=64)
-        for u, number in enumerate((3, 7)):
+        for u, number in enumerate((4, 0)):
             turn_interleaved(h_turned, h_flat, u, number, "h_turn%d" % u)
         quantise(h_i, E5M2, h_turned[:], 0, R)
-        turn_interleaved(w_turned, w_flat, 1, 6, "w_turn1")
+        dv_half[last, 0] = sb.tile([P, HALF], F32, name="dv3_0", tag="h", align_bytes=64)
+        nc.scalar.copy(dv_half[last, 0][:], last_ps[:, 0:HALF])
+        turn_interleaved(w_turned, w_flat, 1, 5, "w_turn1")
         quantise(w_i, E4M3, w_turned[:], D // 2, D // 2)
-        dv_last = sb.tile([P, 2, HALF], F32, name="dv_last", tag="h", align_bytes=64)
-        for c in (2, 3):
-            nc.scalar.copy(dv_last[:, :, items(c - 2)], rest_ps[c][:, 2:PACK, :])
-        du = [sb.tile([P, P, PACK], F32, name="du%d" % t, tag="u_rows%d" % t) for t in range(PACK)]
-        for t, number in enumerate((0, 4, 5, 3)):
+        for t, number in enumerate((3, 7, 2, 6)):
             ps = bank(number, [P, PACK, P], "du_ps%d" % t)
-            product(ps[:].rearrange("p s q -> p (s q)"), w_i, t * P, h_i, E5M2, 0, R)
+            operand, first = (w_i_second, 0) if t == 1 else (w_i, t * P)
+            product(ps[:].rearrange("p s q -> p (s q)"), operand, first, h_i, E5M2, 0, R)
             nc.scalar.copy(du[t][:], ps[:].rearrange("p s q -> p q s"))
 
-        def window(o, t):
-            return windows[o][t % len(windows[o])]
-
-        def scatter_chunk(t, c, values):
-            nc.vector.tensor_tensor(window(0, t)[:].indirect(list_part(item_list, c * CHUNK, CHUNK)), values, zeros[:], ADD)
+        def scatter(o, t, offsets, values):
+            nc.vector.tensor_copy(windows[o][t % len(windows[o])][:].indirect(offsets), values)
 
         def store(o, t):
-            nc.sync.dma_start(out_hbm[o][:, t, :], window(o, t)[:])
+            nc.sync.dma_start(out_hbm[o][:, t, :], windows[o][t % len(windows[o])][:])
 
-        scatter_chunk(0, 0, dv_00[:])
-        for t in range(1, last):
-            scatter_chunk(t, 0, dv_0[:, t - 1, :])
-        scatter_chunk(last, 0, dv_03[:])
-        for t in range(PACK):
-            scatter_chunk(t, 1, dv_1[:, t, :])
-        for t in range(PACK):
-            values = (dv_rest, dv_last)[t // 2][:, t % 2, :]
-            nc.vector.tensor_copy(window(0, t)[:].indirect(list_part(item_list, HALF, HALF)), values)
-            store(0, t)
-        for t in range(PACK):
-            nc.vector.tensor_copy(window(1, t)[:].indirect(user_list[:]), du[t][:].rearrange("p q s -> p (q s)"))
+        def user_block(t):
+            scatter(1, t, user_list[:], du[t][:].rearrange("p q s -> p (q s)"))
             store(1, t)
+
+        for t in range(last):
+            scatter(0, t, list_half(item_list, 0), dv_half[t, 0][:])
+        for t in range(last):
+            scatter(0, t, list_half(item_list, 1), dv_half[t, 1][:])
+            store(0, t)
+        scatter(0, last, list_half(item_list, 0), dv_half[last, 0][:])
+        user_block(0)
+        user_block(1)
+        dv_half[last, 1] = sb.tile([P, HALF], F32, name="dv3_1", tag="du0")
+        nc.scalar.copy(dv_half[last, 1][:], last_ps[:, HALF:N])
+        scatter(0, last, list_half(item_list, 1), dv_half[last, 1][:])
+        store(0, last)
+        user_block(2)
+        user_block(3)

@@ -194,8 +194,8 @@ def tile_attend_gmf_sq_vu_kernel(tc, uT, vT, y, us, ts, offs, uoffs, out_0, out_
         for c in late:
             add_turned(c, minus_us_y[:, :, c * CHUNK - HALF:(c + 1) * CHUNK - HALF], True, False)
 
-        a = {c: sb.tile([P, CHUNK // 2, PACK, 2], F32, name="a%d" % c, tag="a%d" % c, align_bytes=64) for c in direct}
-        g = {c: sb.tile([P, CHUNK // 2, PACK, 2], F32, name="g%d" % c, tag="g%d" % c) for c in direct}
+        a = {c: sb.tile([P, PACK, CHUNK], F32, name="a%d" % c, tag="a%d" % c, align_bytes=64) for c in direct}
+        g = {c: sb.tile([P, PACK, CHUNK], F32, name="g%d" % c, tag="g%d" % c) for c in direct}
         h = sb.tile([P, N, PACK], BF16, name="h", tag="h", align_bytes=64)
         h_flat = h[:].rearrange("p i t -> p (i t)")
         h_r = mx_tiles("h_r", HALF + N)
@@ -209,15 +209,15 @@ def tile_attend_gmf_sq_vu_kernel(tc, uT, vT, y, us, ts, offs, uoffs, out_0, out_
             return rows.rearrange("p t (j e) -> p j t e", e=2)
 
         def scale_a(c):
-            nc.vector.tensor_tensor(a[c][:], by_pairs(a_ps[c][:]), by_pairs(scale[:, :, items(c)]), MULT)
+            nc.vector.tensor_tensor(a[c][:], a_ps[c][:], scale[:, :, items(c)], MULT)
 
         def subtract_y(c):
-            nc.vector.tensor_tensor(g[c][:], a[c][:], by_pairs(y_sb[:, :, items(c)]), SUB)
+            nc.vector.tensor_tensor(g[c][:], a[c][:], y_sb[:, :, items(c)], SUB)
 
         def scale_g(c):
             nc.vector.tensor_tensor(
                 h[:, items(c), :].rearrange("p (j e) t -> p j t e", e=2),
-                g[c][:], by_pairs(scale[:, :, items(c)]), MULT)
+                by_pairs(g[c][:]), by_pairs(scale[:, :, items(c)]), MULT)
 
         def quantise_h(c):
             quantise(h_r, E5M2, h_flat, c * CHUNK, CHUNK, HALF)

@@ -105,9 +105,10 @@ def tile_attend_gmf_sq_vu_kernel(tc, uT, vT, y, us, ts, offs, uoffs, out_0, out_
             ps = bank(number, [P, PACK * P], name)
             for s in range(PACK):
                 nc.tensor.transpose(ps[:, s * P:(s + 1) * P], words[:, s, u, :], identity[:])
-            nc.scalar.copy(
-                turned[:, u * 1024:(u + 1) * 1024].rearrange("q (e p s) -> q e p s", e=2, s=PACK),
-                ps[:].bitcast(BF16).rearrange("q (s p e) -> q e p s", s=PACK, e=2))
+            planes = ps[:].bitcast(BF16).rearrange("q (s p e) -> q e p s", s=PACK, e=2)
+            for e in range(2):
+                plane = 2 * u + e
+                nc.scalar.copy(turned[:, plane * D:(plane + 1) * D].rearrange("q (p s) -> q p s", s=PACK), planes[:, e])
 
         x_turned = sb.tile([P, PACK * D], BF16, name="x_turned", tag="x_turned", align_bytes=64)
         x_gathered = sb.tile([P, 2 * R], F32, name="x_gathered")
@@ -275,9 +276,14 @@ def tile_attend_gmf_sq_vu_kernel(tc, uT, vT, y, us, ts, offs, uoffs, out_0, out_
             quantise_h(c)
         half_product(2, 0, 6)
         half_copy(2, 0, "h_by_item3")
-        for t, number in enumerate((4, 0, 5)):
+        for t, number in enumerate((4, 0)):
             half_product(t, 1, number)
             half_copy(t, 1, "dv%d_1" % t)
+        h_turned = sb.tile([P, PACK * R], BF16, name="h_turned", align_bytes=64)
+        turn_interleaved(h_turned, h_flat, 0, 3, "h_turn0")
+        half_product(2, 1, 3)
+        half_copy(2, 1, "dv2_1")
+        turn_interleaved(h_turned, h_flat, 1, 4, "h_turn1")
 
         zeroed_by_vector = 2
         for window in windows[0][:zeroed_by_vector]:
@@ -285,18 +291,16 @@ def tile_attend_gmf_sq_vu_kernel(tc, uT, vT, y, us, ts, offs, uoffs, out_0, out_
         for window in windows[0][zeroed_by_vector:] + windows[1]:
             nc.gpsimd.memset(window[:], 0.0)
 
-        last_ps = bank(1, [P, N], "dv_ps3")
+        last_ps = bank(0, [P, N], "dv_ps3")
         product(last_ps[:], x_r, last * P, h_r, E5M2, HALF, N)
         h_i = mx_tiles("h_i")
-        h_turned = sb.tile([P, PACK * R], BF16, name="h_turned", align_bytes=64)
-        for u, number in enumerate((4, 0)):
-            turn_interleaved(h_turned, h_flat, u, number, "h_turn%d" % u)
         quantise(h_i, E5M2, h_turned[:], 0, R)
         dv_half[last, 0] = sb.tile([P, HALF], F32, name="dv3_0", tag="h", align_bytes=64)
         nc.scalar.copy(dv_half[last, 0][:], last_ps[:, 0:HALF])
-        turn_interleaved(w_turned, w_flat, 1, 5, "w_turn1")
-        quantise(w_i, E4M3, w_turned[:], D // 2, D // 2)
-        for t, number in enumerate((3, 7, 2, 6)):
+        for t, number in enumerate((5, 4, 7, 2)):
+            if t == 1:
+                turn_interleaved(w_turned, w_flat, 1, 4, "w_turn1")
+                quantise(w_i, E4M3, w_turned[:], D // 2, D // 2)
             ps = bank(number, [P, PACK, P], "du_ps%d" % t)
             operand, first = (w_i_second, 0) if t == 1 else (w_i, t * P)
             product(ps[:].rearrange("p s q -> p (s q)"), operand, first, h_i, E5M2, 0, R)
@@ -320,7 +324,7 @@ def tile_attend_gmf_sq_vu_kernel(tc, uT, vT, y, us, ts, offs, uoffs, out_0, out_
         scatter(0, last, list_half(item_list, 0), dv_half[last, 0][:])
         user_block(0)
         user_block(1)
-        dv_half[last, 1] = sb.tile([P, HALF], F32, name="dv3_1", tag="du0")
+        dv_half[last, 1] = sb.tile([P, HALF], F32, name="dv3_1", tag="scale", align_bytes=64)
         nc.scalar.copy(dv_half[last, 1][:], last_ps[:, HALF:N])
         scatter(0, last, list_half(item_list, 1), dv_half[last, 1][:])
         store(0, last)

@@ -122,12 +122,12 @@ def tile_attend_gmf_sq_vu_kernel(tc, uT, vT, y, us, ts, offs, uoffs, out_0, out_
         ts_gathered = sb.tile([P, N], F32, name="ts_gathered")
         nc.vector.tensor_copy(ts_gathered[:], ts_row[:].indirect(item_list[:]))
 
-        ts_ps = bank(0, [P, PACK, P], "ts_ps")
-        for c in range(N // P):
-            nc.tensor.transpose(ts_ps[:, c, :], ts_gathered[:, c * P:(c + 1) * P], identity[:])
-        ts_col = sb.tile([P, N // P], F32, name="ts_col")
-        nc.scalar.copy(ts_col[:], ts_ps[:, :, 0])
         direct, late = (0, 1), (2, 3)
+        ts_ps = bank(0, [P, len(late), P], "ts_ps")
+        for k, c in enumerate(late):
+            nc.tensor.transpose(ts_ps[:, k, :], ts_gathered[:, c * P:(c + 1) * P], identity[:])
+        ts_col = sb.tile([P, len(late)], F32, name="ts_col")
+        nc.scalar.copy(ts_col[:], ts_ps[:, :, 0])
         x = sb.tile([P, PACK, P, PACK], BF16, name="x", tag="ts_row", align_bytes=64)
         nc.scalar.copy(
             x[:, :, :, 0:2].rearrange("p s q e -> p q e s"), x_gathered[:].rearrange("p (e q s) -> p q e s", e=2, s=PACK))
@@ -172,9 +172,10 @@ def tile_attend_gmf_sq_vu_kernel(tc, uT, vT, y, us, ts, offs, uoffs, out_0, out_
         nc.vector.tensor_copy(w[:, 0:HALF, last], v_rows[last][:].indirect(list_half(item_list, 0)))
         for c in direct:
             quantise(w_d, E4M3, w_flat, c * CHUNK, CHUNK)
-            a_ps[c] = bank(c, [P, PACK, CHUNK], "a_ps%d" % c)
-            for t in range(PACK):
-                product(a_ps[c][:, t, :], x_d, t * P, w_d, E4M3, c * CHUNK, CHUNK)
+            for u in range(2):
+                a_ps[c, u] = bank(2 * c + u, [P, 2, CHUNK], "a_ps%d_%d" % (c, u))
+                for e in range(2):
+                    product(a_ps[c, u][:, e, :], x_d, (2 * u + e) * P, w_d, E4M3, c * CHUNK, CHUNK)
         nc.vector.tensor_copy(w_late[:, HALF:N], v_rows[last][:].indirect(list_half(item_list, 1)))
         nc.scalar.copy(
             w[:, HALF:N, 2:4].rearrange("p (j f) e -> p j e f", f=4), w_late[:].rearrange("p (e j f) -> p j e f", e=2, f=4))
@@ -210,7 +211,9 @@ def tile_attend_gmf_sq_vu_kernel(tc, uT, vT, y, us, ts, offs, uoffs, out_0, out_
             return rows.rearrange("p t (j e) -> p j t e", e=2)
 
         def scale_a(c):
-            nc.vector.tensor_tensor(a[c][:], a_ps[c][:], scale[:, :, items(c)], MULT)
+            for u in range(2):
+                rows = slice(2 * u, 2 * u + 2)
+                nc.vector.tensor_tensor(a[c][:, rows, :], a_ps[c, u][:], scale[:, rows, items(c)], MULT)
 
         def subtract_y(c):
             nc.vector.tensor_tensor(g[c][:], a[c][:], y_sb[:, :, items(c)], SUB)
@@ -262,7 +265,7 @@ def tile_attend_gmf_sq_vu_kernel(tc, uT, vT, y, us, ts, offs, uoffs, out_0, out_
             add_turned(c, us_a[:], False, True)
             h_by_item[c] = sb.tile([P, 2, P, 2], BF16, name="h_by_item%d" % c, tag="h_by_item%d" % c)
             nc.scalar.activation(
-                h_by_item[c][:], us_g[c][:].rearrange("i u e q -> i u q e"), COPY, scale=ts_col[:, c:c + 1])
+                h_by_item[c][:], us_g[c][:].rearrange("i u e q -> i u q e"), COPY, scale=ts_col[:, c - 2:c - 1])
         w_i_second = mx_tiles("w_i_second", P, tag="scale")
         quantise(w_i_second, E4M3, w_turned[:], P, P, -P)
         for c, number in zip(late, (7, 2)):

@@ -9,7 +9,6 @@ PACK = 4
 CHUNK = 128
 HALF = N // 2
 PER_COLUMN = 16
-WINDOWS = 3
 FLOPS = 3 * 2 * D * R * N
 BYTES = 4 * (4 * D * T + R * N + R + T) + 2 * P * (R + N) // PER_COLUMN
 
@@ -22,7 +21,6 @@ E4M3 = mybir.dt.float8_e4m3fn_x4
 E5M2 = mybir.dt.float8_e5m2_x4
 MULT = mybir.AluOpType.mult
 SUB = mybir.AluOpType.subtract
-ADD = mybir.AluOpType.add
 COPY = mybir.ActivationFunctionType.Copy
 
 
@@ -49,10 +47,10 @@ def tile_attend_gmf_sq_vu_kernel(tc, uT, vT, y, us, ts, offs, uoffs, out_0, out_
                 in_=values[:, PACK * first:PACK * (first + count)],
             )
 
-        def product(out, lhs, lhs_first, rhs, rhs_fmt, rhs_first, rhs_count, lhs_fmt=E4M3):
+        def product(out, lhs, lhs_first, rhs, rhs_fmt, rhs_first, rhs_count):
             nc.tensor.matmul_mx(
                 out=out,
-                lhsT=lhs[0][:, lhs_first:lhs_first + P].bitcast(lhs_fmt),
+                lhsT=lhs[0][:, lhs_first:lhs_first + P].bitcast(E4M3),
                 lhsT_scale=lhs[1][:, lhs_first:lhs_first + P],
                 rhs=rhs[0][:, rhs_first:rhs_first + rhs_count].bitcast(rhs_fmt),
                 rhs_scale=rhs[1][:, rhs_first:rhs_first + rhs_count],
@@ -60,11 +58,8 @@ def tile_attend_gmf_sq_vu_kernel(tc, uT, vT, y, us, ts, offs, uoffs, out_0, out_
                 stop=True,
             )
 
-        def list_part(index_list, first, count):
-            return index_list[:, first // PER_COLUMN:(first + count) // PER_COLUMN]
-
         def list_half(index_list, k):
-            return list_part(index_list, k * HALF, HALF)
+            return index_list[:, k * HALF // PER_COLUMN:(k + 1) * HALF // PER_COLUMN]
 
         item_list = lists.tile([P, N // PER_COLUMN], U16, name="item_list")
         user_list = lists.tile([P, R // PER_COLUMN], U16, name="user_list")
@@ -122,12 +117,6 @@ def tile_attend_gmf_sq_vu_kernel(tc, uT, vT, y, us, ts, offs, uoffs, out_0, out_
         ts_gathered = sb.tile([P, N], F32, name="ts_gathered")
         nc.vector.tensor_copy(ts_gathered[:], ts_row[:].indirect(item_list[:]))
 
-        direct, late = (0, 1), (2, 3)
-        ts_ps = bank(0, [P, len(late), P], "ts_ps")
-        for k, c in enumerate(late):
-            nc.tensor.transpose(ts_ps[:, k, :], ts_gathered[:, c * P:(c + 1) * P], identity[:])
-        ts_col = sb.tile([P, len(late)], F32, name="ts_col")
-        nc.scalar.copy(ts_col[:], ts_ps[:, :, 0])
         x = sb.tile([P, PACK, P, PACK], BF16, name="x", tag="ts_row", align_bytes=64)
         nc.scalar.copy(
             x[:, :, :, 0:2].rearrange("p s q e -> p q e s"), x_gathered[:].rearrange("p (e q s) -> p q e s", e=2, s=PACK))
@@ -156,8 +145,8 @@ def tile_attend_gmf_sq_vu_kernel(tc, uT, vT, y, us, ts, offs, uoffs, out_0, out_
         turn_w_plane(0, 6, w_turned_first[:])
         x_r = mx_tiles("x_r")
         quantise(x_r, E4M3, x_turned[:], 0, D)
-        w_i = mx_tiles("w_i", tag="x_turned")
-        quantise(w_i, E4M3, w_turned_first[:], 0, P)
+        w_i_first = mx_tiles("w_i_first", P, tag="x_turned")
+        quantise(w_i_first, E4M3, w_turned_first[:], 0, P)
         w = sb.tile([P, N, PACK], BF16, name="w", tag="w", align_bytes=64)
         w_flat = w[:].rearrange("p i t -> p (i t)")
         nc.vector.tensor_copy(w_gathered[:, N:2 * N], v_rows[1][:].indirect(item_list[:]))
@@ -169,40 +158,22 @@ def tile_attend_gmf_sq_vu_kernel(tc, uT, vT, y, us, ts, offs, uoffs, out_0, out_
         turn_w_plane(1, 7, w_turned[:, D:2 * D])
 
         a_ps = {}
+        early, late = (0, 1), (2, 3)
         nc.vector.tensor_copy(w[:, 0:HALF, last], v_rows[last][:].indirect(list_half(item_list, 0)))
-        for c in direct:
+        nc.scalar.activation(w_late[:, HALF:N], v_rows[last][:].indirect(list_half(item_list, 1)), COPY)
+        nc.scalar.copy(
+            w[:, HALF:N, 2:4].rearrange("p (j f) e -> p j e f", f=4), w_late[:].rearrange("p (e j f) -> p j e f", e=2, f=4))
+        for c in early:
             quantise(w_d, E4M3, w_flat, c * CHUNK, CHUNK)
             for u in range(2):
                 a_ps[c, u] = bank(2 * c + u, [P, 2, CHUNK], "a_ps%d_%d" % (c, u))
                 for e in range(2):
                     product(a_ps[c, u][:, e, :], x_d, (2 * u + e) * P, w_d, E4M3, c * CHUNK, CHUNK)
-        nc.vector.tensor_copy(w_late[:, HALF:N], v_rows[last][:].indirect(list_half(item_list, 1)))
-        nc.scalar.copy(
-            w[:, HALF:N, 2:4].rearrange("p (j f) e -> p j e f", f=4), w_late[:].rearrange("p (e j f) -> p j e f", e=2, f=4))
 
-        minus_us = sb.tile([P, PACK], F32, name="minus_us", tag="v_rows3", align_bytes=64)
-        nc.scalar.activation(minus_us[:], us_col[:], COPY, scale=-1.0)
-        minus_us_y = sb.tile([P, PACK, HALF], F32, name="minus_us_y")
-        for t in range(PACK):
-            nc.scalar.activation(minus_us_y[:, t, :], y_sb[:, t, HALF:N], COPY, scale=minus_us[:, t:t + 1])
-        us_g = {c: bank(2 + c, [P, 2, 2, P], "us_g%d" % c) for c in late}
-
-        def add_turned(c, rows, first, final):
-            for t in range(PACK):
-                nc.tensor.matmul(
-                    us_g[c][:, t // 2, t % 2, :], rows[:, t, :], identity[:],
-                    start=first and t == 0, stop=final and t == last, is_transpose=True)
-
-        for c in late:
-            add_turned(c, minus_us_y[:, :, c * CHUNK - HALF:(c + 1) * CHUNK - HALF], True, False)
-
-        a = {c: sb.tile([P, PACK, CHUNK], F32, name="a%d" % c, tag="a%d" % c, align_bytes=64) for c in direct}
-        g = {c: sb.tile([P, PACK, CHUNK], F32, name="g%d" % c, tag="g%d" % c) for c in direct}
+        a, g = {}, {}
         h = sb.tile([P, N, PACK], BF16, name="h", tag="h", align_bytes=64)
         h_flat = h[:].rearrange("p i t -> p (i t)")
-        h_r = mx_tiles("h_r", HALF + N)
-        nc.gpsimd.memset(h_r[0][:, 0:HALF], 0)
-        nc.gpsimd.memset(h_r[1][:, 0:HALF].bitcast(U32), 0)
+        h_r = mx_tiles("h_r")
 
         def items(c):
             return slice(c * CHUNK, (c + 1) * CHUNK)
@@ -210,12 +181,11 @@ def tile_attend_gmf_sq_vu_kernel(tc, uT, vT, y, us, ts, offs, uoffs, out_0, out_
         def by_pairs(rows):
             return rows.rearrange("p t (j e) -> p j t e", e=2)
 
-        def scale_a(c):
-            for u in range(2):
-                rows = slice(2 * u, 2 * u + 2)
-                nc.vector.tensor_tensor(a[c][:, rows, :], a_ps[c, u][:], scale[:, rows, items(c)], MULT)
+        def work_tile(name, slot):
+            return sb.tile([P, PACK, CHUNK], F32, name=name, tag="work%d" % slot, align_bytes=64)
 
         def subtract_y(c):
+            g[c] = work_tile("g%d" % c, (c + 2) % 4)
             nc.vector.tensor_tensor(g[c][:], a[c][:], y_sb[:, :, items(c)], SUB)
 
         def scale_g(c):
@@ -224,112 +194,123 @@ def tile_attend_gmf_sq_vu_kernel(tc, uT, vT, y, us, ts, offs, uoffs, out_0, out_
                 by_pairs(g[c][:]), by_pairs(scale[:, :, items(c)]), MULT)
 
         def quantise_h(c):
-            quantise(h_r, E5M2, h_flat, c * CHUNK, CHUNK, HALF)
+            quantise(h_r, E5M2, h_flat, c * CHUNK, CHUNK)
 
-        windows = [[sb.tile([P, T], F32, name="window%d_%d" % (o, k)) for k in range(count)] for o, count in enumerate((4, 2))]
-        out_hbm = [out.rearrange("(p t) n -> p t n", t=PACK) for out in (out_0, out_1)]
-        du = [sb.tile([P, P, PACK], F32, name="du%d" % t, tag="du%d" % t) for t in range(PACK)]
-        dv_half = {}
-        dv_ps = {}
-
-        def half_product(t, k, number):
-            dv_ps[t, k] = bank(number, [P, N], "dv_ps%d_%d" % (t, k))
-            product(dv_ps[t, k][:], x_r, t * P, h_r, E5M2, k * HALF, N)
-
-        def half_copy(t, k, tag):
-            dv_half[t, k] = sb.tile([P, HALF], F32, name="dv%d_%d" % (t, k), tag=tag)
-            nc.scalar.copy(dv_half[t, k][:], dv_ps[t, k][:, HALF:N])
-
-        for step in (scale_a, subtract_y):
-            for c in direct:
-                step(c)
-        w_d_late = mx_tiles("w_d_late", HALF, tag="a0")
-        quantise(w_d_late, E4M3, w_flat, HALF, HALF, -HALF)
-        late_ps = [bank(2 + u, [P, 2, HALF], "late_ps%d" % u) for u in range(2)]
-        for t in range(PACK):
-            product(late_ps[t // 2][:, t % 2, :], x_d, t * P, w_d_late, E4M3, 0, HALF)
-        for step in (scale_g, quantise_h):
-            for c in direct:
-                step(c)
-        half_product(0, 0, 0)
-        half_copy(0, 0, "dv0_0")
-        half_product(1, 0, 1)
-        half_copy(1, 0, "dv1_0")
-        h_by_item = {}
-        for c in late:
-            us_a = sb.tile([P, PACK, CHUNK], F32, name="us_a%d" % c, tag="g%d" % (c - 2))
-            for t in range(PACK):
-                nc.vector.scalar_tensor_tensor(
-                    us_a[:, t, :], late_ps[t // 2][:, t % 2, items(c - 2)], us_col[:, t:t + 1], scale[:, t, items(c)],
-                    MULT, MULT)
-            add_turned(c, us_a[:], False, True)
-            h_by_item[c] = sb.tile([P, 2, P, 2], BF16, name="h_by_item%d" % c, tag="h_by_item%d" % c)
-            nc.scalar.activation(
-                h_by_item[c][:], us_g[c][:].rearrange("i u e q -> i u q e"), COPY, scale=ts_col[:, c - 2:c - 1])
-        w_i_second = mx_tiles("w_i_second", P, tag="scale")
-        quantise(w_i_second, E4M3, w_turned[:], P, P, -P)
-        for c, number in zip(late, (7, 2)):
-            ps = bank(number, [P, 2, P], "h_back%d" % c)
-            words = h_by_item[c][:].rearrange("i u q e -> i (u q e)").bitcast(F32)
+        for c in early:
+            a[c] = work_tile("a%d" % c, c)
             for u in range(2):
-                nc.tensor.transpose(ps[:, u, :], words[:, u * P:(u + 1) * P], identity[:])
-            nc.scalar.copy(
-                h_flat[:, c * CHUNK * PACK:(c + 1) * CHUNK * PACK].bitcast(F32).rearrange("q (i u) -> q i u", u=2),
-                ps[:].rearrange("q u i -> q i u"))
-            quantise_h(c)
-        half_product(2, 0, 6)
-        half_copy(2, 0, "h_by_item3")
-        for t, number in enumerate((4, 0)):
-            half_product(t, 1, number)
-            half_copy(t, 1, "dv%d_1" % t)
-        h_turned = sb.tile([P, PACK * R], BF16, name="h_turned", align_bytes=64)
-        turn_interleaved(h_turned, h_flat, 0, 3, "h_turn0")
-        half_product(2, 1, 3)
-        half_copy(2, 1, "dv2_1")
-        turn_interleaved(h_turned, h_flat, 1, 4, "h_turn1")
+                rows = slice(2 * u, 2 * u + 2)
+                nc.vector.tensor_tensor(a[c][:, rows, :], a_ps[c, u][:], scale[:, rows, items(c)], MULT)
+        turn_interleaved(w_turned, w_flat, 1, 0, "w_turn1")
+        for c in early:
+            subtract_y(c)
+        w_d_late = mx_tiles("w_d_late", HALF, tag="work0")
+        quantise(w_d_late, E4M3, w_flat, HALF, HALF, -HALF)
+        for c in late:
+            a_ps[c] = bank(2 + c, [P, PACK, CHUNK], "a_ps%d" % c)
+            for t in range(PACK):
+                product(a_ps[c][:, t, :], x_d, t * P, w_d_late, E4M3, c * CHUNK - HALF, CHUNK)
+        for step in (scale_g, quantise_h):
+            for c in early:
+                step(c)
 
-        zeroed_by_vector = 2
+        windows = [[sb.tile([P, T], F32, name="window%d_%d" % (o, t)) for t in range(PACK)] for o in range(2)]
+        out_hbm = [out.rearrange("(p t) n -> p t n", t=PACK) for out in (out_0, out_1)]
+        zeroed_by_vector = 3
         for window in windows[0][:zeroed_by_vector]:
             nc.vector.memset(window[:], 0.0)
         for window in windows[0][zeroed_by_vector:] + windows[1]:
             nc.gpsimd.memset(window[:], 0.0)
 
-        last_ps = bank(0, [P, N], "dv_ps3")
-        product(last_ps[:], x_r, last * P, h_r, E5M2, HALF, N)
-        h_i = mx_tiles("h_i")
-        quantise(h_i, E5M2, h_turned[:], 0, R)
-        dv_half[last, 0] = sb.tile([P, HALF], F32, name="dv3_0", tag="h", align_bytes=64)
-        nc.scalar.copy(dv_half[last, 0][:], last_ps[:, 0:HALF])
-        for t, number in enumerate((5, 4, 7, 2)):
-            if t == 1:
-                turn_interleaved(w_turned, w_flat, 1, 4, "w_turn1")
-                quantise(w_i, E4M3, w_turned[:], D // 2, D // 2)
-            ps = bank(number, [P, PACK, P], "du_ps%d" % t)
-            operand, first = (w_i_second, 0) if t == 1 else (w_i, t * P)
-            product(ps[:].rearrange("p s q -> p (s q)"), operand, first, h_i, E5M2, 0, R)
-            nc.scalar.copy(du[t][:], ps[:].rearrange("p s q -> p q s"))
+        def dv_bank(number, parts):
+            ps = bank(number, [P, len(parts), HALF], "dv_ps%d_%d" % parts[0])
+            return ps
 
-        def scatter(o, t, offsets, values):
-            nc.vector.tensor_copy(windows[o][t % len(windows[o])][:].indirect(offsets), values)
+        def dv_product(ps, slot, t, k):
+            product(ps[:, slot, :], x_r, t * P, h_r, E5M2, k * HALF, HALF)
+
+        def scatter(engine, o, t, offsets, values):
+            if engine == "vector":
+                nc.vector.tensor_copy(windows[o][t][:].indirect(offsets), values)
+            else:
+                nc.scalar.activation(windows[o][t][:].indirect(offsets), values, COPY)
 
         def store(o, t):
-            nc.sync.dma_start(out_hbm[o][:, t, :], windows[o][t % len(windows[o])][:])
+            nc.sync.dma_start(out_hbm[o][:, t, :], windows[o][t][:])
 
-        def user_block(t):
-            scatter(1, t, user_list[:], du[t][:].rearrange("p q s -> p (q s)"))
+        def copy_out(engine, out, ps):
+            if engine == "vector":
+                nc.vector.tensor_copy(out, ps)
+            else:
+                nc.scalar.copy(out, ps)
+
+        dv = {}
+
+        def dv_copy(engine, ps, parts, tag=None):
+            name = "dv%d_%d" % parts[0]
+            values = sb.tile([P, len(parts), HALF], F32, name=name, tag=tag or name)
+            copy_out(engine, values[:], ps[:])
+            for slot, part in enumerate(parts):
+                dv[part] = values[:, slot, :]
+
+        def dv_scatter(engine, t, k):
+            scatter(engine, 0, t, list_half(item_list, k), dv[t, k])
+            if k == 1:
+                store(0, t)
+
+        for t in range(2):
+            ps = dv_bank(6 + t, [(t, 0)])
+            dv_product(ps, 0, t, 0)
+            dv_copy("scalar", ps, [(t, 0)])
+            dv_scatter("scalar", t, 0)
+        pair_b, pair_d = [(2, 0), (1, 1)], [(2, 1), (3, 0)]
+        ps_b = dv_bank(1, pair_b)
+        dv_product(ps_b, 0, 2, 0)
+        ps_d = dv_bank(3, pair_d)
+        dv_product(ps_d, 1, 3, 0)
+
+        for c in late:
+            a[c] = work_tile("a%d" % c, c)
+            nc.vector.tensor_tensor(a[c][:], a_ps[c][:], scale[:, :, items(c)], MULT)
+        for step in (subtract_y, scale_g, quantise_h):
+            for c in late:
+                step(c)
+
+        ps_c = dv_bank(2, [(0, 1)])
+        dv_product(ps_c, 0, 0, 1)
+        dv_product(ps_b, 1, 1, 1)
+        dv_product(ps_d, 0, 2, 1)
+        ps_e = dv_bank(0, [(3, 1)])
+        dv_product(ps_e, 0, 3, 1)
+        dv_copy("vector", ps_c, [(0, 1)])
+        dv_scatter("vector", 0, 1)
+        dv_copy("scalar", ps_b, pair_b, "dv_pair")
+        dv_scatter("scalar", 2, 0)
+        dv_scatter("vector", 1, 1)
+        h_turned = sb.tile([P, PACK * R], BF16, name="h_turned", tag="h_turned", align_bytes=64)
+        turn_interleaved(h_turned, h_flat, 0, 2, "h_turn0")
+        turn_interleaved(h_turned, h_flat, 1, 1, "h_turn1")
+        dv_copy("vector", ps_d, pair_d, "dv_pair")
+        dv_scatter("vector", 2, 1)
+        dv_scatter("scalar", 3, 0)
+        dv_copy("scalar", ps_e, [(3, 1)])
+        dv_scatter("scalar", 3, 1)
+
+        h_i = mx_tiles("h_i")
+        quantise(h_i, E5M2, h_turned[:], 0, R)
+        w_i_rest = mx_tiles("w_i_rest", tag="h_turned")
+        quantise(w_i_rest, E4M3, w_turned[:], P, P)
+        quantise(w_i_rest, E4M3, w_turned[:], D // 2, D // 2)
+        for t in range(PACK):
+            engine = ("vector", "scalar")[t % 2]
+            ps = bank(4 + t, [P, PACK, P], "du_ps%d" % t)
+            product(ps[:].rearrange("p s q -> p (s q)"), w_i_rest if t else w_i_first, t * P, h_i, E5M2, 0, R)
+            du = sb.tile([P, P, PACK], F32, name="du%d" % t, tag="du%d" % (t % 2))
+            copy_out(engine, du[:], ps[:].rearrange("p s q -> p q s"))
+            values = du[:].rearrange("p q s -> p (q s)")
+            if engine == "vector":
+                scatter(engine, 1, t, user_list[:], values)
+            else:
+                for k in range(2):
+                    scatter(engine, 1, t, list_half(user_list, k), values[:, k * HALF:(k + 1) * HALF])
             store(1, t)
-
-        for t in range(last):
-            scatter(0, t, list_half(item_list, 0), dv_half[t, 0][:])
-        for t in range(last):
-            scatter(0, t, list_half(item_list, 1), dv_half[t, 1][:])
-            store(0, t)
-        scatter(0, last, list_half(item_list, 0), dv_half[last, 0][:])
-        user_block(0)
-        user_block(1)
-        dv_half[last, 1] = sb.tile([P, HALF], F32, name="dv3_1", tag="scale", align_bytes=64)
-        nc.scalar.copy(dv_half[last, 1][:], last_ps[:, HALF:N])
-        scatter(0, last, list_half(item_list, 1), dv_half[last, 1][:])
-        store(0, last)
-        user_block(2)
-        user_block(3)

@@ -96,14 +96,14 @@ def tile_attend_gmf_sq_vu_kernel(tc, uT, vT, y, us, ts, offs, uoffs, out_0, out_
         def turn_interleaved(turned, values, u, number, name):
             turn_words(turned, values.bitcast(F32).rearrange("p (q s u) -> p s u q", s=PACK, u=2), u, number, name)
 
-        def turn_words(turned, words, u, number, name):
+        def turn_words(turned, words, u, number, name, parts=1):
             ps = bank(number, [P, PACK * P], name)
             for s in range(PACK):
                 nc.tensor.transpose(ps[:, s * P:(s + 1) * P], words[:, s, u, :], identity[:])
-            planes = ps[:].bitcast(BF16).rearrange("q (s p e) -> q e p s", s=PACK, e=2)
+            planes = ps[:].bitcast(BF16).rearrange("q (s k p e) -> q e k p s", s=PACK, k=parts, e=2)
+            places = turned[:].rearrange("q (k t p s) -> q t k p s", k=parts, t=PACK, s=PACK)
             for e in range(2):
-                plane = 2 * u + e
-                nc.scalar.copy(turned[:, plane * D:(plane + 1) * D].rearrange("q (p s) -> q p s", s=PACK), planes[:, e])
+                nc.scalar.copy(places[:, 2 * u + e], planes[:, e])
 
         x_turned = sb.tile([P, PACK * D], BF16, name="x_turned", tag="x_turned", align_bytes=64)
         x_gathered = sb.tile([P, 2 * R], F32, name="x_gathered")
@@ -145,17 +145,17 @@ def tile_attend_gmf_sq_vu_kernel(tc, uT, vT, y, us, ts, offs, uoffs, out_0, out_
         turn_w_plane(0, 6, w_turned_first[:])
         x_r = mx_tiles("x_r")
         quantise(x_r, E4M3, x_turned[:], 0, D)
-        w_i_first = mx_tiles("w_i_first", P, tag="x_turned")
+        nc.vector.tensor_copy(w_gathered[:, N:2 * N], v_rows[1][:].indirect(item_list[:]))
+        turn_w_plane(1, 7, w_turned[:, D:2 * D])
+        w_i_first = mx_tiles("w_i_first", P, tag="v_rows1")
         quantise(w_i_first, E4M3, w_turned_first[:], 0, P)
         w = sb.tile([P, N, PACK], BF16, name="w", tag="w", align_bytes=64)
         w_flat = w[:].rearrange("p i t -> p (i t)")
-        nc.vector.tensor_copy(w_gathered[:, N:2 * N], v_rows[1][:].indirect(item_list[:]))
-        nc.scalar.copy(
+        nc.vector.tensor_copy(
             w[:, :, 0:2].rearrange("p (j f) e -> p j e f", f=4), w_gathered[:].rearrange("p (e j f) -> p j e f", e=2, f=4))
         nc.vector.tensor_copy(w[:, 0:HALF, 2], v_rows[2][:].indirect(list_half(item_list, 0)))
-        w_late = sb.tile([P, 2 * HALF], F32, name="w_late", tag="v_rows1", align_bytes=64)
-        nc.vector.tensor_copy(w_late[:, 0:HALF], v_rows[2][:].indirect(list_half(item_list, 1)))
-        turn_w_plane(1, 7, w_turned[:, D:2 * D])
+        w_late = sb.tile([P, 2 * HALF], F32, name="w_late", tag="u_rows3")
+        nc.scalar.activation(w_late[:, 0:HALF], v_rows[2][:].indirect(list_half(item_list, 1)), COPY)
 
         a_ps = {}
         early, late = (0, 1), (2, 3)
@@ -169,17 +169,19 @@ def tile_attend_gmf_sq_vu_kernel(tc, uT, vT, y, us, ts, offs, uoffs, out_0, out_
                 a_ps[c, u] = bank(2 * c + u, [P, 2, CHUNK], "a_ps%d_%d" % (c, u))
                 for e in range(2):
                     product(a_ps[c, u][:, e, :], x_d, (2 * u + e) * P, w_d, E4M3, c * CHUNK, CHUNK)
+        w_d_late = mx_tiles("w_d_late", HALF)
+        quantise(w_d_late, E4M3, w_flat, HALF, HALF, -HALF)
 
         a, g = {}, {}
-        h = sb.tile([P, N, PACK], BF16, name="h", tag="h", align_bytes=64)
-        h_flat = h[:].rearrange("p i t -> p (i t)")
+        h = sb.tile([P, PACK, P, PACK], BF16, name="h", tag="h", align_bytes=64)
+        h_flat = h[:].rearrange("p s q t -> p (s q t)")
         h_r = mx_tiles("h_r")
 
         def items(c):
             return slice(c * CHUNK, (c + 1) * CHUNK)
 
-        def by_pairs(rows):
-            return rows.rearrange("p t (j e) -> p j t e", e=2)
+        def by_fours(rows):
+            return rows.rearrange("p t (q s) -> p q t s", s=PACK)
 
         def work_tile(name, slot):
             return sb.tile([P, PACK, CHUNK], F32, name=name, tag="work%d" % slot, align_bytes=64)
@@ -190,11 +192,14 @@ def tile_attend_gmf_sq_vu_kernel(tc, uT, vT, y, us, ts, offs, uoffs, out_0, out_
 
         def scale_g(c):
             nc.vector.tensor_tensor(
-                h[:, items(c), :].rearrange("p (j e) t -> p j t e", e=2),
-                by_pairs(g[c][:]), by_pairs(scale[:, :, items(c)]), MULT)
+                h[:, :, c * CHUNK // PACK:(c + 1) * CHUNK // PACK, :].rearrange("p s q t -> p q t s"),
+                by_fours(g[c][:]), by_fours(scale[:, :, items(c)]), MULT)
 
-        def quantise_h(c):
-            quantise(h_r, E5M2, h_flat, c * CHUNK, CHUNK)
+        def quantise_h(k):
+            run = HALF // PACK
+            for s in range(PACK):
+                first = s * P + k * run
+                quantise(h_r, E5M2, h_flat, first, run, k * HALF + s * run - first)
 
         for c in early:
             a[c] = work_tile("a%d" % c, c)
@@ -204,19 +209,17 @@ def tile_attend_gmf_sq_vu_kernel(tc, uT, vT, y, us, ts, offs, uoffs, out_0, out_
         turn_interleaved(w_turned, w_flat, 1, 0, "w_turn1")
         for c in early:
             subtract_y(c)
-        w_d_late = mx_tiles("w_d_late", HALF, tag="work0")
-        quantise(w_d_late, E4M3, w_flat, HALF, HALF, -HALF)
         for c in late:
             a_ps[c] = bank(2 + c, [P, PACK, CHUNK], "a_ps%d" % c)
             for t in range(PACK):
                 product(a_ps[c][:, t, :], x_d, t * P, w_d_late, E4M3, c * CHUNK - HALF, CHUNK)
-        for step in (scale_g, quantise_h):
-            for c in early:
-                step(c)
+        for c in early:
+            scale_g(c)
+        quantise_h(0)
 
         windows = [[sb.tile([P, T], F32, name="window%d_%d" % (o, t)) for t in range(PACK)] for o in range(2)]
         out_hbm = [out.rearrange("(p t) n -> p t n", t=PACK) for out in (out_0, out_1)]
-        zeroed_by_vector = 3
+        zeroed_by_vector = 2
         for window in windows[0][:zeroed_by_vector]:
             nc.vector.memset(window[:], 0.0)
         for window in windows[0][zeroed_by_vector:] + windows[1]:
@@ -248,8 +251,9 @@ def tile_attend_gmf_sq_vu_kernel(tc, uT, vT, y, us, ts, offs, uoffs, out_0, out_
 
         def dv_copy(engine, ps, parts, tag=None):
             name = "dv%d_%d" % parts[0]
-            values = sb.tile([P, len(parts), HALF], F32, name=name, tag=tag or name)
-            copy_out(engine, values[:], ps[:])
+            values = sb.tile([P, len(parts), HALF], F32, name=name, tag=tag or name, align_bytes=64)
+            copy_out(
+                engine, values[:].rearrange("p n (q s) -> p n q s", s=PACK), ps[:].rearrange("p n (s q) -> p n q s", s=PACK))
             for slot, part in enumerate(parts):
                 dv[part] = values[:, slot, :]
 
@@ -262,55 +266,57 @@ def tile_attend_gmf_sq_vu_kernel(tc, uT, vT, y, us, ts, offs, uoffs, out_0, out_
             ps = dv_bank(6 + t, [(t, 0)])
             dv_product(ps, 0, t, 0)
             dv_copy("scalar", ps, [(t, 0)])
+        for t in range(2):
             dv_scatter("scalar", t, 0)
-        pair_b, pair_d = [(2, 0), (1, 1)], [(2, 1), (3, 0)]
-        ps_b = dv_bank(1, pair_b)
-        dv_product(ps_b, 0, 2, 0)
-        ps_d = dv_bank(3, pair_d)
-        dv_product(ps_d, 1, 3, 0)
+        whole = {t: dv_bank(number, [(t, 0), (t, 1)]) for t, number in ((2, 3), (3, 7))}
+        for t in whole:
+            dv_product(whole[t], 0, t, 0)
 
         for c in late:
             a[c] = work_tile("a%d" % c, c)
             nc.vector.tensor_tensor(a[c][:], a_ps[c][:], scale[:, :, items(c)], MULT)
-        for step in (subtract_y, scale_g, quantise_h):
+        for step in (subtract_y, scale_g):
             for c in late:
                 step(c)
+        quantise_h(1)
 
-        ps_c = dv_bank(2, [(0, 1)])
-        dv_product(ps_c, 0, 0, 1)
-        dv_product(ps_b, 1, 1, 1)
-        dv_product(ps_d, 0, 2, 1)
-        ps_e = dv_bank(0, [(3, 1)])
-        dv_product(ps_e, 0, 3, 1)
-        dv_copy("vector", ps_c, [(0, 1)])
-        dv_scatter("vector", 0, 1)
-        dv_copy("scalar", ps_b, pair_b, "dv_pair")
-        dv_scatter("scalar", 2, 0)
-        dv_scatter("vector", 1, 1)
+        w_i_second = mx_tiles("w_i_second", P, tag="work1")
+        quantise(w_i_second, E4M3, w_turned[:], P, P, -P)
         h_turned = sb.tile([P, PACK * R], BF16, name="h_turned", tag="h_turned", align_bytes=64)
-        turn_interleaved(h_turned, h_flat, 0, 2, "h_turn0")
-        turn_interleaved(h_turned, h_flat, 1, 1, "h_turn1")
-        dv_copy("vector", ps_d, pair_d, "dv_pair")
-        dv_scatter("vector", 2, 1)
-        dv_scatter("scalar", 3, 0)
-        dv_copy("scalar", ps_e, [(3, 1)])
-        dv_scatter("scalar", 3, 1)
-
+        h_words = h_flat.bitcast(F32).rearrange("p (s q u) -> p s u q", s=PACK, u=2)
+        turn_words(h_turned, h_words, 0, 0, "h_turn0", 2)
+        for t, number in ((0, 2), (1, 1)):
+            ps = dv_bank(number, [(t, 1)])
+            dv_product(ps, 0, t, 1)
+            dv_copy("vector", ps, [(t, 1)])
+        for t in range(2):
+            dv_scatter("vector", t, 1)
+        dv_product(whole[2], 1, 2, 1)
+        dv_copy("scalar", whole[2], [(2, 0), (2, 1)])
+        turn_words(h_turned, h_words, 1, 2, "h_turn1", 2)
+        dv_product(whole[3], 1, 3, 1)
+        dv_scatter("scalar", 2, 0)
         h_i = mx_tiles("h_i")
         quantise(h_i, E5M2, h_turned[:], 0, R)
-        w_i_rest = mx_tiles("w_i_rest", tag="h_turned")
-        quantise(w_i_rest, E4M3, w_turned[:], P, P)
-        quantise(w_i_rest, E4M3, w_turned[:], D // 2, D // 2)
+        w_i_last = mx_tiles("w_i_last", D // 2, tag="h_turned")
+        quantise(w_i_last, E4M3, w_turned[:], D // 2, D // 2, -D // 2)
+
+        def in_list_order(values, ps):
+            return values.rearrange("p (k q s) -> p k q s", k=2, s=PACK), ps.rearrange("p (k s q) -> p k q s", k=2, s=PACK)
+
+        dv_last = sb.tile([P, N], F32, name="dv3")
+        nc.scalar.copy(*in_list_order(dv_last[:], whole[3][:].rearrange("p k n -> p (k n)")))
+        dv_scatter("scalar", 2, 1)
+        scatter("vector", 0, last, item_list[:], dv_last[:])
+        store(0, last)
+
+        stationary = ((w_i_first, 0), (w_i_second, 0), (w_i_last, 0), (w_i_last, P))
+        engines = ("scalar", "vector")
         for t in range(PACK):
-            engine = ("vector", "scalar")[t % 2]
-            ps = bank(4 + t, [P, PACK, P], "du_ps%d" % t)
-            product(ps[:].rearrange("p s q -> p (s q)"), w_i_rest if t else w_i_first, t * P, h_i, E5M2, 0, R)
-            du = sb.tile([P, P, PACK], F32, name="du%d" % t, tag="du%d" % (t % 2))
-            copy_out(engine, du[:], ps[:].rearrange("p s q -> p q s"))
-            values = du[:].rearrange("p q s -> p (q s)")
-            if engine == "vector":
-                scatter(engine, 1, t, user_list[:], values)
-            else:
-                for k in range(2):
-                    scatter(engine, 1, t, list_half(user_list, k), values[:, k * HALF:(k + 1) * HALF])
+            ps = bank(4 + t, [P, R], "du_ps%d" % t)
+            product(ps[:], stationary[t][0], stationary[t][1], h_i, E5M2, 0, R)
+            du = sb.tile([P, R], F32, name="du%d" % t, tag="du%d" % (t % 2))
+            copy_out(engines[t % 2], *in_list_order(du[:], ps[:]))
+            for k in range(2):
+                scatter(engines[k], 1, t, list_half(user_list, k), du[:, k * HALF:(k + 1) * HALF])
             store(1, t)

@@ -117,6 +117,12 @@ def tile_attend_gmf_sq_vu_kernel(tc, uT, vT, y, us, ts, offs, uoffs, out_0, out_
         ts_gathered = sb.tile([P, N], F32, name="ts_gathered")
         nc.vector.tensor_copy(ts_gathered[:], ts_row[:].indirect(item_list[:]))
 
+        early, late = (0, 1), (2, 3)
+        ts_ps = bank(0, [P, len(late), P], "ts_ps")
+        for k, c in enumerate(late):
+            nc.tensor.transpose(ts_ps[:, k, :], ts_gathered[:, c * P:(c + 1) * P], identity[:])
+        ts_col = sb.tile([P, len(late)], F32, name="ts_col")
+        nc.scalar.copy(ts_col[:], ts_ps[:, :, 0])
         x = sb.tile([P, PACK, P, PACK], BF16, name="x", tag="ts_row", align_bytes=64)
         nc.scalar.copy(
             x[:, :, :, 0:2].rearrange("p s q e -> p q e s"), x_gathered[:].rearrange("p (e q s) -> p q e s", e=2, s=PACK))
@@ -158,8 +164,9 @@ def tile_attend_gmf_sq_vu_kernel(tc, uT, vT, y, us, ts, offs, uoffs, out_0, out_
         nc.scalar.activation(w_late[:, 0:HALF], v_rows[2][:].indirect(list_half(item_list, 1)), COPY)
 
         a_ps = {}
-        early, late = (0, 1), (2, 3)
         nc.vector.tensor_copy(w[:, 0:HALF, last], v_rows[last][:].indirect(list_half(item_list, 0)))
+        w_i_second = mx_tiles("w_i_second", P)
+        quantise(w_i_second, E4M3, w_turned[:], P, P, -P)
         nc.scalar.activation(w_late[:, HALF:N], v_rows[last][:].indirect(list_half(item_list, 1)), COPY)
         nc.scalar.copy(
             w[:, HALF:N, 2:4].rearrange("p (j f) e -> p j e f", f=4), w_late[:].rearrange("p (e j f) -> p j e f", e=2, f=4))
@@ -187,13 +194,13 @@ def tile_attend_gmf_sq_vu_kernel(tc, uT, vT, y, us, ts, offs, uoffs, out_0, out_
             return sb.tile([P, PACK, CHUNK], F32, name=name, tag="work%d" % slot, align_bytes=64)
 
         def subtract_y(c):
-            g[c] = work_tile("g%d" % c, (c + 2) % 4)
-            nc.vector.tensor_tensor(g[c][:], a[c][:], y_sb[:, :, items(c)], SUB)
+            g[c] = work_tile("g%d" % c, c + 2)[:]
+            nc.vector.tensor_tensor(g[c], a[c][:], y_sb[:, :, items(c)], SUB)
 
         def scale_g(c):
             nc.vector.tensor_tensor(
                 h[:, :, c * CHUNK // PACK:(c + 1) * CHUNK // PACK, :].rearrange("p s q t -> p q t s"),
-                by_fours(g[c][:]), by_fours(scale[:, :, items(c)]), MULT)
+                by_fours(g[c]), by_fours(scale[:, :, items(c)]), MULT)
 
         def quantise_h(k):
             run = HALF // PACK
@@ -206,13 +213,19 @@ def tile_attend_gmf_sq_vu_kernel(tc, uT, vT, y, us, ts, offs, uoffs, out_0, out_
             for u in range(2):
                 rows = slice(2 * u, 2 * u + 2)
                 nc.vector.tensor_tensor(a[c][:, rows, :], a_ps[c, u][:], scale[:, rows, items(c)], MULT)
+        by_item = {}
+        for c in late:
+            ps = bank(2 + c, [P, R], "a_by_item%d" % c)
+            product(ps[:], w_d_late, c * CHUNK - HALF, x_d, E4M3, 0, R)
+            by_item[c] = sb.tile([P, R], F32, name="ts_a%d" % c)
+            nc.scalar.activation(by_item[c][:], ps[:], COPY, scale=ts_col[:, c - 2:c - 1])
         turn_interleaved(w_turned, w_flat, 1, 0, "w_turn1")
+        late_ps = [bank(1 + u, [P, 2, HALF], "late_ps%d" % u) for u in range(2)]
+        for c in late:
+            for t in range(PACK):
+                nc.tensor.transpose(late_ps[t // 2][:, t % 2, items(c - 2)], by_item[c][:, t * P:(t + 1) * P], identity[:])
         for c in early:
             subtract_y(c)
-        for c in late:
-            a_ps[c] = bank(2 + c, [P, PACK, CHUNK], "a_ps%d" % c)
-            for t in range(PACK):
-                product(a_ps[c][:, t, :], x_d, t * P, w_d_late, E4M3, c * CHUNK - HALF, CHUNK)
         for c in early:
             scale_g(c)
         quantise_h(0)
@@ -272,16 +285,17 @@ def tile_attend_gmf_sq_vu_kernel(tc, uT, vT, y, us, ts, offs, uoffs, out_0, out_
         for t in whole:
             dv_product(whole[t], 0, t, 0)
 
+        g_late = sb.tile([P, PACK, HALF], F32, name="g_late", tag="work3", align_bytes=64)
+        for t in range(PACK):
+            nc.vector.scalar_tensor_tensor(
+                g_late[:, t, :], late_ps[t // 2][:, t % 2, :], us_col[:, t:t + 1], y_sb[:, t, HALF:N], MULT, SUB)
         for c in late:
-            a[c] = work_tile("a%d" % c, c)
-            nc.vector.tensor_tensor(a[c][:], a_ps[c][:], scale[:, :, items(c)], MULT)
-        for step in (subtract_y, scale_g):
-            for c in late:
-                step(c)
+            g[c] = g_late[:, :, items(c - 2)]
+            scale_g(c)
         quantise_h(1)
 
-        w_i_second = mx_tiles("w_i_second", P, tag="work1")
-        quantise(w_i_second, E4M3, w_turned[:], P, P, -P)
+        w_i_last = mx_tiles("w_i_last", D // 2, tag="work3")
+        quantise(w_i_last, E4M3, w_turned[:], D // 2, D // 2, -D // 2)
         h_turned = sb.tile([P, PACK * R], BF16, name="h_turned", tag="h_turned", align_bytes=64)
         h_words = h_flat.bitcast(F32).rearrange("p (s q u) -> p s u q", s=PACK, u=2)
         turn_words(h_turned, h_words, 0, 0, "h_turn0", 2)
@@ -298,14 +312,12 @@ def tile_attend_gmf_sq_vu_kernel(tc, uT, vT, y, us, ts, offs, uoffs, out_0, out_
         dv_scatter("scalar", 2, 0)
         h_i = mx_tiles("h_i")
         quantise(h_i, E5M2, h_turned[:], 0, R)
-        w_i_last = mx_tiles("w_i_last", D // 2, tag="h_turned")
-        quantise(w_i_last, E4M3, w_turned[:], D // 2, D // 2, -D // 2)
 
         def in_list_order(values, ps):
             return values.rearrange("p (k q s) -> p k q s", k=2, s=PACK), ps.rearrange("p (k s q) -> p k q s", k=2, s=PACK)
 
-        dv_last = sb.tile([P, N], F32, name="dv3")
-        nc.scalar.copy(*in_list_order(dv_last[:], whole[3][:].rearrange("p k n -> p (k n)")))
+        dv_last = sb.tile([P, N], F32, name="dv3", tag="h_turned", align_bytes=64)
+        nc.vector.tensor_copy(*in_list_order(dv_last[:], whole[3][:].rearrange("p k n -> p (k n)")))
         dv_scatter("scalar", 2, 1)
         scatter("vector", 0, last, item_list[:], dv_last[:])
         store(0, last)
@@ -315,8 +327,9 @@ def tile_attend_gmf_sq_vu_kernel(tc, uT, vT, y, us, ts, offs, uoffs, out_0, out_
         for t in range(PACK):
             ps = bank(4 + t, [P, R], "du_ps%d" % t)
             product(ps[:], stationary[t][0], stationary[t][1], h_i, E5M2, 0, R)
-            du = sb.tile([P, R], F32, name="du%d" % t, tag="du%d" % (t % 2))
-            copy_out(engines[t % 2], *in_list_order(du[:], ps[:]))
+            copier, tag = (("scalar", "du0"), ("scalar", "du1"), ("vector", "h_turned"), ("scalar", "du0"))[t]
+            du = sb.tile([P, R], F32, name="du%d" % t, tag=tag, align_bytes=64)
+            copy_out(copier, *in_list_order(du[:], ps[:]))
             for k in range(2):
                 scatter(engines[k], 1, t, list_half(user_list, k), du[:, k * HALF:(k + 1) * HALF])
             store(1, t)

@@ -58,8 +58,11 @@ def tile_attend_gmf_sq_vu_kernel(tc, uT, vT, y, us, ts, offs, uoffs, out_0, out_
                 stop=True,
             )
 
+        def list_part(index_list, first, count):
+            return index_list[:, first // PER_COLUMN:(first + count) // PER_COLUMN]
+
         def list_half(index_list, k):
-            return index_list[:, k * HALF // PER_COLUMN:(k + 1) * HALF // PER_COLUMN]
+            return list_part(index_list, k * HALF, HALF)
 
         item_list = lists.tile([P, N // PER_COLUMN], U16, name="item_list")
         user_list = lists.tile([P, R // PER_COLUMN], U16, name="user_list")
@@ -167,9 +170,13 @@ def tile_attend_gmf_sq_vu_kernel(tc, uT, vT, y, us, ts, offs, uoffs, out_0, out_
         nc.vector.tensor_copy(w[:, 0:HALF, last], v_rows[last][:].indirect(list_half(item_list, 0)))
         w_i_second = mx_tiles("w_i_second", P)
         quantise(w_i_second, E4M3, w_turned[:], P, P, -P)
-        nc.scalar.activation(w_late[:, HALF:N], v_rows[last][:].indirect(list_half(item_list, 1)), COPY)
-        nc.scalar.copy(
-            w[:, HALF:N, 2:4].rearrange("p (j f) e -> p j e f", f=4), w_late[:].rearrange("p (e j f) -> p j e f", e=2, f=4))
+        for c in late:
+            first = c * CHUNK
+            nc.scalar.activation(
+                w_late[:, first:first + CHUNK], v_rows[last][:].indirect(list_part(item_list, first, CHUNK)), COPY)
+        late_planes = w_late[:].rearrange("p (e c j f) -> p c j e f", e=2, c=2, f=4)
+        for c in late:
+            nc.scalar.copy(w[:, c * CHUNK:(c + 1) * CHUNK, 2:4].rearrange("p (j f) e -> p j e f", f=4), late_planes[:, c - 2])
         for c in early:
             quantise(w_d, E4M3, w_flat, c * CHUNK, CHUNK)
             for u in range(2):
@@ -177,7 +184,8 @@ def tile_attend_gmf_sq_vu_kernel(tc, uT, vT, y, us, ts, offs, uoffs, out_0, out_
                 for e in range(2):
                     product(a_ps[c, u][:, e, :], x_d, (2 * u + e) * P, w_d, E4M3, c * CHUNK, CHUNK)
         w_d_late = mx_tiles("w_d_late", HALF)
-        quantise(w_d_late, E4M3, w_flat, HALF, HALF, -HALF)
+        for c in late:
+            quantise(w_d_late, E4M3, w_flat, c * CHUNK, CHUNK, -HALF)
 
         a, g = {}, {}
         h = sb.tile([P, PACK, P, PACK], BF16, name="h", tag="h", align_bytes=64)
@@ -289,9 +297,11 @@ def tile_attend_gmf_sq_vu_kernel(tc, uT, vT, y, us, ts, offs, uoffs, out_0, out_
         for t in range(PACK):
             nc.vector.scalar_tensor_tensor(
                 g_late[:, t, :], late_ps[t // 2][:, t % 2, :], us_col[:, t:t + 1], y_sb[:, t, HALF:N], MULT, SUB)
-        for c in late:
-            g[c] = g_late[:, :, items(c - 2)]
-            scale_g(c)
+        for j in range(2):
+            places = slice(2 * j, 2 * j + 2)
+            nc.vector.tensor_tensor(
+                h[:, places, HALF // PACK:, :].rearrange("p s q t -> p q t s"),
+                by_fours(g_late[:])[:, :, :, places], by_fours(scale[:, :, HALF:N])[:, :, :, places], MULT)
         quantise_h(1)
 
         w_i_last = mx_tiles("w_i_last", D // 2, tag="work3")
@@ -301,7 +311,11 @@ def tile_attend_gmf_sq_vu_kernel(tc, uT, vT, y, us, ts, offs, uoffs, out_0, out_
         turn_words(h_turned, h_words, 0, 0, "h_turn0", 2)
         for t, number in ((0, 2), (1, 1)):
             ps = dv_bank(number, [(t, 1)])
-            dv_product(ps, 0, t, 1)
+            if t == 0:
+                for j in range(2):
+                    product(ps[:, 0, items(j)], x_r, 0, h_r, E5M2, HALF + j * CHUNK, CHUNK)
+            else:
+                dv_product(ps, 0, t, 1)
             dv_copy("vector", ps, [(t, 1)])
         for t in range(2):
             dv_scatter("vector", t, 1)

@@ -75,11 +75,11 @@ def tile_attend_gmf_sq_vu_kernel(tc, uT, vT, y, us, ts, offs, uoffs, out_0, out_
         v_hbm = vT.rearrange("(p t) n -> p t n", t=PACK)
 
         ts_runs = sb.tile([P, T // P], F32, name="ts_runs")
-        nc.sync.dma_start(ts_runs[:], ts[0:1, :].rearrange("o (p k) -> p (o k)", p=P))
+        nc.scalar.dma_start(ts_runs[:], ts[0:1, :].rearrange("o (p k) -> p (o k)", p=P))
         nc.sync.dma_start(u_rows[0][:], u_hbm[:, 0, :])
         nc.sync.dma_start(user_list[:], uoffs)
         nc.sync.dma_start(item_list[:], offs)
-        nc.sync.dma_start(us_col[:], us.rearrange("b (p t) o -> p (b t o)", t=PACK))
+        nc.scalar.dma_start(us_col[:], us.rearrange("b (p t) o -> p (b t o)", t=PACK))
         for t in range(1, PACK):
             nc.sync.dma_start(u_rows[t][:], u_hbm[:, t, :])
         for t in range(PACK):
@@ -96,13 +96,10 @@ def tile_attend_gmf_sq_vu_kernel(tc, uT, vT, y, us, ts, offs, uoffs, out_0, out_
             nc.scalar.copy(
                 ts_row[:].rearrange("m (n b k) -> m b n k", b=T // P // PACK, k=PACK)[:, b], ps[:].rearrange("m k n -> m n k"))
 
-        def turn_interleaved(turned, values, u, number, name):
-            turn_words(turned, values.bitcast(F32).rearrange("p (q s u) -> p s u q", s=PACK, u=2), u, number, name)
-
         def turn_words(turned, words, u, number, name, parts=1):
             ps = bank(number, [P, PACK * P], name)
             for s in range(PACK):
-                nc.tensor.transpose(ps[:, s * P:(s + 1) * P], words[:, s, u, :], identity[:])
+                nc.tensor.transpose(ps[:, s * P:(s + 1) * P], words[s], identity[:])
             planes = ps[:].bitcast(BF16).rearrange("q (s k p e) -> q e k p s", s=PACK, k=parts, e=2)
             places = turned[:].rearrange("q (k t p s) -> q t k p s", k=parts, t=PACK, s=PACK)
             for e in range(2):
@@ -134,7 +131,8 @@ def tile_attend_gmf_sq_vu_kernel(tc, uT, vT, y, us, ts, offs, uoffs, out_0, out_
         x_flat = x[:].rearrange("p s q t -> p (s q t)")
         x_d = mx_tiles("x_d")
         quantise(x_d, E4M3, x_flat, 0, R)
-        turn_words(x_turned, x_flat.bitcast(F32).rearrange("p (s q u) -> p s u q", s=PACK, u=2), 1, 4, "x_turn_words")
+        x_words = x_flat.bitcast(F32).rearrange("p (s q u) -> p s u q", s=PACK, u=2)
+        turn_words(x_turned, [x_words[:, s, 1, :] for s in range(PACK)], 1, 4, "x_turn_words")
         scale = sb.tile([P, PACK, N], F32, name="scale", tag="scale", align_bytes=64)
         for t in range(PACK):
             nc.scalar.activation(scale[:, t, :], ts_gathered[:], COPY, scale=us_col[:, t:t + 1])
@@ -186,10 +184,13 @@ def tile_attend_gmf_sq_vu_kernel(tc, uT, vT, y, us, ts, offs, uoffs, out_0, out_
         w_d_late = mx_tiles("w_d_late", HALF)
         for c in late:
             quantise(w_d_late, E4M3, w_flat, c * CHUNK, CHUNK, -HALF)
+        w_dealt = sb.tile([P, PACK, P], F32, name="w_dealt")
+        nc.scalar.copy(
+            w_dealt[:].rearrange("p s q -> p q s"), w_flat.bitcast(F32).rearrange("p (q s u) -> p u q s", s=PACK, u=2)[:, 1])
 
         a, g = {}, {}
-        h = sb.tile([P, PACK, P, PACK], BF16, name="h", tag="h", align_bytes=64)
-        h_flat = h[:].rearrange("p s q t -> p (s q t)")
+        h = [sb.tile([P, 2, P, PACK], BF16, name="h%d" % j, tag="h%d" % j, align_bytes=64) for j in range(2)]
+        h_flat = [part[:].rearrange("p s q t -> p (s q t)") for part in h]
         h_r = mx_tiles("h_r")
 
         def items(c):
@@ -205,16 +206,18 @@ def tile_attend_gmf_sq_vu_kernel(tc, uT, vT, y, us, ts, offs, uoffs, out_0, out_
             g[c] = work_tile("g%d" % c, c + 2)[:]
             nc.vector.tensor_tensor(g[c], a[c][:], y_sb[:, :, items(c)], SUB)
 
-        def scale_g(c):
-            nc.vector.tensor_tensor(
-                h[:, :, c * CHUNK // PACK:(c + 1) * CHUNK // PACK, :].rearrange("p s q t -> p q t s"),
-                by_fours(g[c]), by_fours(scale[:, :, items(c)]), MULT)
+        def scale_g(values, first, count):
+            for j in range(2):
+                places = slice(2 * j, 2 * j + 2)
+                nc.vector.tensor_tensor(
+                    h[j][:, :, first // PACK:(first + count) // PACK, :].rearrange("p s q t -> p q t s"),
+                    by_fours(values)[:, :, :, places], by_fours(scale[:, :, first:first + count])[:, :, :, places], MULT)
 
         def quantise_h(k):
             run = HALF // PACK
             for s in range(PACK):
-                first = s * P + k * run
-                quantise(h_r, E5M2, h_flat, first, run, k * HALF + s * run - first)
+                first = s % 2 * P + k * run
+                quantise(h_r, E5M2, h_flat[s // 2], first, run, k * HALF + s * run - first)
 
         for c in early:
             a[c] = work_tile("a%d" % c, c)
@@ -227,15 +230,16 @@ def tile_attend_gmf_sq_vu_kernel(tc, uT, vT, y, us, ts, offs, uoffs, out_0, out_
             product(ps[:], w_d_late, c * CHUNK - HALF, x_d, E4M3, 0, R)
             by_item[c] = sb.tile([P, R], F32, name="ts_a%d" % c)
             nc.scalar.activation(by_item[c][:], ps[:], COPY, scale=ts_col[:, c - 2:c - 1])
-        turn_interleaved(w_turned, w_flat, 1, 0, "w_turn1")
+        turn_words(w_turned, [w_dealt[:, s, :] for s in range(PACK)], 1, 0, "w_turn1")
         late_ps = [bank(1 + u, [P, 2, HALF], "late_ps%d" % u) for u in range(2)]
-        for c in late:
-            for t in range(PACK):
-                nc.tensor.transpose(late_ps[t // 2][:, t % 2, items(c - 2)], by_item[c][:, t * P:(t + 1) * P], identity[:])
+        for u in range(2):
+            for c in late:
+                for t in (2 * u, 2 * u + 1):
+                    nc.tensor.transpose(late_ps[u][:, t % 2, items(c - 2)], by_item[c][:, t * P:(t + 1) * P], identity[:])
         for c in early:
             subtract_y(c)
         for c in early:
-            scale_g(c)
+            scale_g(g[c], c * CHUNK, CHUNK)
         quantise_h(0)
 
         windows = [[sb.tile([P, T], F32, name="window%d_%d" % (o, t)) for t in range(PACK)] for o in range(2)]
@@ -274,7 +278,7 @@ def tile_attend_gmf_sq_vu_kernel(tc, uT, vT, y, us, ts, offs, uoffs, out_0, out_
             name = "dv%d_%d" % parts[0]
             values = sb.tile([P, len(parts), HALF], F32, name=name, tag=tag or name, align_bytes=64)
             copy_out(
-                engine, values[:].rearrange("p n (q s) -> p n q s", s=PACK), ps[:].rearrange("p n (s q) -> p n q s", s=PACK))
+                engine, values[:].rearrange("p n (q s) -> p n q s", s=PACK), ps.rearrange("p n (s q) -> p n q s", s=PACK))
             for slot, part in enumerate(parts):
                 dv[part] = values[:, slot, :]
 
@@ -285,8 +289,12 @@ def tile_attend_gmf_sq_vu_kernel(tc, uT, vT, y, us, ts, offs, uoffs, out_0, out_
 
         for t in range(2):
             ps = dv_bank(6 + t, [(t, 0)])
-            dv_product(ps, 0, t, 0)
-            dv_copy("scalar", ps, [(t, 0)])
+            if t == 0:
+                for j in range(2):
+                    product(ps[:, 0, items(j)], x_r, 0, h_r, E5M2, j * CHUNK, CHUNK)
+            else:
+                dv_product(ps, 0, t, 0)
+            dv_copy("scalar", ps[:], [(t, 0)])
         for t in range(2):
             dv_scatter("scalar", t, 0)
         whole = {t: dv_bank(number, [(t, 0), (t, 1)]) for t, number in ((2, 3), (3, 7))}
@@ -297,18 +305,15 @@ def tile_attend_gmf_sq_vu_kernel(tc, uT, vT, y, us, ts, offs, uoffs, out_0, out_
         for t in range(PACK):
             nc.vector.scalar_tensor_tensor(
                 g_late[:, t, :], late_ps[t // 2][:, t % 2, :], us_col[:, t:t + 1], y_sb[:, t, HALF:N], MULT, SUB)
-        for j in range(2):
-            places = slice(2 * j, 2 * j + 2)
-            nc.vector.tensor_tensor(
-                h[:, places, HALF // PACK:, :].rearrange("p s q t -> p q t s"),
-                by_fours(g_late[:])[:, :, :, places], by_fours(scale[:, :, HALF:N])[:, :, :, places], MULT)
+        scale_g(g_late[:], HALF, HALF)
         quantise_h(1)
 
         w_i_last = mx_tiles("w_i_last", D // 2, tag="work3")
         quantise(w_i_last, E4M3, w_turned[:], D // 2, D // 2, -D // 2)
         h_turned = sb.tile([P, PACK * R], BF16, name="h_turned", tag="h_turned", align_bytes=64)
-        h_words = h_flat.bitcast(F32).rearrange("p (s q u) -> p s u q", s=PACK, u=2)
-        turn_words(h_turned, h_words, 0, 0, "h_turn0", 2)
+        h_parts = [part.bitcast(F32).rearrange("p (s q u) -> p s u q", s=2, u=2) for part in h_flat]
+        h_words = [[h_parts[s // 2][:, s % 2, u, :] for s in range(PACK)] for u in range(2)]
+        turn_words(h_turned, h_words[0], 0, 0, "h_turn0", 2)
         for t, number in ((0, 2), (1, 1)):
             ps = dv_bank(number, [(t, 1)])
             if t == 0:
@@ -316,14 +321,15 @@ def tile_attend_gmf_sq_vu_kernel(tc, uT, vT, y, us, ts, offs, uoffs, out_0, out_
                     product(ps[:, 0, items(j)], x_r, 0, h_r, E5M2, HALF + j * CHUNK, CHUNK)
             else:
                 dv_product(ps, 0, t, 1)
-            dv_copy("vector", ps, [(t, 1)])
+            dv_copy("vector", ps[:], [(t, 1)])
         for t in range(2):
             dv_scatter("vector", t, 1)
         dv_product(whole[2], 1, 2, 1)
-        dv_copy("scalar", whole[2], [(2, 0), (2, 1)])
-        turn_words(h_turned, h_words, 1, 2, "h_turn1", 2)
+        dv_copy("scalar", whole[2][:, 0:1, :], [(2, 0)])
+        turn_words(h_turned, h_words[1], 1, 2, "h_turn1", 2)
         dv_product(whole[3], 1, 3, 1)
         dv_scatter("scalar", 2, 0)
+        dv_copy("scalar", whole[2][:, 1:2, :], [(2, 1)], "h1")
         h_i = mx_tiles("h_i")
         quantise(h_i, E5M2, h_turned[:], 0, R)
 
@@ -338,12 +344,35 @@ def tile_attend_gmf_sq_vu_kernel(tc, uT, vT, y, us, ts, offs, uoffs, out_0, out_
 
         stationary = ((w_i_first, 0), (w_i_second, 0), (w_i_last, 0), (w_i_last, P))
         engines = ("scalar", "vector")
-        for t in range(PACK):
+        du = {}
+
+        def du_product(t):
             ps = bank(4 + t, [P, R], "du_ps%d" % t)
             product(ps[:], stationary[t][0], stationary[t][1], h_i, E5M2, 0, R)
-            copier, tag = (("scalar", "du0"), ("scalar", "du1"), ("vector", "h_turned"), ("scalar", "du0"))[t]
-            du = sb.tile([P, R], F32, name="du%d" % t, tag=tag, align_bytes=64)
-            copy_out(copier, *in_list_order(du[:], ps[:]))
+            return ps
+
+        def du_copy(t, engine, tag):
+            values = sb.tile([P, R], F32, name="du%d" % t, tag=tag, align_bytes=64)
+            copy_out(engine, *in_list_order(values[:], du_product(t)[:]))
             for k in range(2):
-                scatter(engines[k], 1, t, list_half(user_list, k), du[:, k * HALF:(k + 1) * HALF])
+                du[t, k] = values[:, k * HALF:(k + 1) * HALF]
+
+        def du_scatter(t):
+            for k in range(2):
+                scatter(engines[k], 1, t, list_half(user_list, k), du[t, k])
             store(1, t)
+
+        ps = du_product(0)
+        for k, tag in enumerate(("du_first", "h_turned")):
+            values = sb.tile([P, HALF], F32, name="du0_%d" % k, tag=tag, align_bytes=64)
+            copy_out(
+                engines[k], values[:].rearrange("p (q s) -> p q s", s=PACK),
+                ps[:, k * HALF:(k + 1) * HALF].rearrange("p (s q) -> p q s", s=PACK))
+            du[0, k] = values[:]
+        du_copy(1, "scalar", "du_second")
+        du_scatter(0)
+        du_scatter(1)
+        du_copy(2, "scalar", "du_first")
+        du_copy(3, "vector", "du_second")
+        du_scatter(2)
+        du_scatter(3)

@@ -105,6 +105,21 @@ def tile_attend_gmf_sq_vu_kernel(tc, uT, vT, y, us, ts, offs, uoffs, out_0, out_
             for e in range(2):
                 nc.scalar.copy(places[:, 2 * u + e], planes[:, e])
 
+        def turn_words_apart(turned, words, u, number, name, parts):
+            ps = bank(number, [P, PACK * P], name)
+            planes = ps[:].bitcast(BF16).rearrange("q (s k p e) -> q e k p s", s=PACK, k=parts, e=2)
+            places = turned[:].rearrange("q (k t p s) -> q t k p s", k=parts, t=PACK, s=PACK)
+
+            def transposes():
+                for s in range(PACK):
+                    nc.tensor.transpose(ps[:, s * P:(s + 1) * P], words[s], identity[:])
+
+            def copies():
+                for e in range(2):
+                    nc.scalar.copy(places[:, 2 * u + e], planes[:, e])
+
+            return transposes, copies
+
         x_turned = sb.tile([P, PACK * D], BF16, name="x_turned", tag="x_turned", align_bytes=64)
         x_gathered = sb.tile([P, 2 * R], F32, name="x_gathered")
         for t in range(2):
@@ -189,8 +204,7 @@ def tile_attend_gmf_sq_vu_kernel(tc, uT, vT, y, us, ts, offs, uoffs, out_0, out_
             w_dealt[:].rearrange("p s q -> p q s"), w_flat.bitcast(F32).rearrange("p (q s u) -> p u q s", s=PACK, u=2)[:, 1])
 
         a, g = {}, {}
-        h = [sb.tile([P, 2, P, PACK], BF16, name="h%d" % j, tag="h%d" % j, align_bytes=64) for j in range(2)]
-        h_flat = [part[:].rearrange("p s q t -> p (s q t)") for part in h]
+        h = sb.tile([P, PACK * N], BF16, name="h", tag="h", align_bytes=64)
         h_r = mx_tiles("h_r")
 
         def items(c):
@@ -206,18 +220,14 @@ def tile_attend_gmf_sq_vu_kernel(tc, uT, vT, y, us, ts, offs, uoffs, out_0, out_
             g[c] = work_tile("g%d" % c, c + 2)[:]
             nc.vector.tensor_tensor(g[c], a[c][:], y_sb[:, :, items(c)], SUB)
 
-        def scale_g(values, first, count):
-            for j in range(2):
-                places = slice(2 * j, 2 * j + 2)
-                nc.vector.tensor_tensor(
-                    h[j][:, :, first // PACK:(first + count) // PACK, :].rearrange("p s q t -> p q t s"),
-                    by_fours(values)[:, :, :, places], by_fours(scale[:, :, first:first + count])[:, :, :, places], MULT)
+        def scale_g(values, c):
+            nc.vector.tensor_tensor(
+                h[:, PACK * c * CHUNK:PACK * (c + 1) * CHUNK].rearrange("p (q s t) -> p q t s", s=PACK, t=PACK),
+                by_fours(values), by_fours(scale[:, :, items(c)]), MULT)
 
         def quantise_h(k):
-            run = HALF // PACK
-            for s in range(PACK):
-                first = s % 2 * P + k * run
-                quantise(h_r, E5M2, h_flat[s // 2], first, run, k * HALF + s * run - first)
+            for c in (2 * k, 2 * k + 1):
+                quantise(h_r, E5M2, h[:], c * CHUNK, CHUNK)
 
         for c in early:
             a[c] = work_tile("a%d" % c, c)
@@ -231,16 +241,16 @@ def tile_attend_gmf_sq_vu_kernel(tc, uT, vT, y, us, ts, offs, uoffs, out_0, out_
             by_item[c] = sb.tile([P, R], F32, name="ts_a%d" % c)
             nc.scalar.activation(by_item[c][:], ps[:], COPY, scale=ts_col[:, c - 2:c - 1])
         turn_words(w_turned, [w_dealt[:, s, :] for s in range(PACK)], 1, 0, "w_turn1")
-        late_ps = [bank(1 + u, [P, 2, HALF], "late_ps%d" % u) for u in range(2)]
-        for u in range(2):
-            for c in late:
-                for t in (2 * u, 2 * u + 1):
-                    nc.tensor.transpose(late_ps[u][:, t % 2, items(c - 2)], by_item[c][:, t * P:(t + 1) * P], identity[:])
+        late_ps = {c: bank(c - 1, [P, PACK, CHUNK], "late_ps%d" % c) for c in late}
+        for c in late:
+            for t in range(PACK):
+                nc.tensor.transpose(late_ps[c][:, t, :], by_item[c][:, t * P:(t + 1) * P], identity[:])
         for c in early:
             subtract_y(c)
         for c in early:
-            scale_g(g[c], c * CHUNK, CHUNK)
+            scale_g(g[c], c)
         quantise_h(0)
+
 
         windows = [[sb.tile([P, T], F32, name="window%d_%d" % (o, t)) for t in range(PACK)] for o in range(2)]
         out_hbm = [out.rearrange("(p t) n -> p t n", t=PACK) for out in (out_0, out_1)]
@@ -249,13 +259,6 @@ def tile_attend_gmf_sq_vu_kernel(tc, uT, vT, y, us, ts, offs, uoffs, out_0, out_
             nc.vector.memset(window[:], 0.0)
         for window in windows[0][zeroed_by_vector:] + windows[1]:
             nc.gpsimd.memset(window[:], 0.0)
-
-        def dv_bank(number, parts):
-            ps = bank(number, [P, len(parts), HALF], "dv_ps%d_%d" % parts[0])
-            return ps
-
-        def dv_product(ps, slot, t, k):
-            product(ps[:, slot, :], x_r, t * P, h_r, E5M2, k * HALF, HALF)
 
         def scatter(engine, o, t, offsets, values):
             if engine == "vector":
@@ -272,107 +275,97 @@ def tile_attend_gmf_sq_vu_kernel(tc, uT, vT, y, us, ts, offs, uoffs, out_0, out_
             else:
                 nc.scalar.copy(out, ps)
 
-        dv = {}
+        engines = ("scalar", "vector")
+        index_lists = (item_list, user_list)
+        stationary = ((w_i_first, 0), (w_i_second, 0))
+        halves = {}
 
-        def dv_copy(engine, ps, parts, tag=None):
-            name = "dv%d_%d" % parts[0]
-            values = sb.tile([P, len(parts), HALF], F32, name=name, tag=tag or name, align_bytes=64)
-            copy_out(
-                engine, values[:].rearrange("p n (q s) -> p n q s", s=PACK), ps.rearrange("p n (s q) -> p n q s", s=PACK))
-            for slot, part in enumerate(parts):
-                dv[part] = values[:, slot, :]
-
-        def dv_scatter(engine, t, k):
-            scatter(engine, 0, t, list_half(item_list, k), dv[t, k])
-            if k == 1:
-                store(0, t)
-
-        for t in range(2):
-            ps = dv_bank(6 + t, [(t, 0)])
-            if t == 0:
-                for j in range(2):
-                    product(ps[:, 0, items(j)], x_r, 0, h_r, E5M2, j * CHUNK, CHUNK)
+        def multiply(o, t, k, out):
+            if o == 1:
+                product(out, stationary[t][0], stationary[t][1], h_i, E5M2, k * HALF, HALF)
             else:
-                dv_product(ps, 0, t, 0)
-            dv_copy("scalar", ps[:], [(t, 0)])
-        for t in range(2):
-            dv_scatter("scalar", t, 0)
-        whole = {t: dv_bank(number, [(t, 0), (t, 1)]) for t, number in ((2, 3), (3, 7))}
-        for t in whole:
-            dv_product(whole[t], 0, t, 0)
+                product(out, x_r, t * P, h_r, E5M2, k * HALF, HALF)
+
+        def half_bank(o, t, k, number):
+            ps = bank(number, [P, HALF], "half_ps%d_%d_%d" % (o, t, k))
+            multiply(o, t, k, ps[:])
+            return ps
+
+        def fetch(o, t, k, ps, tag=None):
+            name = "half%d_%d_%d" % (o, t, k)
+            values = sb.tile([P, HALF], F32, name=name, tag=tag or name, align_bytes=64)
+            if o == 0:
+                copy_out(engines[k], values[:], ps[:])
+            else:
+                copy_out(
+                    engines[k], values[:].rearrange("p (q s) -> p q s", s=PACK), ps[:].rearrange("p (s q) -> p q s", s=PACK))
+            halves[o, t, k] = values[:]
+
+        def put(o, t, k):
+            scatter(engines[k], o, t, list_half(index_lists[o], k), halves[o, t, k])
+            if k == 1:
+                store(o, t)
+
+        def fetch_by_chunks(k, numbers):
+            values = sb.tile([P, HALF], F32, name="half0_0_%d" % k, align_bytes=64)
+            for j, number in enumerate(numbers):
+                ps = bank(number, [P, CHUNK], "chunk_ps%d_%d" % (k, j))
+                product(ps[:], x_r, 0, h_r, E5M2, k * HALF + j * CHUNK, CHUNK)
+                copy_out(engines[k], values[:, items(j)], ps[:])
+            halves[0, 0, k] = values[:]
+
+        fetch_by_chunks(0, (4, 6))
+        first_ps = {t: half_bank(0, t, 0, number) for t, number in ((1, 7), (2, 3), (3, 0))}
+        fetch(0, 1, 0, first_ps[1])
+        put(0, 0, 0)
+        fetch(0, 2, 0, first_ps[2])
+        put(0, 1, 0)
+        put(0, 2, 0)
 
         g_late = sb.tile([P, PACK, HALF], F32, name="g_late", tag="work3", align_bytes=64)
-        for t in range(PACK):
-            nc.vector.scalar_tensor_tensor(
-                g_late[:, t, :], late_ps[t // 2][:, t % 2, :], us_col[:, t:t + 1], y_sb[:, t, HALF:N], MULT, SUB)
-        scale_g(g_late[:], HALF, HALF)
+        for c in late:
+            for t in range(PACK):
+                nc.vector.scalar_tensor_tensor(
+                    g_late[:, t, items(c - 2)], late_ps[c][:, t, :], us_col[:, t:t + 1], y_sb[:, t, items(c)], MULT, SUB)
+        for c in late:
+            scale_g(g_late[:, :, items(c - 2)], c)
         quantise_h(1)
+
 
         w_i_last = mx_tiles("w_i_last", D // 2, tag="work3")
         quantise(w_i_last, E4M3, w_turned[:], D // 2, D // 2, -D // 2)
         h_turned = sb.tile([P, PACK * R], BF16, name="h_turned", tag="h_turned", align_bytes=64)
-        h_parts = [part.bitcast(F32).rearrange("p (s q u) -> p s u q", s=2, u=2) for part in h_flat]
-        h_words = [[h_parts[s // 2][:, s % 2, u, :] for s in range(PACK)] for u in range(2)]
-        turn_words(h_turned, h_words[0], 0, 0, "h_turn0", 2)
-        for t, number in ((0, 2), (1, 1)):
-            ps = dv_bank(number, [(t, 1)])
-            if t == 0:
-                for j in range(2):
-                    product(ps[:, 0, items(j)], x_r, 0, h_r, E5M2, HALF + j * CHUNK, CHUNK)
-            else:
-                dv_product(ps, 0, t, 1)
-            dv_copy("vector", ps[:], [(t, 1)])
-        for t in range(2):
-            dv_scatter("vector", t, 1)
-        dv_product(whole[2], 1, 2, 1)
-        dv_copy("scalar", whole[2][:, 0:1, :], [(2, 0)])
-        turn_words(h_turned, h_words[1], 1, 2, "h_turn1", 2)
-        dv_product(whole[3], 1, 3, 1)
-        dv_scatter("scalar", 2, 0)
-        dv_copy("scalar", whole[2][:, 1:2, :], [(2, 1)], "h1")
+        h_words = h[:].bitcast(F32).rearrange("p (q s u) -> p u s q", s=PACK, u=2)
+        fetch_by_chunks(1, (5, 2))
+        fetch(0, 1, 1, half_bank(0, 1, 1, 1))
+        ps = bank(4, [P, 2, HALF], "second_ps")
+        for t in (2, 3):
+            multiply(0, t, 1, ps[:, t - 2, :])
+        put(0, 0, 1)
+        values = sb.tile([P, 2, HALF], F32, name="second", align_bytes=64)
+        nc.vector.tensor_copy(values[:], ps[:])
+        for t in (2, 3):
+            halves[0, t, 1] = values[:, t - 2, :]
+        put(0, 1, 1)
+        put(0, 2, 1)
+        turn_words(h_turned, [h_words[:, 0, s, :] for s in range(PACK)], 0, 2, "h_turn0", 2)
+        turn_first, turn_second = turn_words_apart(h_turned, [h_words[:, 1, s, :] for s in range(PACK)], 1, 1, "h_turn1", 2)
+        turn_first()
+        fetch(0, 3, 0, first_ps[3], "h")
+        turn_second()
+        put(0, 3, 0)
         h_i = mx_tiles("h_i")
-        quantise(h_i, E5M2, h_turned[:], 0, R)
+        for k in range(2):
+            quantise(h_i, E5M2, h_turned[:], k * HALF, HALF)
+        put(0, 3, 1)
 
-        def in_list_order(values, ps):
-            return values.rearrange("p (k q s) -> p k q s", k=2, s=PACK), ps.rearrange("p (k s q) -> p k q s", k=2, s=PACK)
 
-        dv_last = sb.tile([P, N], F32, name="dv3", tag="h_turned", align_bytes=64)
-        nc.vector.tensor_copy(*in_list_order(dv_last[:], whole[3][:].rearrange("p k n -> p (k n)")))
-        dv_scatter("scalar", 2, 1)
-        scatter("vector", 0, last, item_list[:], dv_last[:])
-        store(0, last)
-
-        stationary = ((w_i_first, 0), (w_i_second, 0), (w_i_last, 0), (w_i_last, P))
-        engines = ("scalar", "vector")
-        du = {}
-
-        def du_product(t):
-            ps = bank(4 + t, [P, R], "du_ps%d" % t)
-            product(ps[:], stationary[t][0], stationary[t][1], h_i, E5M2, 0, R)
-            return ps
-
-        def du_copy(t, engine, tag):
-            values = sb.tile([P, R], F32, name="du%d" % t, tag=tag, align_bytes=64)
-            copy_out(engine, *in_list_order(values[:], du_product(t)[:]))
+        stationary = stationary + ((w_i_last, 0), (w_i_last, P))
+        for pair, numbers in enumerate((((5, 6), (7, 3)), ((0, 4), (2, 1)))):
             for k in range(2):
-                du[t, k] = values[:, k * HALF:(k + 1) * HALF]
-
-        def du_scatter(t):
-            for k in range(2):
-                scatter(engines[k], 1, t, list_half(user_list, k), du[t, k])
-            store(1, t)
-
-        ps = du_product(0)
-        for k, tag in enumerate(("du_first", "h_turned")):
-            values = sb.tile([P, HALF], F32, name="du0_%d" % k, tag=tag, align_bytes=64)
-            copy_out(
-                engines[k], values[:].rearrange("p (q s) -> p q s", s=PACK),
-                ps[:, k * HALF:(k + 1) * HALF].rearrange("p (s q) -> p q s", s=PACK))
-            du[0, k] = values[:]
-        du_copy(1, "scalar", "du_second")
-        du_scatter(0)
-        du_scatter(1)
-        du_copy(2, "scalar", "du_first")
-        du_copy(3, "vector", "du_second")
-        du_scatter(2)
-        du_scatter(3)
+                for e in range(2):
+                    t = 2 * pair + e
+                    fetch(1, t, k, half_bank(1, t, k, numbers[k][e]), "du%d_%d" % (e, k))
+            for e in range(2):
+                for k in range(2):
+                    put(1, 2 * pair + e, k)

@@ -9,6 +9,7 @@ PACK = 4
 CHUNK = 128
 HALF = N // 2
 PER_COLUMN = 16
+DMA_ALIGN = 256
 FLOPS = 3 * 2 * D * R * N
 BYTES = 4 * (4 * D * T + R * N + R + T) + 2 * P * (R + N) // PER_COLUMN
 
@@ -22,6 +23,7 @@ E5M2 = mybir.dt.float8_e5m2_x4
 MULT = mybir.AluOpType.mult
 SUB = mybir.AluOpType.subtract
 COPY = mybir.ActivationFunctionType.Copy
+SQUARE = mybir.ActivationFunctionType.Square
 
 
 def tile_attend_gmf_sq_vu_kernel(tc, uT, vT, y, us, ts, offs, uoffs, out_0, out_1):
@@ -34,8 +36,8 @@ def tile_attend_gmf_sq_vu_kernel(tc, uT, vT, y, us, ts, offs, uoffs, out_0, out_
         def bank(number, shape, name):
             return psum.tile(shape, F32, name=name, tag="bank%d" % number)
 
-        def mx_tiles(name, width=512, tag=None):
-            codes = sb.tile([P, width], U32, name=name + "_codes", align_bytes=64, tag=tag or name + "_codes")
+        def mx_tiles(name, width=512, tag=None, align=64):
+            codes = sb.tile([P, width], U32, name=name + "_codes", align_bytes=align, tag=tag or name + "_codes")
             scales = sb.tile([P, width], U8, name=name + "_scales", align_bytes=64)
             return codes, scales
 
@@ -66,11 +68,13 @@ def tile_attend_gmf_sq_vu_kernel(tc, uT, vT, y, us, ts, offs, uoffs, out_0, out_
 
         item_list = lists.tile([P, N // PER_COLUMN], U16, name="item_list")
         user_list = lists.tile([P, R // PER_COLUMN], U16, name="user_list")
-        u_rows = [sb.tile([P, T], F32, name="u_rows%d" % t, tag="u_rows%d" % t) for t in range(PACK)]
-        v_rows = [sb.tile([P, T], F32, name="v_rows%d" % t, tag="v_rows%d" % t, align_bytes=64) for t in range(PACK)]
+        u_rows = [sb.tile([P, T], F32, name="u_rows%d" % t, tag="u_rows%d" % t, align_bytes=DMA_ALIGN) for t in range(PACK)]
+        v_rows = [sb.tile([P, T], F32, name="v_rows%d" % t, tag="v_rows%d" % t, align_bytes=DMA_ALIGN) for t in range(PACK)]
         ts_row = sb.tile([P, T], F32, name="ts_row", tag="ts_row", align_bytes=64)
         us_col = sb.tile([P, PACK], F32, name="us_col")
-        y_sb = sb.tile([P, PACK, N], F32, name="y_sb")
+        y_parts = ((CHUNK, CHUNK), (0, CHUNK), (HALF, HALF))
+        y_second, y_first, y_late = [
+            sb.tile([P, PACK, count], F32, name="y%d" % first, align_bytes=DMA_ALIGN) for first, count in y_parts]
         u_hbm = uT.rearrange("(p t) n -> p t n", t=PACK)
         v_hbm = vT.rearrange("(p t) n -> p t n", t=PACK)
 
@@ -84,7 +88,9 @@ def tile_attend_gmf_sq_vu_kernel(tc, uT, vT, y, us, ts, offs, uoffs, out_0, out_
             nc.sync.dma_start(u_rows[t][:], u_hbm[:, t, :])
         for t in range(PACK):
             nc.sync.dma_start(v_rows[t][:], v_hbm[:, t, :])
-        nc.sync.dma_start(y_sb[:], y.rearrange("b (p t) i -> p (b t) i", t=PACK))
+        y_hbm = y.rearrange("b (p t) i -> p (b t) i", t=PACK)
+        for part, (first, count) in zip((y_second, y_first, y_late), y_parts):
+            nc.sync.dma_start(part[:], y_hbm[:, :, first:first + count])
 
         identity = sb.tile([P, P], F32, name="identity")
         make_identity(nc, identity[:])
@@ -104,21 +110,6 @@ def tile_attend_gmf_sq_vu_kernel(tc, uT, vT, y, us, ts, offs, uoffs, out_0, out_
             places = turned[:].rearrange("q (k t p s) -> q t k p s", k=parts, t=PACK, s=PACK)
             for e in range(2):
                 nc.scalar.copy(places[:, 2 * u + e], planes[:, e])
-
-        def turn_words_apart(turned, words, u, number, name, parts):
-            ps = bank(number, [P, PACK * P], name)
-            planes = ps[:].bitcast(BF16).rearrange("q (s k p e) -> q e k p s", s=PACK, k=parts, e=2)
-            places = turned[:].rearrange("q (k t p s) -> q t k p s", k=parts, t=PACK, s=PACK)
-
-            def transposes():
-                for s in range(PACK):
-                    nc.tensor.transpose(ps[:, s * P:(s + 1) * P], words[s], identity[:])
-
-            def copies():
-                for e in range(2):
-                    nc.scalar.copy(places[:, 2 * u + e], planes[:, e])
-
-            return transposes, copies
 
         x_turned = sb.tile([P, PACK * D], BF16, name="x_turned", tag="x_turned", align_bytes=64)
         x_gathered = sb.tile([P, 2 * R], F32, name="x_gathered")
@@ -151,11 +142,12 @@ def tile_attend_gmf_sq_vu_kernel(tc, uT, vT, y, us, ts, offs, uoffs, out_0, out_
         scale = sb.tile([P, PACK, N], F32, name="scale", tag="scale", align_bytes=64)
         for t in range(PACK):
             nc.scalar.activation(scale[:, t, :], ts_gathered[:], COPY, scale=us_col[:, t:t + 1])
+        scale_square = sb.tile([P, PACK, CHUNK], F32, name="scale_square")
+        nc.scalar.activation(scale_square[:], scale[:, :, CHUNK:HALF], SQUARE)
         w_turned_first = sb.tile([P, D], BF16, name="w_turned_first", tag="w", align_bytes=64)
         w_turned = sb.tile([P, PACK * D], BF16, name="w_turned", align_bytes=64)
-        w_d = mx_tiles("w_d", HALF)
         last = PACK - 1
-        w_gathered = sb.tile([P, 2 * N], F32, name="w_gathered", tag="u_rows3")
+        w_gathered = sb.tile([P, 2 * N], F32, name="w_gathered", tag="u_rows3", align_bytes=DMA_ALIGN)
 
         def turn_w_plane(t, number, turned):
             ps = bank(number, [P, PACK, P], "w_turn_plane%d" % t)
@@ -169,39 +161,57 @@ def tile_attend_gmf_sq_vu_kernel(tc, uT, vT, y, us, ts, offs, uoffs, out_0, out_
         quantise(x_r, E4M3, x_turned[:], 0, D)
         nc.vector.tensor_copy(w_gathered[:, N:2 * N], v_rows[1][:].indirect(item_list[:]))
         turn_w_plane(1, 7, w_turned[:, D:2 * D])
-        w_i_first = mx_tiles("w_i_first", P, tag="v_rows1")
+        w_i_first = mx_tiles("w_i_first", P, tag="v_rows1", align=DMA_ALIGN)
         quantise(w_i_first, E4M3, w_turned_first[:], 0, P)
-        w = sb.tile([P, N, PACK], BF16, name="w", tag="w", align_bytes=64)
+        most = N - CHUNK
+        w = sb.tile([P, most, PACK], BF16, name="w", tag="w", align_bytes=64)
+        w_last = sb.tile([P, CHUNK, PACK], BF16, name="w_last", tag="w_last", align_bytes=64)
         w_flat = w[:].rearrange("p i t -> p (i t)")
-        nc.vector.tensor_copy(
-            w[:, :, 0:2].rearrange("p (j f) e -> p j e f", f=4), w_gathered[:].rearrange("p (e j f) -> p j e f", e=2, f=4))
+        w_last_flat = w_last[:].rearrange("p i t -> p (i t)")
+        gathered_planes = w_gathered[:].rearrange("p (e j f) -> p j e f", e=2, f=4)
+        nc.vector.tensor_copy(w[:, :, 0:2].rearrange("p (j f) e -> p j e f", f=4), gathered_planes[:, 0:most // 4])
+        nc.vector.tensor_copy(w_last[:, :, 0:2].rearrange("p (j f) e -> p j e f", f=4), gathered_planes[:, most // 4:])
+        late_places = {2: w[:, HALF:most], 3: w_last[:]}
+
+        def gather_late(t):
+            for c in late:
+                nc.scalar.activation(
+                    late_places[c][:, :, t], v_rows[t][:].indirect(list_part(item_list, c * CHUNK, CHUNK)), COPY)
+
         nc.vector.tensor_copy(w[:, 0:HALF, 2], v_rows[2][:].indirect(list_half(item_list, 0)))
-        w_late = sb.tile([P, 2 * HALF], F32, name="w_late", tag="u_rows3")
-        nc.scalar.activation(w_late[:, 0:HALF], v_rows[2][:].indirect(list_half(item_list, 1)), COPY)
+        gather_late(2)
 
         a_ps = {}
         nc.vector.tensor_copy(w[:, 0:HALF, last], v_rows[last][:].indirect(list_half(item_list, 0)))
         w_i_second = mx_tiles("w_i_second", P)
         quantise(w_i_second, E4M3, w_turned[:], P, P, -P)
-        for c in late:
-            first = c * CHUNK
-            nc.scalar.activation(
-                w_late[:, first:first + CHUNK], v_rows[last][:].indirect(list_part(item_list, first, CHUNK)), COPY)
-        late_planes = w_late[:].rearrange("p (e c j f) -> p c j e f", e=2, c=2, f=4)
-        for c in late:
-            nc.scalar.copy(w[:, c * CHUNK:(c + 1) * CHUNK, 2:4].rearrange("p (j f) e -> p j e f", f=4), late_planes[:, c - 2])
+        gather_late(last)
+        w_d = {}
         for c in early:
-            quantise(w_d, E4M3, w_flat, c * CHUNK, CHUNK)
+            w_d[c] = mx_tiles("w_d%d" % c, CHUNK)
+            quantise(w_d[c], E4M3, w_flat, c * CHUNK, CHUNK, -c * CHUNK)
             for u in range(2):
                 a_ps[c, u] = bank(2 * c + u, [P, 2, CHUNK], "a_ps%d_%d" % (c, u))
                 for e in range(2):
-                    product(a_ps[c, u][:, e, :], x_d, (2 * u + e) * P, w_d, E4M3, c * CHUNK, CHUNK)
-        w_d_late = mx_tiles("w_d_late", HALF)
+                    product(a_ps[c, u][:, e, :], x_d, (2 * u + e) * P, w_d[c], E4M3, 0, CHUNK)
+        by_item = {}
+
+        def late_product(c):
+            w_d[c] = mx_tiles("w_d%d" % c, CHUNK)
+            quantise(w_d[c], E4M3, late_places[c].rearrange("p i t -> p (i t)"), 0, CHUNK)
+            ps = bank(2 + c, [P, R], "a_by_item%d" % c)
+            product(ps[:], w_d[c], 0, x_d, E4M3, 0, R)
+            by_item[c] = sb.tile([P, R], F32, name="ts_a%d" % c)
+            nc.scalar.activation(by_item[c][:], ps[:], COPY, scale=ts_col[:, c - 2:c - 1])
+
         for c in late:
-            quantise(w_d_late, E4M3, w_flat, c * CHUNK, CHUNK, -HALF)
+            late_product(c)
         w_dealt = sb.tile([P, PACK, P], F32, name="w_dealt")
-        nc.scalar.copy(
-            w_dealt[:].rearrange("p s q -> p q s"), w_flat.bitcast(F32).rearrange("p (q s u) -> p u q s", s=PACK, u=2)[:, 1])
+        dealt_places = w_dealt[:].rearrange("p s q -> p q s")
+        for places, values in ((dealt_places[:, 0:most // PACK], w_flat), (dealt_places[:, most // PACK:], w_last_flat)):
+            nc.scalar.copy(places, values.bitcast(F32).rearrange("p (q s u) -> p u q s", s=PACK, u=2)[:, 1])
+        y_scaled = sb.tile([P, PACK, CHUNK], F32, name="y_scaled", tag="w_last", align_bytes=64)
+        nc.gpsimd.tensor_tensor(y_scaled[:], y_second[:], scale[:, :, CHUNK:HALF], MULT)
 
         a, g = {}, {}
         h = sb.tile([P, PACK * N], BF16, name="h", tag="h", align_bytes=64)
@@ -216,43 +226,41 @@ def tile_attend_gmf_sq_vu_kernel(tc, uT, vT, y, us, ts, offs, uoffs, out_0, out_
         def work_tile(name, slot):
             return sb.tile([P, PACK, CHUNK], F32, name=name, tag="work%d" % slot, align_bytes=64)
 
-        def subtract_y(c):
-            g[c] = work_tile("g%d" % c, c + 2)[:]
-            nc.vector.tensor_tensor(g[c], a[c][:], y_sb[:, :, items(c)], SUB)
+        def h_chunk(c):
+            return h[:, PACK * c * CHUNK:PACK * (c + 1) * CHUNK].rearrange("p (q s t) -> p q t s", s=PACK, t=PACK)
 
         def scale_g(values, c):
-            nc.vector.tensor_tensor(
-                h[:, PACK * c * CHUNK:PACK * (c + 1) * CHUNK].rearrange("p (q s t) -> p q t s", s=PACK, t=PACK),
-                by_fours(values), by_fours(scale[:, :, items(c)]), MULT)
+            nc.vector.tensor_tensor(h_chunk(c), by_fours(values), by_fours(scale[:, :, items(c)]), MULT)
 
         def quantise_h(k):
             for c in (2 * k, 2 * k + 1):
                 quantise(h_r, E5M2, h[:], c * CHUNK, CHUNK)
 
+        factors = (scale[:, :, items(0)], scale_square[:])
         for c in early:
             a[c] = work_tile("a%d" % c, c)
             for u in range(2):
                 rows = slice(2 * u, 2 * u + 2)
-                nc.vector.tensor_tensor(a[c][:, rows, :], a_ps[c, u][:], scale[:, rows, items(c)], MULT)
-        by_item = {}
-        for c in late:
-            ps = bank(2 + c, [P, R], "a_by_item%d" % c)
-            product(ps[:], w_d_late, c * CHUNK - HALF, x_d, E4M3, 0, R)
-            by_item[c] = sb.tile([P, R], F32, name="ts_a%d" % c)
-            nc.scalar.activation(by_item[c][:], ps[:], COPY, scale=ts_col[:, c - 2:c - 1])
-        turn_words(w_turned, [w_dealt[:, s, :] for s in range(PACK)], 1, 0, "w_turn1")
+                nc.vector.tensor_tensor(a[c][:, rows, :], a_ps[c, u][:], factors[c][:, rows, :], MULT)
+        w_turn_ps = bank(0, [P, PACK * P], "w_turn_ps")
+        for s in range(PACK):
+            nc.tensor.transpose(w_turn_ps[:, s * P:(s + 1) * P], w_dealt[:, s, :], identity[:])
+        w_planes = w_turn_ps[:].bitcast(BF16).rearrange("q (s p e) -> q e p s", s=PACK, e=2)
+        w_places = w_turned[:].rearrange("q (t p s) -> q t p s", t=PACK, s=PACK)
+        nc.scalar.copy(w_places[:, 2:4], w_planes)
         late_ps = {c: bank(c - 1, [P, PACK, CHUNK], "late_ps%d" % c) for c in late}
         for c in late:
             for t in range(PACK):
                 nc.tensor.transpose(late_ps[c][:, t, :], by_item[c][:, t * P:(t + 1) * P], identity[:])
-        for c in early:
-            subtract_y(c)
-        for c in early:
-            scale_g(g[c], c)
-        quantise_h(0)
+        g_first = work_tile("g_first", 2)
+        nc.vector.tensor_tensor(g_first[:], a[0][:], y_first[:], SUB)
+        nc.vector.tensor_tensor(h_chunk(1), by_fours(a[1][:]), by_fours(y_scaled[:]), SUB)
+        scale_g(g_first[:], 0)
+        for c in (1, 0):
+            quantise(h_r, E5M2, h[:], c * CHUNK, CHUNK)
 
 
-        windows = [[sb.tile([P, T], F32, name="window%d_%d" % (o, t)) for t in range(PACK)] for o in range(2)]
+        windows = [[sb.tile([P, T], F32, name="window%d_%d" % (o, t), align_bytes=DMA_ALIGN) for t in range(PACK)] for o in range(2)]
         out_hbm = [out.rearrange("(p t) n -> p t n", t=PACK) for out in (out_0, out_1)]
         zeroed_by_vector = 2
         for window in windows[0][:zeroed_by_vector]:
@@ -282,7 +290,7 @@ def tile_attend_gmf_sq_vu_kernel(tc, uT, vT, y, us, ts, offs, uoffs, out_0, out_
 
         def multiply(o, t, k, out):
             if o == 1:
-                product(out, stationary[t][0], stationary[t][1], h_i, E5M2, k * HALF, HALF)
+                product(out, stationary[t][0], stationary[t][1], h_i[k], E5M2, 0, HALF)
             else:
                 product(out, x_r, t * P, h_r, E5M2, k * HALF, HALF)
 
@@ -291,14 +299,15 @@ def tile_attend_gmf_sq_vu_kernel(tc, uT, vT, y, us, ts, offs, uoffs, out_0, out_
             multiply(o, t, k, ps[:])
             return ps
 
-        def fetch(o, t, k, ps, tag=None):
+        def fetch(o, t, k, ps, tag=None, engine=None):
             name = "half%d_%d_%d" % (o, t, k)
             values = sb.tile([P, HALF], F32, name=name, tag=tag or name, align_bytes=64)
             if o == 0:
-                copy_out(engines[k], values[:], ps[:])
+                copy_out(engine or engines[k], values[:], ps[:])
             else:
                 copy_out(
-                    engines[k], values[:].rearrange("p (q s) -> p q s", s=PACK), ps[:].rearrange("p (s q) -> p q s", s=PACK))
+                    engine or engines[k], values[:].rearrange("p (q s) -> p q s", s=PACK),
+                    ps[:].rearrange("p (s q) -> p q s", s=PACK))
             halves[o, t, k] = values[:]
 
         def put(o, t, k):
@@ -307,7 +316,7 @@ def tile_attend_gmf_sq_vu_kernel(tc, uT, vT, y, us, ts, offs, uoffs, out_0, out_
                 store(o, t)
 
         def fetch_by_chunks(k, numbers):
-            values = sb.tile([P, HALF], F32, name="half0_0_%d" % k, align_bytes=64)
+            values = sb.tile([P, HALF], F32, name="half0_0_%d" % k, tag="half0_0_%d" % k, align_bytes=64)
             for j, number in enumerate(numbers):
                 ps = bank(number, [P, CHUNK], "chunk_ps%d_%d" % (k, j))
                 product(ps[:], x_r, 0, h_r, E5M2, k * HALF + j * CHUNK, CHUNK)
@@ -315,57 +324,83 @@ def tile_attend_gmf_sq_vu_kernel(tc, uT, vT, y, us, ts, offs, uoffs, out_0, out_
             halves[0, 0, k] = values[:]
 
         fetch_by_chunks(0, (4, 6))
-        first_ps = {t: half_bank(0, t, 0, number) for t, number in ((1, 7), (2, 3), (3, 0))}
-        fetch(0, 1, 0, first_ps[1])
+        fetch(0, 1, 0, half_bank(0, 1, 0, 7))
+        first_ps = bank(3, [P, 2, HALF], "first_ps")
+        for t in (2, 3):
+            multiply(0, t, 0, first_ps[:, t - 2, :])
         put(0, 0, 0)
-        fetch(0, 2, 0, first_ps[2])
         put(0, 1, 0)
-        put(0, 2, 0)
 
-        g_late = sb.tile([P, PACK, HALF], F32, name="g_late", tag="work3", align_bytes=64)
         for c in late:
+            g[c] = work_tile("g%d" % c, c - 2)
             for t in range(PACK):
                 nc.vector.scalar_tensor_tensor(
-                    g_late[:, t, items(c - 2)], late_ps[c][:, t, :], us_col[:, t:t + 1], y_sb[:, t, items(c)], MULT, SUB)
+                    g[c][:, t, :], late_ps[c][:, t, :], us_col[:, t:t + 1], y_late[:, t, items(c - 2)], MULT, SUB)
         for c in late:
-            scale_g(g_late[:, :, items(c - 2)], c)
+            scale_g(g[c][:], c)
         quantise_h(1)
 
 
-        w_i_last = mx_tiles("w_i_last", D // 2, tag="work3")
-        quantise(w_i_last, E4M3, w_turned[:], D // 2, D // 2, -D // 2)
-        h_turned = sb.tile([P, PACK * R], BF16, name="h_turned", tag="h_turned", align_bytes=64)
-        h_words = h[:].bitcast(F32).rearrange("p (q s u) -> p u s q", s=PACK, u=2)
+        w_i_third = mx_tiles("w_i_third", P, tag="work1")
+        quantise(w_i_third, E4M3, w_turned[:], 2 * P, P, -2 * P)
         fetch_by_chunks(1, (5, 2))
-        fetch(0, 1, 1, half_bank(0, 1, 1, 1))
-        ps = bank(4, [P, 2, HALF], "second_ps")
+        fetch(0, 1, 1, half_bank(0, 1, 1, 1), None, "scalar")
+        for t in range(2):
+            put(0, t, 1)
+
+        h_words = h[:].bitcast(F32).rearrange("p (q s u) -> p u s q", s=PACK, u=2)
+        h_planes = []
+        for u, number in enumerate((5, 2)):
+            ps = bank(number, [P, PACK * P], "h_turn%d" % u)
+            for s in range(PACK):
+                nc.tensor.transpose(ps[:, s * P:(s + 1) * P], h_words[:, u, s, :], identity[:])
+            h_planes.append(ps[:].bitcast(BF16).rearrange("q (s k p e) -> q k e p s", s=PACK, k=2, e=2))
+        ps = bank(1, [P, 2, HALF], "second_ps")
         for t in (2, 3):
             multiply(0, t, 1, ps[:, t - 2, :])
-        put(0, 0, 1)
-        values = sb.tile([P, 2, HALF], F32, name="second", align_bytes=64)
+        values = sb.tile([P, 2, HALF], F32, name="second", tag="second", align_bytes=64)
         nc.vector.tensor_copy(values[:], ps[:])
         for t in (2, 3):
             halves[0, t, 1] = values[:, t - 2, :]
-        put(0, 1, 1)
+        h_turned = [sb.tile([P, PACK * HALF], BF16, name="h_turned%d" % k, tag="h_turned%d" % k, align_bytes=64) for k in range(2)]
+        h_i = [mx_tiles("h_i%d" % k, HALF) for k in range(2)]
+
+        def h_places(k, u):
+            return h_turned[k][:].rearrange("q (u e p s) -> q u e p s", u=2, e=2, s=PACK)[:, u]
+
+        nc.scalar.copy(h_places(0, 0), h_planes[0][:, 0])
+        values = sb.tile([P, 2, HALF], F32, name="first", tag="h", align_bytes=64)
+        nc.scalar.copy(values[:], first_ps[:])
+        for t in (2, 3):
+            halves[0, t, 0] = values[:, t - 2, :]
+        nc.scalar.copy(h_places(0, 1), h_planes[1][:, 0])
+        put(0, 2, 0)
+        quantise(h_i[0], E5M2, h_turned[0][:], 0, HALF)
+        nc.vector.tensor_copy(h_places(1, 0), h_planes[0][:, 1])
         put(0, 2, 1)
-        turn_words(h_turned, [h_words[:, 0, s, :] for s in range(PACK)], 0, 2, "h_turn0", 2)
-        turn_first, turn_second = turn_words_apart(h_turned, [h_words[:, 1, s, :] for s in range(PACK)], 1, 1, "h_turn1", 2)
-        turn_first()
-        fetch(0, 3, 0, first_ps[3], "h")
-        turn_second()
+        nc.scalar.copy(h_places(1, 1), h_planes[1][:, 1])
         put(0, 3, 0)
-        h_i = mx_tiles("h_i")
-        for k in range(2):
-            quantise(h_i, E5M2, h_turned[:], k * HALF, HALF)
+        quantise(h_i[1], E5M2, h_turned[1][:], 0, HALF)
         put(0, 3, 1)
 
-
-        stationary = stationary + ((w_i_last, 0), (w_i_last, P))
-        for pair, numbers in enumerate((((5, 6), (7, 3)), ((0, 4), (2, 1)))):
+        for t in range(2):
+            fetch(1, t, 0, half_bank(1, t, 0, (1, 6)[t]), "du%d_0" % t)
+        fetch(1, 0, 1, half_bank(1, 0, 1, 7), "du0_1")
+        for k in range(2):
+            put(1, 0, k)
+        w_i_last = mx_tiles("w_i_last", P, tag="du0_1")
+        quantise(w_i_last, E4M3, w_turned[:], 3 * P, P, -3 * P)
+        stationary = stationary + ((w_i_third, 0), (w_i_last, 0))
+        put(1, 1, 0)
+        fetch(1, 1, 1, half_bank(1, 1, 1, 0), "du0_0", "scalar")
+        put(1, 1, 1)
+        fetch(1, 2, 0, half_bank(1, 2, 0, 3), "du1_0")
+        fetch(1, 3, 0, half_bank(1, 3, 0, 4))
+        last_ps = bank(0, [P, 2, HALF], "last_ps")
+        for t in (2, 3):
+            multiply(1, t, 1, last_ps[:, t - 2, :])
+        for t in (2, 3):
+            fetch(1, t, 1, last_ps[:, t - 2, :])
+        for t in (2, 3):
             for k in range(2):
-                for e in range(2):
-                    t = 2 * pair + e
-                    fetch(1, t, k, half_bank(1, t, k, numbers[k][e]), "du%d_%d" % (e, k))
-            for e in range(2):
-                for k in range(2):
-                    put(1, 2 * pair + e, k)
+                put(1, t, k)

@@ -247,7 +247,9 @@ def tile_attend_gmf_sq_vu_kernel(tc, uT, vT, y, us, ts, offs, uoffs, out_0, out_
             nc.tensor.transpose(w_turn_ps[:, s * P:(s + 1) * P], w_dealt[:, s, :], identity[:])
         w_planes = w_turn_ps[:].bitcast(BF16).rearrange("q (s p e) -> q e p s", s=PACK, e=2)
         w_places = w_turned[:].rearrange("q (t p s) -> q t p s", t=PACK, s=PACK)
-        nc.scalar.copy(w_places[:, 2:4], w_planes)
+        w_turned_third = sb.tile([P, D], BF16, name="w_turned_third", tag="late_window", align_bytes=DMA_ALIGN)
+        nc.scalar.copy(w_turned_third[:].rearrange("q (p s) -> q p s", s=PACK), w_planes[:, 0])
+        nc.scalar.copy(w_places[:, 3], w_planes[:, 1])
         late_ps = {c: bank(c - 1, [P, PACK, CHUNK], "late_ps%d" % c) for c in late}
         for c in late:
             for t in range(PACK):
@@ -260,9 +262,9 @@ def tile_attend_gmf_sq_vu_kernel(tc, uT, vT, y, us, ts, offs, uoffs, out_0, out_
             quantise(h_r, E5M2, h[:], c * CHUNK, CHUNK)
 
 
-        windows = [[sb.tile([P, T], F32, name="window%d_%d" % (o, t), align_bytes=DMA_ALIGN) for t in range(PACK)] for o in range(2)]
+        windows = [[sb.tile([P, T], F32, name="window%d_%d" % (o, t), align_bytes=DMA_ALIGN) for t in range(PACK - o)] for o in range(2)]
         out_hbm = [out.rearrange("(p t) n -> p t n", t=PACK) for out in (out_0, out_1)]
-        zeroed_by_vector = 2
+        zeroed_by_vector = 1
         for window in windows[0][:zeroed_by_vector]:
             nc.vector.memset(window[:], 0.0)
         for window in windows[0][zeroed_by_vector:] + windows[1]:
@@ -342,7 +344,9 @@ def tile_attend_gmf_sq_vu_kernel(tc, uT, vT, y, us, ts, offs, uoffs, out_0, out_
 
 
         w_i_third = mx_tiles("w_i_third", P, tag="work1")
-        quantise(w_i_third, E4M3, w_turned[:], 2 * P, P, -2 * P)
+        quantise(w_i_third, E4M3, w_turned_third[:], 0, P)
+        windows[1].append(sb.tile([P, T], F32, name="window1_3", tag="late_window", align_bytes=DMA_ALIGN))
+        nc.gpsimd.memset(windows[1][last][:], 0.0)
         fetch_by_chunks(1, (5, 2))
         fetch(0, 1, 1, half_bank(0, 1, 1, 1), None, "scalar")
         for t in range(2):

from contextlib import ExitStack

import concourse.mybir as mybir
from concourse.masks import make_identity

D, R, N, T = 512, 512, 512, 2048
P = 128
PACK = 4
CHUNK = 128
HALF = N // 2
PER_COLUMN = 16
DMA_ALIGN = 256
FLOPS = 3 * 2 * D * R * N
BYTES = 4 * (4 * D * T + R * N + R + T) + 2 * P * (R + N) // PER_COLUMN

F32 = mybir.dt.float32
BF16 = mybir.dt.bfloat16
U32 = mybir.dt.uint32
U16 = mybir.dt.uint16
U8 = mybir.dt.uint8
E4M3 = mybir.dt.float8_e4m3fn_x4
E5M2 = mybir.dt.float8_e5m2_x4
MULT = mybir.AluOpType.mult
SUB = mybir.AluOpType.subtract
COPY = mybir.ActivationFunctionType.Copy
SQUARE = mybir.ActivationFunctionType.Square


def tile_attend_gmf_sq_vu_kernel(tc, uT, vT, y, us, ts, offs, uoffs, out_0, out_1):
    nc = tc.nc
    with ExitStack() as ctx:
        lists = ctx.enter_context(tc.tile_pool(name="lists", bufs=1))
        sb = ctx.enter_context(tc.tile_pool(name="sb", bufs=1))
        psum = ctx.enter_context(tc.psum_pool(name="psum", bufs=1))

        def bank(number, shape, name):
            return psum.tile(shape, F32, name=name, tag="bank%d" % number)

        def mx_tiles(name, width=512, tag=None, align=64):
            codes = sb.tile([P, width], U32, name=name + "_codes", align_bytes=align, tag=tag or name + "_codes")
            scales = sb.tile([P, width], U8, name=name + "_scales", align_bytes=64)
            return codes, scales

        def quantise(operand, fmt, values, first, count, shift=0):
            codes, scales = operand
            nc.vector.quantize_mx(
                out=codes[:, shift + first:shift + first + count].bitcast(fmt),
                scales=scales[:, shift + first:shift + first + count],
                in_=values[:, PACK * first:PACK * (first + count)],
            )

        def product(out, lhs, lhs_first, rhs, rhs_fmt, rhs_first, rhs_count):
            nc.tensor.matmul_mx(
                out=out,
                lhsT=lhs[0][:, lhs_first:lhs_first + P].bitcast(E4M3),
                lhsT_scale=lhs[1][:, lhs_first:lhs_first + P],
                rhs=rhs[0][:, rhs_first:rhs_first + rhs_count].bitcast(rhs_fmt),
                rhs_scale=rhs[1][:, rhs_first:rhs_first + rhs_count],
                start=True,
                stop=True,
            )

        def list_part(index_list, first, count):
            return index_list[:, first // PER_COLUMN:(first + count) // PER_COLUMN]

        def list_half(index_list, k):
            return list_part(index_list, k * HALF, HALF)

        item_list = lists.tile([P, N // PER_COLUMN], U16, name="item_list")
        user_list = lists.tile([P, R // PER_COLUMN], U16, name="user_list")
        u_rows = [sb.tile([P, T], F32, name="u_rows%d" % t, tag="u_rows%d" % t, align_bytes=DMA_ALIGN) for t in range(PACK)]
        v_rows = [sb.tile([P, T], F32, name="v_rows%d" % t, tag="v_rows%d" % t, align_bytes=DMA_ALIGN) for t in range(PACK)]
        ts_row = sb.tile([P, T], F32, name="ts_row", tag="ts_row", align_bytes=64)
        us_col = sb.tile([P, PACK], F32, name="us_col")
        y_parts = ((CHUNK, CHUNK), (0, CHUNK), (HALF, HALF))
        y_second, y_first, y_late = [
            sb.tile([P, PACK, count], F32, name="y%d" % first, align_bytes=DMA_ALIGN) for first, count in y_parts]
        u_hbm = uT.rearrange("(p t) n -> p t n", t=PACK)
        v_hbm = vT.rearrange("(p t) n -> p t n", t=PACK)

        ts_runs = sb.tile([P, T // P], F32, name="ts_runs")
        nc.scalar.dma_start(ts_runs[:], ts[0:1, :].rearrange("o (p k) -> p (o k)", p=P))
        nc.sync.dma_start(u_rows[0][:], u_hbm[:, 0, :])
        nc.sync.dma_start(user_list[:], uoffs)
        nc.sync.dma_start(item_list[:], offs)
        nc.scalar.dma_start(us_col[:], us.rearrange("b (p t) o -> p (b t o)", t=PACK))
        for t in range(1, PACK):
            nc.sync.dma_start(u_rows[t][:], u_hbm[:, t, :])
        for t in range(PACK):
            nc.sync.dma_start(v_rows[t][:], v_hbm[:, t, :])
        y_hbm = y.rearrange("b (p t) i -> p (b t) i", t=PACK)
        for part, (first, count) in zip((y_second, y_first, y_late), y_parts):
            nc.sync.dma_start(part[:], y_hbm[:, :, first:first + count])

        identity = sb.tile([P, P], F32, name="identity")
        make_identity(nc, identity[:])
        for b in range(T // P // PACK):
            ps = bank(b, [P, PACK, P], "ts_spread%d" % b)
            for k in range(PACK):
                column = b * PACK + k
                nc.tensor.transpose(ps[:, k, :], ts_runs[:, column:column + 1].to_broadcast([P, P]), identity[:])
            nc.scalar.copy(
                ts_row[:].rearrange("m (n b k) -> m b n k", b=T // P // PACK, k=PACK)[:, b], ps[:].rearrange("m k n -> m n k"))

        def turn_words(turned, words, u, number, name, parts=1):
            ps = bank(number, [P, PACK * P], name)
            for s in range(PACK):
                nc.tensor.transpose(ps[:, s * P:(s + 1) * P], words[s], identity[:])
            planes = ps[:].bitcast(BF16).rearrange("q (s k p e) -> q e k p s", s=PACK, k=parts, e=2)
            places = turned[:].rearrange("q (k t p s) -> q t k p s", k=parts, t=PACK, s=PACK)
            for e in range(2):
                nc.scalar.copy(places[:, 2 * u + e], planes[:, e])

        x_turned = sb.tile([P, PACK * D], BF16, name="x_turned", tag="x_turned", align_bytes=64)
        x_gathered = sb.tile([P, 2 * R], F32, name="x_gathered")
        for t in range(2):
            nc.vector.tensor_copy(x_gathered[:, t * R:(t + 1) * R], u_rows[t][:].indirect(user_list[:]))
            ps = bank(4 + t, [P, PACK, P], "x_turn%d" % t)
            for s in range(PACK):
                nc.tensor.transpose(ps[:, s, :], x_gathered[:, t * R + s:(t + 1) * R:PACK], identity[:])
            nc.scalar.copy(
                x_turned[:, t * D:(t + 1) * D].rearrange("q (p s) -> q p s", s=PACK), ps[:].rearrange("q s p -> q p s"))
        ts_gathered = sb.tile([P, N], F32, name="ts_gathered")
        nc.vector.tensor_copy(ts_gathered[:], ts_row[:].indirect(item_list[:]))

        early, late = (0, 1), (2, 3)
        ts_ps = bank(0, [P, len(late), P], "ts_ps")
        for k, c in enumerate(late):
            nc.tensor.transpose(ts_ps[:, k, :], ts_gathered[:, c * P:(c + 1) * P], identity[:])
        ts_col = sb.tile([P, len(late)], F32, name="ts_col")
        nc.scalar.copy(ts_col[:], ts_ps[:, :, 0])
        x = sb.tile([P, PACK, P, PACK], BF16, name="x", tag="ts_row", align_bytes=64)
        nc.scalar.copy(
            x[:, :, :, 0:2].rearrange("p s q e -> p q e s"), x_gathered[:].rearrange("p (e q s) -> p q e s", e=2, s=PACK))
        for t in range(2, PACK):
            nc.vector.tensor_copy(x[:, :, :, t].rearrange("p s q -> p q s"), u_rows[t][:].indirect(user_list[:]))
        x_flat = x[:].rearrange("p s q t -> p (s q t)")
        x_d = mx_tiles("x_d")
        quantise(x_d, E4M3, x_flat, 0, R)
        x_words = x_flat.bitcast(F32).rearrange("p (s q u) -> p s u q", s=PACK, u=2)
        turn_words(x_turned, [x_words[:, s, 1, :] for s in range(PACK)], 1, 4, "x_turn_words")
        scale = sb.tile([P, PACK, N], F32, name="scale", tag="scale", align_bytes=64)
        for t in range(PACK):
            nc.scalar.activation(scale[:, t, :], ts_gathered[:], COPY, scale=us_col[:, t:t + 1])
        scale_square = sb.tile([P, PACK, CHUNK], F32, name="scale_square")
        nc.scalar.activation(scale_square[:], scale[:, :, CHUNK:HALF], SQUARE)
        w_turned_first = sb.tile([P, D], BF16, name="w_turned_first", tag="w", align_bytes=64)
        w_turned = sb.tile([P, PACK * D], BF16, name="w_turned", align_bytes=64)
        last = PACK - 1
        w_gathered = sb.tile([P, 2 * N], F32, name="w_gathered", tag="u_rows3", align_bytes=DMA_ALIGN)

        def turn_w_plane(t, number, turned):
            ps = bank(number, [P, PACK, P], "w_turn_plane%d" % t)
            for s in range(PACK):
                nc.tensor.transpose(ps[:, s, :], w_gathered[:, t * N + s:(t + 1) * N:PACK], identity[:])
            nc.scalar.copy(turned.rearrange("q (p s) -> q p s", s=PACK), ps[:].rearrange("q s p -> q p s"))

        nc.vector.tensor_copy(w_gathered[:, 0:N], v_rows[0][:].indirect(item_list[:]))
        turn_w_plane(0, 6, w_turned_first[:])
        x_r = mx_tiles("x_r")
        quantise(x_r, E4M3, x_turned[:], 0, D)
        nc.vector.tensor_copy(w_gathered[:, N:2 * N], v_rows[1][:].indirect(item_list[:]))
        turn_w_plane(1, 7, w_turned[:, D:2 * D])
        w_i_first = mx_tiles("w_i_first", P, tag="v_rows1", align=DMA_ALIGN)
        quantise(w_i_first, E4M3, w_turned_first[:], 0, P)
        most = N - CHUNK
        w = sb.tile([P, most, PACK], BF16, name="w", tag="w", align_bytes=64)
        w_last = sb.tile([P, CHUNK, PACK], BF16, name="w_last", tag="w_last", align_bytes=64)
        w_flat = w[:].rearrange("p i t -> p (i t)")
        w_last_flat = w_last[:].rearrange("p i t -> p (i t)")
        gathered_planes = w_gathered[:].rearrange("p (e j f) -> p j e f", e=2, f=4)
        nc.vector.tensor_copy(w[:, :, 0:2].rearrange("p (j f) e -> p j e f", f=4), gathered_planes[:, 0:most // 4])
        nc.vector.tensor_copy(w_last[:, :, 0:2].rearrange("p (j f) e -> p j e f", f=4), gathered_planes[:, most // 4:])
        late_places = {2: w[:, HALF:most], 3: w_last[:]}

        def gather_late(t):
            for c in late:
                nc.scalar.activation(
                    late_places[c][:, :, t], v_rows[t][:].indirect(list_part(item_list, c * CHUNK, CHUNK)), COPY)

        nc.vector.tensor_copy(w[:, 0:HALF, 2], v_rows[2][:].indirect(list_half(item_list, 0)))
        gather_late(2)

        a_ps = {}
        nc.vector.tensor_copy(w[:, 0:HALF, last], v_rows[last][:].indirect(list_half(item_list, 0)))
        w_i_second = mx_tiles("w_i_second", P)
        quantise(w_i_second, E4M3, w_turned[:], P, P, -P)
        gather_late(last)
        w_d = {}
        for c in early:
            w_d[c] = mx_tiles("w_d%d" % c, CHUNK)
            quantise(w_d[c], E4M3, w_flat, c * CHUNK, CHUNK, -c * CHUNK)
            for u in range(2):
                a_ps[c, u] = bank(2 * c + u, [P, 2, CHUNK], "a_ps%d_%d" % (c, u))
                for e in range(2):
                    product(a_ps[c, u][:, e, :], x_d, (2 * u + e) * P, w_d[c], E4M3, 0, CHUNK)
        by_item = {}

        def late_product(c):
            w_d[c] = mx_tiles("w_d%d" % c, CHUNK)
            quantise(w_d[c], E4M3, late_places[c].rearrange("p i t -> p (i t)"), 0, CHUNK)
            ps = bank(2 + c, [P, R], "a_by_item%d" % c)
            product(ps[:], w_d[c], 0, x_d, E4M3, 0, R)
            by_item[c] = sb.tile([P, R], F32, name="ts_a%d" % c)
            nc.scalar.activation(by_item[c][:], ps[:], COPY, scale=ts_col[:, c - 2:c - 1])

        for c in late:
            late_product(c)
        w_dealt = sb.tile([P, PACK, P], F32, name="w_dealt")
        dealt_places = w_dealt[:].rearrange("p s q -> p q s")
        for places, values in ((dealt_places[:, 0:most // PACK], w_flat), (dealt_places[:, most // PACK:], w_last_flat)):
            nc.scalar.copy(places, values.bitcast(F32).rearrange("p (q s u) -> p u q s", s=PACK, u=2)[:, 1])
        y_scaled = sb.tile([P, PACK, CHUNK], F32, name="y_scaled", tag="w_last", align_bytes=64)
        nc.gpsimd.tensor_tensor(y_scaled[:], y_second[:], scale[:, :, CHUNK:HALF], MULT)

        a, g = {}, {}
        h = sb.tile([P, PACK * N], BF16, name="h", tag="h", align_bytes=64)
        h_r = mx_tiles("h_r")

        def items(c):
            return slice(c * CHUNK, (c + 1) * CHUNK)

        def by_fours(rows):
            return rows.rearrange("p t (q s) -> p q t s", s=PACK)

        def work_tile(name, slot):
            return sb.tile([P, PACK, CHUNK], F32, name=name, tag="work%d" % slot, align_bytes=64)

        def h_chunk(c):
            return h[:, PACK * c * CHUNK:PACK * (c + 1) * CHUNK].rearrange("p (q s t) -> p q t s", s=PACK, t=PACK)

        def scale_g(values, c):
            nc.vector.tensor_tensor(h_chunk(c), by_fours(values), by_fours(scale[:, :, items(c)]), MULT)

        def quantise_h(k):
            for c in (2 * k, 2 * k + 1):
                quantise(h_r, E5M2, h[:], c * CHUNK, CHUNK)

        factors = (scale[:, :, items(0)], scale_square[:])
        for c in early:
            a[c] = work_tile("a%d" % c, c)
            for u in range(2):
                rows = slice(2 * u, 2 * u + 2)
                nc.vector.tensor_tensor(a[c][:, rows, :], a_ps[c, u][:], factors[c][:, rows, :], MULT)
        w_turn_ps = bank(0, [P, PACK * P], "w_turn_ps")
        for s in range(PACK):
            nc.tensor.transpose(w_turn_ps[:, s * P:(s + 1) * P], w_dealt[:, s, :], identity[:])
        w_planes = w_turn_ps[:].bitcast(BF16).rearrange("q (s p e) -> q e p s", s=PACK, e=2)
        w_places = w_turned[:].rearrange("q (t p s) -> q t p s", t=PACK, s=PACK)
        w_turned_third = sb.tile([P, D], BF16, name="w_turned_third", tag="late_window", align_bytes=DMA_ALIGN)
        nc.scalar.copy(w_turned_third[:].rearrange("q (p s) -> q p s", s=PACK), w_planes[:, 0])
        nc.scalar.copy(w_places[:, 3], w_planes[:, 1])
        late_ps = {c: bank(c - 1, [P, PACK, CHUNK], "late_ps%d" % c) for c in late}
        for c in late:
            for t in range(PACK):
                nc.tensor.transpose(late_ps[c][:, t, :], by_item[c][:, t * P:(t + 1) * P], identity[:])
        g_first = work_tile("g_first", 2)
        nc.vector.tensor_tensor(g_first[:], a[0][:], y_first[:], SUB)
        nc.vector.tensor_tensor(h_chunk(1), by_fours(a[1][:]), by_fours(y_scaled[:]), SUB)
        scale_g(g_first[:], 0)
        for c in (1, 0):
            quantise(h_r, E5M2, h[:], c * CHUNK, CHUNK)


        windows = [[sb.tile([P, T], F32, name="window%d_%d" % (o, t), align_bytes=DMA_ALIGN) for t in range(PACK - o)] for o in range(2)]
        out_hbm = [out.rearrange("(p t) n -> p t n", t=PACK) for out in (out_0, out_1)]
        zeroed_by_vector = 1
        for window in windows[0][:zeroed_by_vector]:
            nc.vector.memset(window[:], 0.0)
        for window in windows[0][zeroed_by_vector:] + windows[1]:
            nc.gpsimd.memset(window[:], 0.0)

        def scatter(engine, o, t, offsets, values):
            if engine == "vector":
                nc.vector.tensor_copy(windows[o][t][:].indirect(offsets), values)
            else:
                nc.scalar.activation(windows[o][t][:].indirect(offsets), values, COPY)

        def store(o, t):
            nc.sync.dma_start(out_hbm[o][:, t, :], windows[o][t][:])

        def copy_out(engine, out, ps):
            if engine == "vector":
                nc.vector.tensor_copy(out, ps)
            else:
                nc.scalar.copy(out, ps)

        engines = ("scalar", "vector")
        index_lists = (item_list, user_list)
        stationary = ((w_i_first, 0), (w_i_second, 0))
        halves = {}

        def multiply(o, t, k, out):
            if o == 1:
                product(out, stationary[t][0], stationary[t][1], h_i[k], E5M2, 0, HALF)
            else:
                product(out, x_r, t * P, h_r, E5M2, k * HALF, HALF)

        def half_bank(o, t, k, number):
            ps = bank(number, [P, HALF], "half_ps%d_%d_%d" % (o, t, k))
            multiply(o, t, k, ps[:])
            return ps

        def fetch(o, t, k, ps, tag=None, engine=None):
            name = "half%d_%d_%d" % (o, t, k)
            values = sb.tile([P, HALF], F32, name=name, tag=tag or name, align_bytes=64)
            if o == 0:
                copy_out(engine or engines[k], values[:], ps[:])
            else:
                copy_out(
                    engine or engines[k], values[:].rearrange("p (q s) -> p q s", s=PACK),
                    ps[:].rearrange("p (s q) -> p q s", s=PACK))
            halves[o, t, k] = values[:]

        def put(o, t, k):
            scatter(engines[k], o, t, list_half(index_lists[o], k), halves[o, t, k])
            if k == 1:
                store(o, t)

        def fetch_by_chunks(k, numbers):
            values = sb.tile([P, HALF], F32, name="half0_0_%d" % k, tag="half0_0_%d" % k, align_bytes=64)
            for j, number in enumerate(numbers):
                ps = bank(number, [P, CHUNK], "chunk_ps%d_%d" % (k, j))
                product(ps[:], x_r, 0, h_r, E5M2, k * HALF + j * CHUNK, CHUNK)
                copy_out(engines[k], values[:, items(j)], ps[:])
            halves[0, 0, k] = values[:]

        fetch_by_chunks(0, (4, 6))
        fetch(0, 1, 0, half_bank(0, 1, 0, 7))
        first_ps = bank(3, [P, 2, HALF], "first_ps")
        for t in (2, 3):
            multiply(0, t, 0, first_ps[:, t - 2, :])
        put(0, 0, 0)
        put(0, 1, 0)

        for c in late:
            g[c] = work_tile("g%d" % c, c - 2)
            for t in range(PACK):
                nc.vector.scalar_tensor_tensor(
                    g[c][:, t, :], late_ps[c][:, t, :], us_col[:, t:t + 1], y_late[:, t, items(c - 2)], MULT, SUB)
        for c in late:
            scale_g(g[c][:], c)
        quantise_h(1)


        w_i_third = mx_tiles("w_i_third", P, tag="work1")
        quantise(w_i_third, E4M3, w_turned_third[:], 0, P)
        windows[1].append(sb.tile([P, T], F32, name="window1_3", tag="late_window", align_bytes=DMA_ALIGN))
        nc.gpsimd.memset(windows[1][last][:], 0.0)
        fetch_by_chunks(1, (5, 2))
        fetch(0, 1, 1, half_bank(0, 1, 1, 1), None, "scalar")
        for t in range(2):
            put(0, t, 1)

        h_words = h[:].bitcast(F32).rearrange("p (q s u) -> p u s q", s=PACK, u=2)
        h_planes = []
        for u, number in enumerate((5, 2)):
            ps = bank(number, [P, PACK * P], "h_turn%d" % u)
            for s in range(PACK):
                nc.tensor.transpose(ps[:, s * P:(s + 1) * P], h_words[:, u, s, :], identity[:])
            h_planes.append(ps[:].bitcast(BF16).rearrange("q (s k p e) -> q k e p s", s=PACK, k=2, e=2))
        ps = bank(1, [P, 2, HALF], "second_ps")
        for t in (2, 3):
            multiply(0, t, 1, ps[:, t - 2, :])
        values = sb.tile([P, 2, HALF], F32, name="second", tag="second", align_bytes=64)
        nc.vector.tensor_copy(values[:], ps[:])
        for t in (2, 3):
            halves[0, t, 1] = values[:, t - 2, :]
        h_turned = [sb.tile([P, PACK * HALF], BF16, name="h_turned%d" % k, tag="h_turned%d" % k, align_bytes=64) for k in range(2)]
        h_i = [mx_tiles("h_i%d" % k, HALF) for k in range(2)]

        def h_places(k, u):
            return h_turned[k][:].rearrange("q (u e p s) -> q u e p s", u=2, e=2, s=PACK)[:, u]

        nc.scalar.copy(h_places(0, 0), h_planes[0][:, 0])
        values = sb.tile([P, 2, HALF], F32, name="first", tag="h", align_bytes=64)
        nc.scalar.copy(values[:], first_ps[:])
        for t in (2, 3):
            halves[0, t, 0] = values[:, t - 2, :]
        nc.scalar.copy(h_places(0, 1), h_planes[1][:, 0])
        put(0, 2, 0)
        quantise(h_i[0], E5M2, h_turned[0][:], 0, HALF)
        nc.vector.tensor_copy(h_places(1, 0), h_planes[0][:, 1])
        put(0, 2, 1)
        nc.scalar.copy(h_places(1, 1), h_planes[1][:, 1])
        put(0, 3, 0)
        quantise(h_i[1], E5M2, h_turned[1][:], 0, HALF)
        put(0, 3, 1)

        for t in range(2):
            fetch(1, t, 0, half_bank(1, t, 0, (1, 6)[t]), "du%d_0" % t)
        fetch(1, 0, 1, half_bank(1, 0, 1, 7), "du0_1")
        for k in range(2):
            put(1, 0, k)
        w_i_last = mx_tiles("w_i_last", P, tag="du0_1")
        quantise(w_i_last, E4M3, w_turned[:], 3 * P, P, -3 * P)
        stationary = stationary + ((w_i_third, 0), (w_i_last, 0))
        put(1, 1, 0)
        fetch(1, 1, 1, half_bank(1, 1, 1, 0), "du0_0", "scalar")
        put(1, 1, 1)
        fetch(1, 2, 0, half_bank(1, 2, 0, 3), "du1_0")
        fetch(1, 3, 0, half_bank(1, 3, 0, 4))
        last_ps = bank(0, [P, 2, HALF], "last_ps")
        for t in (2, 3):
            multiply(1, t, 1, last_ps[:, t - 2, :])
        for t in (2, 3):
            fetch(1, t, 1, last_ps[:, t - 2, :])
        for t in (2, 3):
            for k in range(2):
                put(1, t, k)
